import numpy as np
import ml_dtypes


def mxq(x, axis, fmt="e4m3"):
    dtype, down = {"e4m3": (ml_dtypes.float8_e4m3fn, 7), "e5m2": (ml_dtypes.float8_e5m2, 14)}[fmt]
    v = np.moveaxis(np.asarray(x, np.float32).astype(ml_dtypes.bfloat16).astype(np.float64), axis, -1)
    blocks = v.reshape(v.shape[:-1] + (-1, 32))
    amax = np.abs(blocks).max(-1, keepdims=True)
    byte = np.maximum(np.where(amax > 0, np.frexp(amax)[1] - 1 + 127, 0) - down, 1)
    scale = np.exp2(byte - 127.0)
    codes = (blocks / scale).astype(np.float32).astype(dtype).astype(np.float64)
    return np.moveaxis((codes * scale).reshape(v.shape), -1, axis)


WIDE = False


def mx_kscale(k):
    if not WIDE:
        return np.ones(k)
    levels = np.array([10, -10, 5, -5, 0])
    if k % 512:
        return np.exp2(np.random.permutation(np.resize(levels, k // 32))).repeat(32)
    a = np.empty((k // 512, 16))
    for p in range(k // 512):
        a[p, :8] = np.random.permutation(np.resize(levels, 8))
        for g in range(8):
            far = levels[np.abs(levels - a[p, g]) >= 10]
            a[p, g + 8] = far[np.random.randint(len(far))]
    return np.exp2(a.ravel()).repeat(32)


def f64(x):
    return np.asarray(x).astype(np.float64)


def striped(idx):
    return np.tile(idx.reshape(-1, 16).T, (8, 1)).astype(np.uint16)


def unstriped(offs):
    return offs[:16].T.reshape(-1).astype(np.int64)


E2M1 = np.array([0.0, 0.5, 1.0, 1.5, 2.0, 3.0, 4.0, 6.0, -0.0, -0.5, -1.0, -1.5, -2.0, -3.0, -4.0, -6.0])


def pack_weight(w, fmt):
    k, n = w.shape
    w = f64(np.asarray(w, np.float32).astype(ml_dtypes.bfloat16)).reshape(k // 32, 32, n)
    amax = np.abs(w).max(1)
    if fmt == "e4m3":
        byte = np.frexp(amax)[1] - 1 + 127 - 7
    else:
        mant, ex = np.frexp(amax / 6.0)
        byte = np.where(mant > 0.5, ex, ex - 1) + 127
    byte = np.clip(np.where(amax > 0, byte, 1), 1, 254)
    scaled = (w * np.exp2(127.0 - byte)[:, None, :]).reshape(k, n).astype(np.float32)
    by_word = np.ascontiguousarray(scaled.reshape(k // 512, 128, 4, n).transpose(0, 1, 3, 2))
    if fmt == "e4m3":
        words = by_word.astype(ml_dtypes.float8_e4m3fn).view(np.uint8)
    else:
        c = by_word.astype(ml_dtypes.float4_e2m1fn).view(np.uint8) & 0xF
        words = (c[..., 0::2] | (c[..., 1::2] << 4)).reshape(k // 512, 128, 2 * n)
    return np.ascontiguousarray(words), np.ascontiguousarray(byte.astype(np.uint8).reshape(k // 512, 16, n))


def unpack_weight(words, scales, fmt):
    g, _, n = scales.shape
    words = np.ascontiguousarray(words).reshape(g, 128, n, -1)
    if fmt == "e4m3":
        vals = words.view(ml_dtypes.float8_e4m3fn).astype(np.float64)
    else:
        nib = np.empty((g, 128, n, 4), np.uint8)
        nib[..., 0::2] = words & 0xF
        nib[..., 1::2] = words >> 4
        vals = E2M1[nib]
    vals = vals * np.repeat(np.exp2(scales.astype(np.float64) - 127.0), 8, axis=1)[..., None]
    return vals.transpose(0, 1, 3, 2).reshape(g * 512, n)


K, T, E, C = 512, 512, 6, 256


def deal():
    deal = np.repeat(np.arange(E), C).reshape(3, T)[:, np.random.permutation(T)]
    deal = np.take_along_axis(deal, np.argsort(np.random.rand(3, T), axis=0), axis=0)
    for _ in range(8):
        s_, t_ = np.random.permutation(T).reshape(2, -1); r = np.random.randint(3, size=T // 2); x, y = deal[r, s_].copy(), deal[r, t_].copy()
        ok = ~((deal[:, s_] == y).any(0) | (deal[:, t_] == x).any(0)); deal[r[ok], s_[ok]] = y[ok]; deal[r[ok], t_[ok]] = x[ok]
    order = np.argsort(deal.reshape(-1) + 0.5 * np.random.rand(3 * T))
    slot_token = order % T; pos = np.empty(3 * T, np.int64); pos[order] = np.arange(3 * T); pos = pos.reshape(3, T)
    g = np.random.uniform(0.5, 1.5, (3, T)); g = g / g.sum(0)
    return slot_token, pos, g


def by_expert(wq, xq):
    return np.concatenate([wq[e].T @ xq[:, e * C:(e + 1) * C] for e in range(E)], axis=1)


def setup_inputs():
    n = np.random.standard_normal
    s = mx_kscale(K)
    slots1, pos1, g1 = deal()
    slots2, pos2, g2 = deal()
    x = pack_weight(n((K, T)) * s[:, None], "e4m3")
    w = [pack_weight(m, "e2m1") for m in n((E, K, K)) / np.sqrt(K) / s[None, :, None] * s]
    return {
        "x_words": x[0],
        "x_scales": x[1],
        "w_words": np.stack([m[0] for m in w]),
        "w_scales": np.stack([m[1] for m in w]),
        "gate1": (np.stack([np.tile(r, (128, 1)) for r in g1])).astype(np.float32),
        "gate2": (np.stack([np.tile(r, (128, 1)) for r in g2])).astype(np.float32),
        "offs": striped(slots1),
        "pos1": striped(pos1[0]),
        "pos2": striped(pos1[1]),
        "pos3": striped(pos1[2]),
        "offs2": striped(slots2),
        "pos4": striped(pos2[0]),
        "pos5": striped(pos2[1]),
        "pos6": striped(pos2[2]),
    }


def reference(x_words, x_scales, w_words, w_scales, gate1, gate2, offs, pos1, pos2, pos3, offs2, pos4, pos5, pos6):
    w = np.stack([unpack_weight(w_words[e], w_scales[e], "e2m1") for e in range(E)])
    idx, idx2 = unstriped(offs), unstriped(offs2)
    y = by_expert(w, unpack_weight(x_words, x_scales, "e4m3")[:, idx])
    c = sum(f64(gate1[r, :1]) * y[:, unstriped(p)] for r, p in enumerate((pos1, pos2, pos3)))
    z = by_expert(w, mxq(c[:, idx2], 0, "e4m3"))
    out = sum(f64(gate2[r, :1]) * z[:, unstriped(p)] for r, p in enumerate((pos4, pos5, pos6)))
    return out

@@ -1,0 +1,214 @@
+from contextlib import ExitStack
+
+import concourse.mybir as mybir
+from concourse.masks import make_identity
+
+F32 = mybir.dt.float32
+BF16 = mybir.dt.bfloat16
+I32 = mybir.dt.int32
+U32 = mybir.dt.uint32
+U16 = mybir.dt.uint16
+U8 = mybir.dt.uint8
+FP8X4 = mybir.dt.float8_e4m3fn_x4
+FP4X4 = mybir.dt.float4_e2m1fn_x4
+MULT = mybir.AluOpType.mult
+ADD = mybir.AluOpType.add
+COPY = mybir.ActivationFunctionType.Copy
+
+K, T, E, C = 512, 512, 6, 256
+S = E * C
+P = 128
+PACK = 4
+LIST_COLS = C // 16
+FLOPS = 2 * 2 * K * K * S
+
+
+def tile_moe_uni_none_kernel(
+    tc, x_words, x_scales, w_words, w_scales, gate1, gate2, offs, pos1, pos2, pos3, offs2, pos4, pos5, pos6, out
+):
+    nc = tc.nc
+    with ExitStack() as ctx:
+        keep = ctx.enter_context(tc.tile_pool(name="keep", bufs=1))
+        ring = ctx.enter_context(tc.tile_pool(name="ring", bufs=2))
+        mm_psum = ctx.enter_context(tc.psum_pool(name="mm_psum", bufs=4))
+        sum_psum = ctx.enter_context(tc.psum_pool(name="sum_psum", bufs=2))
+        back_psum = ctx.enter_context(tc.psum_pool(name="back_psum", bufs=2))
+
+        def load_list(src, name):
+            lst = keep.tile([P, src.shape[1]], U16, name=name)
+            nc.sync.dma_start(lst[:], src)
+            return lst
+
+        x_w = keep.tile([P, T], I32, name="x_w", align_bytes=64)
+        x_s = keep.tile([P, T // 4], I32, name="x_s", align_bytes=64)
+        w_w = keep.tile([P, E, K // 2], I32, name="w_w", align_bytes=64)
+        w_s = keep.tile([P, E, K // 4], I32, name="w_s", align_bytes=64)
+        nc.vector.memset(x_s[:], 0)
+        nc.vector.memset(w_s[:], 0)
+
+        offs_t = load_list(offs, "offs_t")
+        nc.sync.dma_start(x_w[:], x_words.rearrange("s p t d -> p (s t d)").bitcast(I32))
+        nc.sync.dma_start(w_w[:], w_words.rearrange("e s p n -> p (e s) n").bitcast(I32))
+        for q in range(4):
+            nc.sync.dma_start(
+                w_s[32 * q : 32 * q + 4, :, :],
+                w_scales[:, 0, 4 * q : 4 * q + 4, :].rearrange("e b n -> b e n").bitcast(I32),
+            )
+        for q in range(4):
+            nc.scalar.dma_start(x_s[32 * q : 32 * q + 4, :], x_scales[0, 4 * q : 4 * q + 4, :].bitcast(I32))
+        pos_a = [load_list(src, "pos_a%d" % r) for r, src in enumerate((pos1, pos2, pos3))]
+        gate_a = keep.tile([P, 3, T], F32, name="gate_a")
+        nc.sync.dma_start(gate_a[:], gate1.rearrange("r p n -> p r n"))
+        offs2_t = load_list(offs2, "offs2_t")
+        pos_b = [load_list(src, "pos_b%d" % r) for r, src in enumerate((pos4, pos5, pos6))]
+        gate_b = keep.tile([P, 3, T], F32, name="gate_b")
+        nc.sync.dma_start(gate_b[:], gate2.rearrange("r p n -> p r n"))
+
+        ident_f = keep.tile([P, P], F32, name="ident_f")
+        ident_b = keep.tile([P, P], BF16, name="ident_b")
+        make_identity(nc, ident_f[:])
+        make_identity(nc, ident_b[:])
+
+        wp_w = [keep.tile([P, E * P * 2], U8, name="wp_w%d" % t, align_bytes=64) for t in range(PACK)]
+        wp_s = [keep.tile([P, E * P], U8, name="wp_s%d" % t, align_bytes=64) for t in range(PACK)]
+
+        def permute_weights(t):
+            words = w_w[:].rearrange("p e n -> p (e n)").bitcast(U16).rearrange("p (m t) -> p m t", t=PACK)
+            nc.vector.tensor_copy(wp_w[t][:].bitcast(U16), words[:, :, t])
+            scales = w_s[:].rearrange("p e n -> p (e n)").bitcast(U8).rearrange("p (m t) -> p m t", t=PACK)
+            nc.vector.tensor_copy(wp_s[t][:], scales[:, :, t])
+
+        def experts(codes, scales, dst, t, group):
+            bank = mm_psum.tile([P, len(group) * C], F32, name="bank")
+            for j, e in enumerate(group):
+                nc.tensor.matmul_mx(
+                    out=bank[:, j * C : (j + 1) * C],
+                    lhsT=wp_w[t][:, e * 2 * P : (e + 1) * 2 * P].bitcast(FP4X4),
+                    lhsT_scale=wp_s[t][:, e * P : (e + 1) * P],
+                    rhs=codes[:, e * C : (e + 1) * C].bitcast(FP8X4),
+                    rhs_scale=scales[:, e * C : (e + 1) * C],
+                    start=True,
+                    stop=True,
+                )
+            nc.scalar.copy(dst[:, group[0] * C : (group[-1] + 1) * C], bank[:])
+
+        def gated(window, pos, gate, r, dst):
+            nc.vector.tensor_tensor(dst, window[:].indirect(pos[r][:]), gate[:, r, :], MULT)
+
+        def add_turned(bank, term, first, last):
+            for b in range(4):
+                nc.tensor.matmul(
+                    bank[:, b, :],
+                    lhsT=term[:, b * P : (b + 1) * P],
+                    rhs=ident_f[:],
+                    is_transpose=True,
+                    start=(first and b == 0),
+                    stop=(last and b == 3),
+                )
+
+        def turned_sum(window, pos, gate, terms, dtype):
+            bank = sum_psum.tile([P, 4, P], F32, name="sum_bank")
+            for r in range(terms):
+                term = ring.tile([P, T], F32, name="term", bufs=4)
+                gated(window, pos, gate, r, term[:])
+                add_turned(bank, term, r == 0, r == terms - 1)
+            turned = ring.tile([P, 4, P], dtype, name="turned")
+            nc.scalar.copy(turned[:], bank[:])
+            return turned
+
+        pairs = [(e, e + 1) for e in range(0, E, 2)]
+
+        xg_w = keep.tile([P, S], U32, name="xg_w", align_bytes=64)
+        xg_s = keep.tile([P, S], U8, name="xg_s", align_bytes=64)
+        y = [keep.tile([P, S], F32, name="y%d" % t) for t in range(PACK)]
+
+        wide = 384
+        for a in range(0, S, wide):
+            lst = offs_t[:, a // 16 : (a + wide) // 16]
+            nc.vector.tensor_copy(xg_w[:, a : a + wide], x_w[:].bitcast(U32).indirect(lst))
+        permute_weights(0)
+        for e in range(E):
+            lst = offs_t[:, e * LIST_COLS : (e + 1) * LIST_COLS]
+            nc.vector.tensor_copy(xg_s[:, e * C : (e + 1) * C], x_s[:].bitcast(U8).indirect(lst))
+            experts(xg_w, xg_s, y[0], 0, (e,))
+        for t in range(1, PACK):
+            permute_weights(t)
+            for group in pairs:
+                experts(xg_w, xg_s, y[t], t, group)
+
+        c_single = [keep.tile([P, T], BF16, name="c_single%d" % t) for t in range(2)]
+        for t in range(2):
+            turned = turned_sum(y[t], pos_a, gate_a, 3, BF16)
+            back = back_psum.tile([P, T], BF16, name="back")
+            for b in range(4):
+                nc.tensor.transpose(back[:, b * P : (b + 1) * P], turned[:, b, :], ident_b[:])
+            nc.scalar.copy(c_single[t][:], back[:])
+
+        halves = [back_psum.tile([P, 2, T // 2], F32, name="back") for h in range(2)]
+        for u in range(2):
+            turned = turned_sum(y[2 + u], pos_a, gate_a, 2, F32)
+            for b in range(4):
+                nc.tensor.transpose(halves[b // 2][:, u, (b % 2) * P : (b % 2 + 1) * P], turned[:, b, :], ident_f[:])
+        third = keep.tile([P, 2, T], F32, name="third")
+        for u in range(2):
+            gated(y[2 + u], pos_a, gate_a, 2, third[:, u, :])
+        c_pair = keep.tile([P, T, 2], BF16, name="c_pair", align_bytes=64)
+        for h in range(2):
+            cols = slice(h * T // 2, (h + 1) * T // 2)
+            nc.vector.tensor_tensor(
+                c_pair[:, cols, :],
+                halves[h][:].rearrange("p u n -> p n u"),
+                third[:, :, cols].rearrange("p u n -> p n u"),
+                ADD,
+            )
+
+        cg = keep.tile([P, S, PACK], BF16, name="cg", align_bytes=64)
+        cq_w = keep.tile([P, S], U32, name="cq_w", align_bytes=64)
+        cq_s = keep.tile([P, S], U8, name="cq_s", align_bytes=64)
+        z = [keep.tile([P, S], F32, name="z%d" % t) for t in range(PACK)]
+        cg_words = cg[:].rearrange("p n t -> p (n t)").bitcast(U32).rearrange("p (n u) -> p n u", u=2)
+        c_words = c_pair[:].rearrange("p n u -> p (n u)").bitcast(U32)
+
+        for t in range(2):
+            for e in range(E):
+                lst = offs2_t[:, e * LIST_COLS : (e + 1) * LIST_COLS]
+                nc.scalar.activation(cg[:, e * C : (e + 1) * C, t], c_single[t][:].indirect(lst), COPY)
+
+        def quantise(e):
+            nc.vector.quantize_mx(
+                out=cq_w[:, e * C : (e + 1) * C].bitcast(FP8X4),
+                scales=cq_s[:, e * C : (e + 1) * C],
+                in_=cg[:, e * C : (e + 1) * C, :].rearrange("p n t -> p (n t)"),
+            )
+            experts(cq_w, cq_s, z[0], 0, (e,))
+
+        for e in range(E):
+            lst = offs2_t[:, e * LIST_COLS : (e + 1) * LIST_COLS]
+            nc.vector.tensor_copy(cg_words[:, e * C : (e + 1) * C, 1], c_words.indirect(lst))
+            if e > 0:
+                quantise(e - 1)
+        quantise(E - 1)
+        for t in range(1, PACK):
+            for group in pairs:
+                experts(cq_w, cq_s, z[t], t, group)
+
+        out_rows = out.rearrange("(p t) n -> p t n", t=PACK)
+        backs = []
+        for t in range(PACK):
+            turned = turned_sum(z[t], pos_b, gate_b, 3 if t < 2 else 2, F32)
+            back = back_psum.tile([P, T], F32, name="back")
+            for b in range(4):
+                nc.tensor.transpose(back[:, b * P : (b + 1) * P], turned[:, b, :], ident_f[:])
+            if t < 2:
+                res = ring.tile([P, T], F32, name="res", bufs=4)
+                nc.scalar.copy(res[:], back[:])
+                nc.sync.dma_start(out_rows[:, t, :], res[:])
+            else:
+                backs.append(back)
+        last = keep.tile([P, 2, T], F32, name="last")
+        for u in range(2):
+            gated(z[2 + u], pos_b, gate_b, 2, last[:, u, :])
+        for u in range(2):
+            res = ring.tile([P, T], F32, name="res", bufs=4)
+            nc.vector.tensor_tensor(res[:], backs[u][:], last[:, u, :], ADD)
+            nc.sync.dma_start(out_rows[:, 2 + u, :], res[:])

@@ -44,18 +44,18 @@ def tile_moe_uni_none_kernel(
         w_w = keep.tile([P, E, K // 2], I32, name="w_w", align_bytes=64)
         w_s = keep.tile([P, E, K // 4], I32, name="w_s", align_bytes=64)
         nc.vector.memset(x_s[:], 0)
-        nc.vector.memset(w_s[:], 0)
+        nc.gpsimd.memset(w_s[:], 0)
 
         offs_t = load_list(offs, "offs_t")
-        nc.sync.dma_start(x_w[:], x_words.rearrange("s p t d -> p (s t d)").bitcast(I32))
-        nc.sync.dma_start(w_w[:], w_words.rearrange("e s p n -> p (e s) n").bitcast(I32))
+        nc.scalar.dma_start(x_w[:], x_words.rearrange("s p t d -> p (s t d)").bitcast(I32))
         for q in range(4):
             nc.sync.dma_start(
                 w_s[32 * q : 32 * q + 4, :, :],
                 w_scales[:, 0, 4 * q : 4 * q + 4, :].rearrange("e b n -> b e n").bitcast(I32),
             )
+        nc.sync.dma_start(w_w[:], w_words.rearrange("e s p n -> p (e s) n").bitcast(I32))
         for q in range(4):
-            nc.scalar.dma_start(x_s[32 * q : 32 * q + 4, :], x_scales[0, 4 * q : 4 * q + 4, :].bitcast(I32))
+            nc.sync.dma_start(x_s[32 * q : 32 * q + 4, :], x_scales[0, 4 * q : 4 * q + 4, :].bitcast(I32))
         pos_a = [load_list(src, "pos_a%d" % r) for r, src in enumerate((pos1, pos2, pos3))]
         gate_a = keep.tile([P, 3, T], F32, name="gate_a")
         nc.sync.dma_start(gate_a[:], gate1.rearrange("r p n -> p r n"))
@@ -74,9 +74,10 @@ def tile_moe_uni_none_kernel(
 
         def permute_weights(t):
             words = w_w[:].rearrange("p e n -> p (e n)").bitcast(U16).rearrange("p (m t) -> p m t", t=PACK)
-            nc.vector.tensor_copy(wp_w[t][:].bitcast(U16), words[:, :, t])
             scales = w_s[:].rearrange("p e n -> p (e n)").bitcast(U8).rearrange("p (m t) -> p m t", t=PACK)
-            nc.vector.tensor_copy(wp_s[t][:], scales[:, :, t])
+            nc.gpsimd.tensor_copy(wp_s[t][:], scales[:, :, t])
+            engine = nc.vector if t % 2 == 0 else nc.gpsimd
+            engine.tensor_copy(wp_w[t][:].bitcast(U16), words[:, :, t])
 
         def experts(codes, scales, dst, t, group):
             bank = mm_psum.tile([P, len(group) * C], F32, name="bank")
@@ -131,24 +132,27 @@ def tile_moe_uni_none_kernel(
             lst = offs_t[:, e * LIST_COLS : (e + 1) * LIST_COLS]
             nc.vector.tensor_copy(xg_s[:, e * C : (e + 1) * C], x_s[:].bitcast(U8).indirect(lst))
             experts(xg_w, xg_s, y[0], 0, (e,))
-        for t in range(1, PACK):
+        for t in (2, 3, 1):
             permute_weights(t)
             for group in pairs:
                 experts(xg_w, xg_s, y[t], t, group)
 
         c_single = [keep.tile([P, T], BF16, name="c_single%d" % t) for t in range(2)]
-        for t in range(2):
+
+        def combine_single(t):
             turned = turned_sum(y[t], pos_a, gate_a, 3, BF16)
-            back = back_psum.tile([P, T], BF16, name="back")
+            back = sum_psum.tile([P, T], BF16, name="sum_bank")
             for b in range(4):
                 nc.tensor.transpose(back[:, b * P : (b + 1) * P], turned[:, b, :], ident_b[:])
             nc.scalar.copy(c_single[t][:], back[:])
 
+        combine_single(0)
         halves = [back_psum.tile([P, 2, T // 2], F32, name="back") for h in range(2)]
         for u in range(2):
             turned = turned_sum(y[2 + u], pos_a, gate_a, 2, F32)
             for b in range(4):
                 nc.tensor.transpose(halves[b // 2][:, u, (b % 2) * P : (b % 2 + 1) * P], turned[:, b, :], ident_f[:])
+        combine_single(1)
         third = keep.tile([P, 2, T], F32, name="third")
         for u in range(2):
             gated(y[2 + u], pos_a, gate_a, 2, third[:, u, :])
@@ -174,20 +178,32 @@ def tile_moe_uni_none_kernel(
                 lst = offs2_t[:, e * LIST_COLS : (e + 1) * LIST_COLS]
                 nc.scalar.activation(cg[:, e * C : (e + 1) * C, t], c_single[t][:].indirect(lst), COPY)
 
-        def quantise(e):
+        def quantise(a, b):
             nc.vector.quantize_mx(
-                out=cq_w[:, e * C : (e + 1) * C].bitcast(FP8X4),
-                scales=cq_s[:, e * C : (e + 1) * C],
-                in_=cg[:, e * C : (e + 1) * C, :].rearrange("p n t -> p (n t)"),
+                out=cq_w[:, a:b].bitcast(FP8X4),
+                scales=cq_s[:, a:b],
+                in_=cg[:, a:b, :].rearrange("p n t -> p (n t)"),
             )
-            experts(cq_w, cq_s, z[0], 0, (e,))
+            e = a // C
+            bank = mm_psum.tile([P, b - a], F32, name="bank")
+            nc.tensor.matmul_mx(
+                out=bank[:],
+                lhsT=wp_w[0][:, e * 2 * P : (e + 1) * 2 * P].bitcast(FP4X4),
+                lhsT_scale=wp_s[0][:, e * P : (e + 1) * P],
+                rhs=cq_w[:, a:b].bitcast(FP8X4),
+                rhs_scale=cq_s[:, a:b],
+                start=True,
+                stop=True,
+            )
+            nc.scalar.copy(z[0][:, a:b], bank[:])
 
-        for e in range(E):
-            lst = offs2_t[:, e * LIST_COLS : (e + 1) * LIST_COLS]
-            nc.vector.tensor_copy(cg_words[:, e * C : (e + 1) * C, 1], c_words.indirect(lst))
-            if e > 0:
-                quantise(e - 1)
-        quantise(E - 1)
+        cuts = list(range(0, S - C + 1, C)) + [S - C // 2, S]
+        for i in range(len(cuts) - 1):
+            a, b = cuts[i], cuts[i + 1]
+            nc.vector.tensor_copy(cg_words[:, a:b, 1], c_words.indirect(offs2_t[:, a // 16 : b // 16]))
+            if i > 0:
+                quantise(cuts[i - 1], a)
+        quantise(cuts[-2], S)
         for t in range(1, PACK):
             for group in pairs:
                 experts(cq_w, cq_s, z[t], t, group)
@@ -206,9 +222,20 @@ def tile_moe_uni_none_kernel(
             else:
                 backs.append(back)
         last = keep.tile([P, 2, T], F32, name="last")
-        for u in range(2):
-            gated(z[2 + u], pos_b, gate_b, 2, last[:, u, :])
-        for u in range(2):
-            res = ring.tile([P, T], F32, name="res", bufs=4)
-            nc.vector.tensor_tensor(res[:], backs[u][:], last[:, u, :], ADD)
-            nc.sync.dma_start(out_rows[:, 2 + u, :], res[:])
+        tail = keep.tile([P, 2, T], F32, name="tail")
+
+        def last_term(u, a, b):
+            nc.vector.tensor_tensor(
+                last[:, u, a:b], z[2 + u][:].indirect(pos_b[2][:, a // 16 : b // 16]), gate_b[:, 2, a:b], MULT
+            )
+
+        def finish(u, a, b, queue):
+            nc.vector.tensor_tensor(tail[:, u, a:b], backs[u][:, a:b], last[:, u, a:b], ADD)
+            queue.dma_start(out_rows[:, 2 + u, a:b], tail[:, u, a:b])
+
+        last_term(0, 0, T)
+        last_term(1, 0, T // 2)
+        finish(0, 0, T, nc.sync)
+        last_term(1, T // 2, T)
+        finish(1, 0, T // 2, nc.scalar)
+        finish(1, T // 2, T, nc.sync)

@@ -30,9 +30,9 @@ def tile_moe_uni_none_kernel(
     with ExitStack() as ctx:
         keep = ctx.enter_context(tc.tile_pool(name="keep", bufs=1))
         ring = ctx.enter_context(tc.tile_pool(name="ring", bufs=2))
-        mm_psum = ctx.enter_context(tc.psum_pool(name="mm_psum", bufs=4))
+        mm_psum = ctx.enter_context(tc.psum_pool(name="mm_psum", bufs=3))
         sum_psum = ctx.enter_context(tc.psum_pool(name="sum_psum", bufs=2))
-        back_psum = ctx.enter_context(tc.psum_pool(name="back_psum", bufs=2))
+        back_psum = ctx.enter_context(tc.psum_pool(name="back_psum", bufs=3))
 
         def load_list(src, name):
             lst = keep.tile([P, src.shape[1]], U16, name=name)
@@ -56,9 +56,10 @@ def tile_moe_uni_none_kernel(
         nc.sync.dma_start(w_w[:], w_words.rearrange("e s p n -> p (e s) n").bitcast(I32))
         for q in range(4):
             nc.sync.dma_start(x_s[32 * q : 32 * q + 4, :], x_scales[0, 4 * q : 4 * q + 4, :].bitcast(I32))
-        pos_a = [load_list(src, "pos_a%d" % r) for r, src in enumerate((pos1, pos2, pos3))]
+        pos_a = [load_list(pos1, "pos_a0")]
         gate_a = keep.tile([P, 3, T], F32, name="gate_a")
         nc.sync.dma_start(gate_a[:], gate1.rearrange("r p n -> p r n"))
+        pos_a += [load_list(pos2, "pos_a1"), load_list(pos3, "pos_a2")]
         offs2_t = load_list(offs2, "offs2_t")
         pos_b = [load_list(src, "pos_b%d" % r) for r, src in enumerate((pos4, pos5, pos6))]
         gate_b = keep.tile([P, 3, T], F32, name="gate_b")
@@ -93,8 +94,8 @@ def tile_moe_uni_none_kernel(
                 )
             nc.scalar.copy(dst[:, group[0] * C : (group[-1] + 1) * C], bank[:])
 
-        def gated(window, pos, gate, r, dst):
-            nc.vector.tensor_tensor(dst, window[:].indirect(pos[r][:]), gate[:, r, :], MULT)
+        def gated(window, pos, gate, r, dst, a=0, b=T):
+            nc.vector.tensor_tensor(dst[:, a:b], window[:].indirect(pos[r][:, a // 16 : b // 16]), gate[:, r, a:b], MULT)
 
         def add_turned(bank, term, first, last):
             for b in range(4):
@@ -111,7 +112,7 @@ def tile_moe_uni_none_kernel(
             bank = sum_psum.tile([P, 4, P], F32, name="sum_bank")
             for r in range(terms):
                 term = ring.tile([P, T], F32, name="term", bufs=4)
-                gated(window, pos, gate, r, term[:])
+                gated(window, pos, gate, r, term)
                 add_turned(bank, term, r == 0, r == terms - 1)
             turned = ring.tile([P, 4, P], dtype, name="turned")
             nc.scalar.copy(turned[:], bank[:])
@@ -154,8 +155,9 @@ def tile_moe_uni_none_kernel(
                 nc.tensor.transpose(halves[b // 2][:, u, (b % 2) * P : (b % 2 + 1) * P], turned[:, b, :], ident_f[:])
         combine_single(1)
         third = keep.tile([P, 2, T], F32, name="third")
-        for u in range(2):
-            gated(y[2 + u], pos_a, gate_a, 2, third[:, u, :])
+        gated(y[2], pos_a, gate_a, 2, third[:, 0, :])
+        for h in range(2):
+            gated(y[3], pos_a, gate_a, 2, third[:, 1, :], h * T // 2, (h + 1) * T // 2)
         c_pair = keep.tile([P, T, 2], BF16, name="c_pair", align_bytes=64)
         for h in range(2):
             cols = slice(h * T // 2, (h + 1) * T // 2)
@@ -195,47 +197,73 @@ def tile_moe_uni_none_kernel(
                 start=True,
                 stop=True,
             )
-            nc.scalar.copy(z[0][:, a:b], bank[:])
+            return bank
 
         cuts = list(range(0, S - C + 1, C)) + [S - C // 2, S]
         for i in range(len(cuts) - 1):
             a, b = cuts[i], cuts[i + 1]
             nc.vector.tensor_copy(cg_words[:, a:b, 1], c_words.indirect(offs2_t[:, a // 16 : b // 16]))
-            if i > 0:
-                quantise(cuts[i - 1], a)
-        quantise(cuts[-2], S)
-        for t in range(1, PACK):
+            if 0 < i < len(cuts) - 2:
+                nc.scalar.copy(z[0][:, cuts[i - 1] : a], quantise(cuts[i - 1], a)[:])
+        late = [(cuts[i], cuts[i + 1], quantise(cuts[i], cuts[i + 1])) for i in (-3, -2)]
+        for a, b, bank in late:
+            nc.vector.tensor_copy(z[0][:, a:b], bank[:])
+        for t in (1, 3, 2):
             for group in pairs:
                 experts(cq_w, cq_s, z[t], t, group)
 
         out_rows = out.rearrange("(p t) n -> p t n", t=PACK)
-        backs = []
-        for t in range(PACK):
-            turned = turned_sum(z[t], pos_b, gate_b, 3 if t < 2 else 2, F32)
-            back = back_psum.tile([P, T], F32, name="back")
-            for b in range(4):
+        res = keep.tile([P, PACK, T], F32, name="res")
+
+        def turn_back(turned, blocks):
+            back = back_psum.tile([P, blocks * P], F32, name="back")
+            for b in range(blocks):
                 nc.tensor.transpose(back[:, b * P : (b + 1) * P], turned[:, b, :], ident_f[:])
-            if t < 2:
-                res = ring.tile([P, T], F32, name="res", bufs=4)
-                nc.scalar.copy(res[:], back[:])
-                nc.sync.dma_start(out_rows[:, t, :], res[:])
-            else:
-                backs.append(back)
-        last = keep.tile([P, 2, T], F32, name="last")
-        tail = keep.tile([P, 2, T], F32, name="tail")
+            return back
 
-        def last_term(u, a, b):
-            nc.vector.tensor_tensor(
-                last[:, u, a:b], z[2 + u][:].indirect(pos_b[2][:, a // 16 : b // 16]), gate_b[:, 2, a:b], MULT
-            )
+        for t in range(2):
+            back = turn_back(turned_sum(z[t], pos_b, gate_b, 3, F32), 4)
+            nc.scalar.copy(res[:, t, :], back[:])
+            nc.sync.dma_start(out_rows[:, t, :], res[:, t, :])
+        partial = turn_back(turned_sum(z[3], pos_b, gate_b, 2, F32), 4)
 
-        def finish(u, a, b, queue):
-            nc.vector.tensor_tensor(tail[:, u, a:b], backs[u][:, a:b], last[:, u, a:b], ADD)
-            queue.dma_start(out_rows[:, 2 + u, a:b], tail[:, u, a:b])
+        terms = [ring.tile([P, T], F32, name="term", bufs=4) for r in range(3)]
+        banks = [sum_psum.tile([P, 2, P], F32, name="sum_bank") for h in range(2)]
 
-        last_term(0, 0, T)
-        last_term(1, 0, T // 2)
-        finish(0, 0, T, nc.sync)
-        last_term(1, T // 2, T)
-        finish(1, 0, T // 2, nc.scalar)
-        finish(1, T // 2, T, nc.sync)
+        def add_half(r, h):
+            for b in range(2):
+                nc.tensor.matmul(
+                    banks[h][:, b, :],
+                    lhsT=terms[r][:, (2 * h + b) * P : (2 * h + b + 1) * P],
+                    rhs=ident_f[:],
+                    is_transpose=True,
+                    start=(r == 0 and b == 0),
+                    stop=(r == 2 and b == 1),
+                )
+
+        for r in range(2):
+            gated(z[2], pos_b, gate_b, r, terms[r])
+            for h in range(2):
+                add_half(r, h)
+        for h in range(2):
+            a, b = h * T // 2, (h + 1) * T // 2
+            gated(z[2], pos_b, gate_b, 2, terms[2], a, b)
+            add_half(2, h)
+            turned = ring.tile([P, 2, P], F32, name="turned")
+            nc.scalar.copy(turned[:], banks[h][:])
+            back = turn_back(turned, 2)
+            nc.scalar.copy(res[:, 2, a:b], back[:])
+            nc.scalar.dma_start(out_rows[:, 2, a:b], res[:, 2, a:b])
+
+        last = keep.tile([P, T], F32, name="last")
+
+        def finish(a, b):
+            nc.vector.tensor_tensor(res[:, 3, a:b], partial[:, a:b], last[:, a:b], ADD)
+            nc.sync.dma_start(out_rows[:, 3, a:b], res[:, 3, a:b])
+
+        tail = [0, T // 2, 3 * T // 4, T]
+        for i in range(3):
+            gated(z[3], pos_b, gate_b, 2, last, tail[i], tail[i + 1])
+            if i > 0:
+                finish(tail[i - 1], tail[i])
+        finish(tail[2], T)

@@ -30,9 +30,9 @@ def tile_moe_uni_none_kernel(
     with ExitStack() as ctx:
         keep = ctx.enter_context(tc.tile_pool(name="keep", bufs=1))
         ring = ctx.enter_context(tc.tile_pool(name="ring", bufs=2))
-        mm_psum = ctx.enter_context(tc.psum_pool(name="mm_psum", bufs=3))
+        mm_psum = ctx.enter_context(tc.psum_pool(name="mm_psum", bufs=5))
         sum_psum = ctx.enter_context(tc.psum_pool(name="sum_psum", bufs=2))
-        back_psum = ctx.enter_context(tc.psum_pool(name="back_psum", bufs=3))
+        back_psum = ctx.enter_context(tc.psum_pool(name="back_psum", bufs=1))
 
         def load_list(src, name):
             lst = keep.tile([P, src.shape[1]], U16, name=name)
@@ -77,11 +77,11 @@ def tile_moe_uni_none_kernel(
             words = w_w[:].rearrange("p e n -> p (e n)").bitcast(U16).rearrange("p (m t) -> p m t", t=PACK)
             scales = w_s[:].rearrange("p e n -> p (e n)").bitcast(U8).rearrange("p (m t) -> p m t", t=PACK)
             nc.gpsimd.tensor_copy(wp_s[t][:], scales[:, :, t])
-            engine = nc.vector if t % 2 == 0 else nc.gpsimd
+            engine = nc.vector if t < 2 else nc.gpsimd
             engine.tensor_copy(wp_w[t][:].bitcast(U16), words[:, :, t])
 
-        def experts(codes, scales, dst, t, group):
-            bank = mm_psum.tile([P, len(group) * C], F32, name="bank")
+        def experts(codes, scales, dst, t, group, pool=mm_psum):
+            bank = pool.tile([P, len(group) * C], F32, name="bank")
             for j, e in enumerate(group):
                 nc.tensor.matmul_mx(
                     out=bank[:, j * C : (j + 1) * C],
@@ -111,7 +111,7 @@ def tile_moe_uni_none_kernel(
         def turned_sum(window, pos, gate, terms, dtype):
             bank = sum_psum.tile([P, 4, P], F32, name="sum_bank")
             for r in range(terms):
-                term = ring.tile([P, T], F32, name="term", bufs=4)
+                term = ring.tile([P, T], F32, name="term", bufs=6)
                 gated(window, pos, gate, r, term)
                 add_turned(bank, term, r == 0, r == terms - 1)
             turned = ring.tile([P, 4, P], dtype, name="turned")
@@ -133,37 +133,47 @@ def tile_moe_uni_none_kernel(
             lst = offs_t[:, e * LIST_COLS : (e + 1) * LIST_COLS]
             nc.vector.tensor_copy(xg_s[:, e * C : (e + 1) * C], x_s[:].bitcast(U8).indirect(lst))
             experts(xg_w, xg_s, y[0], 0, (e,))
-        for t in (2, 3, 1):
+        for t in (1, 2, 3):
             permute_weights(t)
             for group in pairs:
-                experts(xg_w, xg_s, y[t], t, group)
+                experts(xg_w, xg_s, y[t], t, group, back_psum if (t, group) == (3, pairs[-1]) else mm_psum)
 
         c_single = [keep.tile([P, T], BF16, name="c_single%d" % t) for t in range(2)]
 
         def combine_single(t):
             turned = turned_sum(y[t], pos_a, gate_a, 3, BF16)
-            back = sum_psum.tile([P, T], BF16, name="sum_bank")
+            back = back_psum.tile([P, T], BF16, name="bank")
             for b in range(4):
                 nc.tensor.transpose(back[:, b * P : (b + 1) * P], turned[:, b, :], ident_b[:])
             nc.scalar.copy(c_single[t][:], back[:])
 
-        combine_single(0)
-        halves = [back_psum.tile([P, 2, T // 2], F32, name="back") for h in range(2)]
-        for u in range(2):
-            turned = turned_sum(y[2 + u], pos_a, gate_a, 2, F32)
+        def turn_back(turned):
+            back = back_psum.tile([P, T], F32, name="bank")
             for b in range(4):
-                nc.tensor.transpose(halves[b // 2][:, u, (b % 2) * P : (b % 2 + 1) * P], turned[:, b, :], ident_f[:])
-        combine_single(1)
+                nc.tensor.transpose(back[:, b * P : (b + 1) * P], turned[:, b, :], ident_f[:])
+            return back
+
+        def two_terms(window, pos, gate):
+            terms = [ring.tile([P, T], F32, name="term", bufs=6) for r in range(2)]
+            for r in range(2):
+                gated(window, pos, gate, r, terms[r])
+            return terms
+
+        for t in range(2):
+            combine_single(t)
+        first_two = keep.tile([P, 2, T], F32, name="first_two")
         third = keep.tile([P, 2, T], F32, name="third")
-        gated(y[2], pos_a, gate_a, 2, third[:, 0, :])
-        for h in range(2):
-            gated(y[3], pos_a, gate_a, 2, third[:, 1, :], h * T // 2, (h + 1) * T // 2)
+        for u in range(2):
+            terms = two_terms(y[2 + u], pos_a, gate_a)
+            gated(y[2 + u], pos_a, gate_a, 2, third[:, u, :], 0, T // 2)
+            nc.vector.tensor_tensor(first_two[:, u, :], terms[0][:], terms[1][:], ADD)
+            gated(y[2 + u], pos_a, gate_a, 2, third[:, u, :], T // 2, T)
         c_pair = keep.tile([P, T, 2], BF16, name="c_pair", align_bytes=64)
         for h in range(2):
             cols = slice(h * T // 2, (h + 1) * T // 2)
             nc.vector.tensor_tensor(
                 c_pair[:, cols, :],
-                halves[h][:].rearrange("p u n -> p n u"),
+                first_two[:, :, cols].rearrange("p u n -> p n u"),
                 third[:, :, cols].rearrange("p u n -> p n u"),
                 ADD,
             )
@@ -208,53 +218,19 @@ def tile_moe_uni_none_kernel(
         late = [(cuts[i], cuts[i + 1], quantise(cuts[i], cuts[i + 1])) for i in (-3, -2)]
         for a, b, bank in late:
             nc.vector.tensor_copy(z[0][:, a:b], bank[:])
-        for t in (1, 3, 2):
+        for t in (1, 2, 3):
             for group in pairs:
                 experts(cq_w, cq_s, z[t], t, group)
 
         out_rows = out.rearrange("(p t) n -> p t n", t=PACK)
         res = keep.tile([P, PACK, T], F32, name="res")
 
-        def turn_back(turned, blocks):
-            back = back_psum.tile([P, blocks * P], F32, name="back")
-            for b in range(blocks):
-                nc.tensor.transpose(back[:, b * P : (b + 1) * P], turned[:, b, :], ident_f[:])
-            return back
+        for t in range(3):
+            nc.scalar.copy(res[:, t, :], turn_back(turned_sum(z[t], pos_b, gate_b, 3, F32))[:])
+            nc.scalar.dma_start(out_rows[:, t, :], res[:, t, :])
 
-        for t in range(2):
-            back = turn_back(turned_sum(z[t], pos_b, gate_b, 3, F32), 4)
-            nc.scalar.copy(res[:, t, :], back[:])
-            nc.sync.dma_start(out_rows[:, t, :], res[:, t, :])
-        partial = turn_back(turned_sum(z[3], pos_b, gate_b, 2, F32), 4)
-
-        terms = [ring.tile([P, T], F32, name="term", bufs=4) for r in range(3)]
-        banks = [sum_psum.tile([P, 2, P], F32, name="sum_bank") for h in range(2)]
-
-        def add_half(r, h):
-            for b in range(2):
-                nc.tensor.matmul(
-                    banks[h][:, b, :],
-                    lhsT=terms[r][:, (2 * h + b) * P : (2 * h + b + 1) * P],
-                    rhs=ident_f[:],
-                    is_transpose=True,
-                    start=(r == 0 and b == 0),
-                    stop=(r == 2 and b == 1),
-                )
-
-        for r in range(2):
-            gated(z[2], pos_b, gate_b, r, terms[r])
-            for h in range(2):
-                add_half(r, h)
-        for h in range(2):
-            a, b = h * T // 2, (h + 1) * T // 2
-            gated(z[2], pos_b, gate_b, 2, terms[2], a, b)
-            add_half(2, h)
-            turned = ring.tile([P, 2, P], F32, name="turned")
-            nc.scalar.copy(turned[:], banks[h][:])
-            back = turn_back(turned, 2)
-            nc.scalar.copy(res[:, 2, a:b], back[:])
-            nc.scalar.dma_start(out_rows[:, 2, a:b], res[:, 2, a:b])
-
+        terms = two_terms(z[3], pos_b, gate_b)
+        partial = keep.tile([P, T], F32, name="partial")
         last = keep.tile([P, T], F32, name="last")
 
         def finish(a, b):
@@ -264,6 +240,8 @@ def tile_moe_uni_none_kernel(
         tail = [0, T // 2, 3 * T // 4, T]
         for i in range(3):
             gated(z[3], pos_b, gate_b, 2, last, tail[i], tail[i + 1])
-            if i > 0:
+            if i == 0:
+                nc.vector.tensor_tensor(partial[:], terms[0][:], terms[1][:], ADD)
+            else:
                 finish(tail[i - 1], tail[i])
         finish(tail[2], T)

@@ -18,8 +18,13 @@ COPY = mybir.ActivationFunctionType.Copy
 K, T, E, C = 512, 512, 6, 256
 S = E * C
 P = 128
-PACK = 4
-LIST_COLS = C // 16
+PLANES = 4
+CHOICES = 3
+QUADS = 4
+BLOCKS = T // P
+PER_COL = 16
+BANK = 512
+WORD_GATHER = 384
 FLOPS = 2 * 2 * K * K * S
 
 
@@ -30,8 +35,8 @@ def tile_moe_uni_none_kernel(
     with ExitStack() as ctx:
         keep = ctx.enter_context(tc.tile_pool(name="keep", bufs=1))
         ring = ctx.enter_context(tc.tile_pool(name="ring", bufs=2))
-        mm_psum = ctx.enter_context(tc.psum_pool(name="mm_psum", bufs=5))
-        sum_psum = ctx.enter_context(tc.psum_pool(name="sum_psum", bufs=2))
+        mm_psum = ctx.enter_context(tc.psum_pool(name="mm_psum", bufs=6))
+        sum_psum = ctx.enter_context(tc.psum_pool(name="sum_psum", bufs=1))
         back_psum = ctx.enter_context(tc.psum_pool(name="back_psum", bufs=1))
 
         def load_list(src, name):
@@ -39,8 +44,11 @@ def tile_moe_uni_none_kernel(
             nc.sync.dma_start(lst[:], src)
             return lst
 
+        def entries(lst, a, b):
+            return lst[:, a // PER_COL : b // PER_COL]
+
         x_w = keep.tile([P, T], I32, name="x_w", align_bytes=64)
-        x_s = keep.tile([P, T // 4], I32, name="x_s", align_bytes=64)
+        x_s = keep.tile([P, T // 4], I32, name="x_s", tag="after_tokens", align_bytes=64)
         w_w = keep.tile([P, E, K // 2], I32, name="w_w", align_bytes=64)
         w_s = keep.tile([P, E, K // 4], I32, name="w_s", align_bytes=64)
         nc.vector.memset(x_s[:], 0)
@@ -48,21 +56,21 @@ def tile_moe_uni_none_kernel(
 
         offs_t = load_list(offs, "offs_t")
         nc.scalar.dma_start(x_w[:], x_words.rearrange("s p t d -> p (s t d)").bitcast(I32))
-        for q in range(4):
+        for q in range(QUADS):
             nc.sync.dma_start(
                 w_s[32 * q : 32 * q + 4, :, :],
                 w_scales[:, 0, 4 * q : 4 * q + 4, :].rearrange("e b n -> b e n").bitcast(I32),
             )
         nc.sync.dma_start(w_w[:], w_words.rearrange("e s p n -> p (e s) n").bitcast(I32))
-        for q in range(4):
+        for q in range(QUADS):
             nc.sync.dma_start(x_s[32 * q : 32 * q + 4, :], x_scales[0, 4 * q : 4 * q + 4, :].bitcast(I32))
         pos_a = [load_list(pos1, "pos_a0")]
-        gate_a = keep.tile([P, 3, T], F32, name="gate_a")
+        gate_a = keep.tile([P, CHOICES, T], F32, name="gate_a")
         nc.sync.dma_start(gate_a[:], gate1.rearrange("r p n -> p r n"))
         pos_a += [load_list(pos2, "pos_a1"), load_list(pos3, "pos_a2")]
         offs2_t = load_list(offs2, "offs2_t")
         pos_b = [load_list(src, "pos_b%d" % r) for r, src in enumerate((pos4, pos5, pos6))]
-        gate_b = keep.tile([P, 3, T], F32, name="gate_b")
+        gate_b = keep.tile([P, CHOICES, T], F32, name="gate_b")
         nc.sync.dma_start(gate_b[:], gate2.rearrange("r p n -> p r n"))
 
         ident_f = keep.tile([P, P], F32, name="ident_f")
@@ -70,178 +78,159 @@ def tile_moe_uni_none_kernel(
         make_identity(nc, ident_f[:])
         make_identity(nc, ident_b[:])
 
-        wp_w = [keep.tile([P, E * P * 2], U8, name="wp_w%d" % t, align_bytes=64) for t in range(PACK)]
-        wp_s = [keep.tile([P, E * P], U8, name="wp_s%d" % t, align_bytes=64) for t in range(PACK)]
+        plane_s = [keep.tile([P, E * P], U8, name="plane_s%d" % t, align_bytes=64) for t in range(PLANES)]
+        w_words16 = w_w[:].rearrange("p e n -> p (e n)").bitcast(U16).rearrange("p (m t) -> p t m", t=PLANES)
+        w_scale_bytes = w_s[:].rearrange("p e n -> p (e n)").bitcast(U8).rearrange("p (m t) -> p t m", t=PLANES)
+        first_w = keep.tile([P, E * P * 2], U8, name="first_w", align_bytes=64)
+        plane_w = [first_w[:]]
+        for t in range(PLANES):
+            nc.gpsimd.tensor_copy(plane_s[t][:], w_scale_bytes[:, t, :])
+            if t == 0:
+                nc.gpsimd.tensor_copy(plane_w[0].bitcast(U16), w_words16[:, 0, :])
 
-        def permute_weights(t):
-            words = w_w[:].rearrange("p e n -> p (e n)").bitcast(U16).rearrange("p (m t) -> p m t", t=PACK)
-            scales = w_s[:].rearrange("p e n -> p (e n)").bitcast(U8).rearrange("p (m t) -> p m t", t=PACK)
-            nc.gpsimd.tensor_copy(wp_s[t][:], scales[:, :, t])
-            engine = nc.vector if t < 2 else nc.gpsimd
-            engine.tensor_copy(wp_w[t][:].bitcast(U16), words[:, :, t])
-
-        def experts(codes, scales, dst, t, group, pool=mm_psum):
-            bank = pool.tile([P, len(group) * C], F32, name="bank")
-            for j, e in enumerate(group):
+        def multiply(codes, scales, t, a, b, pool):
+            bank = pool.tile([P, b - a], F32, name="bank")
+            for lo in range(a, b, C):
+                e, hi = lo // C, min(lo + C, b)
                 nc.tensor.matmul_mx(
-                    out=bank[:, j * C : (j + 1) * C],
-                    lhsT=wp_w[t][:, e * 2 * P : (e + 1) * 2 * P].bitcast(FP4X4),
-                    lhsT_scale=wp_s[t][:, e * P : (e + 1) * P],
-                    rhs=codes[:, e * C : (e + 1) * C].bitcast(FP8X4),
-                    rhs_scale=scales[:, e * C : (e + 1) * C],
+                    out=bank[:, lo - a : hi - a],
+                    lhsT=plane_w[t][:, e * 2 * P : (e + 1) * 2 * P].bitcast(FP4X4),
+                    lhsT_scale=plane_s[t][:, e * P : (e + 1) * P],
+                    rhs=codes[:, lo:hi].bitcast(FP8X4),
+                    rhs_scale=scales[:, lo:hi],
                     start=True,
                     stop=True,
                 )
-            nc.scalar.copy(dst[:, group[0] * C : (group[-1] + 1) * C], bank[:])
+            return bank
+
+        borrowed = {(PLANES - 1, 0): sum_psum, (PLANES - 1, S - BANK): back_psum}
+
+        def whole_plane(codes, scales, t, dst):
+            for a in range(0, S, BANK):
+                bank = multiply(codes, scales, t, a, a + BANK, borrowed.get((t, a), mm_psum))
+                nc.scalar.copy(dst[:, a : a + BANK], bank[:])
 
         def gated(window, pos, gate, r, dst, a=0, b=T):
-            nc.vector.tensor_tensor(dst[:, a:b], window[:].indirect(pos[r][:, a // 16 : b // 16]), gate[:, r, a:b], MULT)
+            nc.vector.tensor_tensor(dst[:, a:b], window[:].indirect(entries(pos[r], a, b)), gate[:, r, a:b], MULT)
 
-        def add_turned(bank, term, first, last):
-            for b in range(4):
-                nc.tensor.matmul(
-                    bank[:, b, :],
-                    lhsT=term[:, b * P : (b + 1) * P],
-                    rhs=ident_f[:],
-                    is_transpose=True,
-                    start=(first and b == 0),
-                    stop=(last and b == 3),
-                )
-
-        def turned_sum(window, pos, gate, terms, dtype):
-            bank = sum_psum.tile([P, 4, P], F32, name="sum_bank")
-            for r in range(terms):
-                term = ring.tile([P, T], F32, name="term", bufs=6)
+        def sum_on_tensor(window, pos, gate, ident):
+            bank = sum_psum.tile([P, BLOCKS, P], F32, name="bank")
+            for r in range(CHOICES):
+                term = ring.tile([P, T], F32, name="term", bufs=3 * CHOICES)
                 gated(window, pos, gate, r, term)
-                add_turned(bank, term, r == 0, r == terms - 1)
-            turned = ring.tile([P, 4, P], dtype, name="turned")
+                for j in range(BLOCKS):
+                    nc.tensor.matmul(
+                        bank[:, j, :],
+                        lhsT=term[:, j * P : (j + 1) * P],
+                        rhs=ident_f[:],
+                        is_transpose=True,
+                        start=(r == 0 and j == 0),
+                        stop=(r == CHOICES - 1 and j == BLOCKS - 1),
+                    )
+            turned = ring.tile([P, BLOCKS, P], ident.dtype, name="turned")
             nc.scalar.copy(turned[:], bank[:])
-            return turned
-
-        pairs = [(e, e + 1) for e in range(0, E, 2)]
-
-        xg_w = keep.tile([P, S], U32, name="xg_w", align_bytes=64)
-        xg_s = keep.tile([P, S], U8, name="xg_s", align_bytes=64)
-        y = [keep.tile([P, S], F32, name="y%d" % t) for t in range(PACK)]
-
-        wide = 384
-        for a in range(0, S, wide):
-            lst = offs_t[:, a // 16 : (a + wide) // 16]
-            nc.vector.tensor_copy(xg_w[:, a : a + wide], x_w[:].bitcast(U32).indirect(lst))
-        permute_weights(0)
-        for e in range(E):
-            lst = offs_t[:, e * LIST_COLS : (e + 1) * LIST_COLS]
-            nc.vector.tensor_copy(xg_s[:, e * C : (e + 1) * C], x_s[:].bitcast(U8).indirect(lst))
-            experts(xg_w, xg_s, y[0], 0, (e,))
-        for t in (1, 2, 3):
-            permute_weights(t)
-            for group in pairs:
-                experts(xg_w, xg_s, y[t], t, group, back_psum if (t, group) == (3, pairs[-1]) else mm_psum)
-
-        c_single = [keep.tile([P, T], BF16, name="c_single%d" % t) for t in range(2)]
-
-        def combine_single(t):
-            turned = turned_sum(y[t], pos_a, gate_a, 3, BF16)
-            back = back_psum.tile([P, T], BF16, name="bank")
-            for b in range(4):
-                nc.tensor.transpose(back[:, b * P : (b + 1) * P], turned[:, b, :], ident_b[:])
-            nc.scalar.copy(c_single[t][:], back[:])
-
-        def turn_back(turned):
-            back = back_psum.tile([P, T], F32, name="bank")
-            for b in range(4):
-                nc.tensor.transpose(back[:, b * P : (b + 1) * P], turned[:, b, :], ident_f[:])
+            back = back_psum.tile([P, T], ident.dtype, name="bank")
+            for j in range(BLOCKS):
+                nc.tensor.transpose(back[:, j * P : (j + 1) * P], turned[:, j, :], ident[:])
             return back
 
-        def two_terms(window, pos, gate):
-            terms = [ring.tile([P, T], F32, name="term", bufs=6) for r in range(2)]
+        def first_two_terms(window, pos, gate):
+            terms = [ring.tile([P, T], F32, name="early_term", bufs=4) for r in range(2)]
             for r in range(2):
                 gated(window, pos, gate, r, terms[r])
             return terms
 
+        xg_w = keep.tile([P, S], U32, name="xg_w", align_bytes=64)
+        xg_s = keep.tile([P, S], U8, name="xg_s", align_bytes=64)
+        y = [keep.tile([P, S], F32, name="y%d" % t) for t in range(PLANES)]
+
+        for a in range(0, S, WORD_GATHER):
+            b = a + WORD_GATHER
+            nc.vector.tensor_copy(xg_w[:, a:b], x_w[:].bitcast(U32).indirect(entries(offs_t, a, b)))
+        for a in range(0, S, C):
+            nc.vector.tensor_copy(xg_s[:, a : a + C], x_s[:].bitcast(U8).indirect(entries(offs_t, a, a + C)))
+            nc.scalar.copy(y[0][:, a : a + C], multiply(xg_w, xg_s, 0, a, a + C, mm_psum)[:])
+        other_w = keep.tile([P, PLANES - 1, E * P * 2], U8, name="other_w", tag="after_tokens", align_bytes=64)
+        for t in range(1, PLANES):
+            plane_w.append(other_w[:, t - 1, :])
+            nc.vector.tensor_copy(plane_w[t].bitcast(U16), w_words16[:, t, :])
+            whole_plane(xg_w, xg_s, t, y[t])
+
+        c_single = [keep.tile([P, T], BF16, name="c_single%d" % t) for t in range(2)]
         for t in range(2):
-            combine_single(t)
-        first_two = keep.tile([P, 2, T], F32, name="first_two")
-        third = keep.tile([P, 2, T], F32, name="third")
+            nc.scalar.copy(c_single[t][:], sum_on_tensor(y[t], pos_a, gate_a, ident_b)[:])
+
+        half = T // 2
+        partial_c = keep.tile([P, 2, T], F32, name="partial_c")
+        third_c = keep.tile([P, 2, T], F32, name="third_c")
         for u in range(2):
-            terms = two_terms(y[2 + u], pos_a, gate_a)
-            gated(y[2 + u], pos_a, gate_a, 2, third[:, u, :], 0, T // 2)
-            nc.vector.tensor_tensor(first_two[:, u, :], terms[0][:], terms[1][:], ADD)
-            gated(y[2 + u], pos_a, gate_a, 2, third[:, u, :], T // 2, T)
+            terms = first_two_terms(y[2 + u], pos_a, gate_a)
+            gated(y[2 + u], pos_a, gate_a, 2, third_c[:, u, :], 0, half)
+            nc.vector.tensor_tensor(partial_c[:, u, :], terms[0][:], terms[1][:], ADD)
+            gated(y[2 + u], pos_a, gate_a, 2, third_c[:, u, :], half, T)
         c_pair = keep.tile([P, T, 2], BF16, name="c_pair", align_bytes=64)
-        for h in range(2):
-            cols = slice(h * T // 2, (h + 1) * T // 2)
+        for a in range(0, T, half):
             nc.vector.tensor_tensor(
-                c_pair[:, cols, :],
-                first_two[:, :, cols].rearrange("p u n -> p n u"),
-                third[:, :, cols].rearrange("p u n -> p n u"),
+                c_pair[:, a : a + half, :],
+                partial_c[:, :, a : a + half].rearrange("p u n -> p n u"),
+                third_c[:, :, a : a + half].rearrange("p u n -> p n u"),
                 ADD,
             )
 
-        cg = keep.tile([P, S, PACK], BF16, name="cg", align_bytes=64)
+        cg = keep.tile([P, S, PLANES], BF16, name="cg", align_bytes=64)
         cq_w = keep.tile([P, S], U32, name="cq_w", align_bytes=64)
         cq_s = keep.tile([P, S], U8, name="cq_s", align_bytes=64)
-        z = [keep.tile([P, S], F32, name="z%d" % t) for t in range(PACK)]
-        cg_words = cg[:].rearrange("p n t -> p (n t)").bitcast(U32).rearrange("p (n u) -> p n u", u=2)
-        c_words = c_pair[:].rearrange("p n u -> p (n u)").bitcast(U32)
+        z = [keep.tile([P, S], F32, name="z%d" % t) for t in range(PLANES)]
+        cg_pairs = cg[:].rearrange("p n t -> p (n t)").bitcast(U32).rearrange("p (n u) -> p n u", u=2)
+        c_pair_words = c_pair[:].rearrange("p n u -> p (n u)").bitcast(U32)
 
         for t in range(2):
-            for e in range(E):
-                lst = offs2_t[:, e * LIST_COLS : (e + 1) * LIST_COLS]
-                nc.scalar.activation(cg[:, e * C : (e + 1) * C, t], c_single[t][:].indirect(lst), COPY)
+            for a in range(0, S, C):
+                nc.scalar.activation(cg[:, a : a + C, t], c_single[t][:].indirect(entries(offs2_t, a, a + C)), COPY)
 
-        def quantise(a, b):
+        def gather_pairs(a, b):
+            nc.vector.tensor_copy(cg_pairs[:, a:b, 1], c_pair_words.indirect(entries(offs2_t, a, b)))
+
+        def quantise_and_multiply(a, b):
             nc.vector.quantize_mx(
                 out=cq_w[:, a:b].bitcast(FP8X4),
                 scales=cq_s[:, a:b],
                 in_=cg[:, a:b, :].rearrange("p n t -> p (n t)"),
             )
-            e = a // C
-            bank = mm_psum.tile([P, b - a], F32, name="bank")
-            nc.tensor.matmul_mx(
-                out=bank[:],
-                lhsT=wp_w[0][:, e * 2 * P : (e + 1) * 2 * P].bitcast(FP4X4),
-                lhsT_scale=wp_s[0][:, e * P : (e + 1) * P],
-                rhs=cq_w[:, a:b].bitcast(FP8X4),
-                rhs_scale=cq_s[:, a:b],
-                start=True,
-                stop=True,
-            )
-            return bank
+            return multiply(cq_w, cq_s, 0, a, b, mm_psum)
 
-        cuts = list(range(0, S - C + 1, C)) + [S - C // 2, S]
-        for i in range(len(cuts) - 1):
-            a, b = cuts[i], cuts[i + 1]
-            nc.vector.tensor_copy(cg_words[:, a:b, 1], c_words.indirect(offs2_t[:, a // 16 : b // 16]))
-            if 0 < i < len(cuts) - 2:
-                nc.scalar.copy(z[0][:, cuts[i - 1] : a], quantise(cuts[i - 1], a)[:])
-        late = [(cuts[i], cuts[i + 1], quantise(cuts[i], cuts[i + 1])) for i in (-3, -2)]
-        for a, b, bank in late:
+        whole = [(a, a + C) for a in range(0, S - C, C)]
+        halves = [(S - C, S - C // 2), (S - C // 2, S)]
+        gather_pairs(*whole[0])
+        for (a, b), following in zip(whole, whole[1:] + halves[:1]):
+            gather_pairs(*following)
+            nc.scalar.copy(z[0][:, a:b], quantise_and_multiply(a, b)[:])
+        gather_pairs(*halves[1])
+        banks = [quantise_and_multiply(a, b) for a, b in halves]
+        for (a, b), bank in zip(halves, banks):
             nc.vector.tensor_copy(z[0][:, a:b], bank[:])
-        for t in (1, 2, 3):
-            for group in pairs:
-                experts(cq_w, cq_s, z[t], t, group)
+        for t in range(1, PLANES):
+            whole_plane(cq_w, cq_s, t, z[t])
 
-        out_rows = out.rearrange("(p t) n -> p t n", t=PACK)
-        res = keep.tile([P, PACK, T], F32, name="res")
+        out_planes = out.rearrange("(p t) n -> p t n", t=PLANES)
+        res = keep.tile([P, PLANES, T], F32, name="res")
+        last = PLANES - 1
+        for t in range(last):
+            nc.scalar.copy(res[:, t, :], sum_on_tensor(z[t], pos_b, gate_b, ident_f)[:])
+            nc.scalar.dma_start(out_planes[:, t, :], res[:, t, :])
 
-        for t in range(3):
-            nc.scalar.copy(res[:, t, :], turn_back(turned_sum(z[t], pos_b, gate_b, 3, F32))[:])
-            nc.scalar.dma_start(out_rows[:, t, :], res[:, t, :])
-
-        terms = two_terms(z[3], pos_b, gate_b)
-        partial = keep.tile([P, T], F32, name="partial")
-        last = keep.tile([P, T], F32, name="last")
+        terms = first_two_terms(z[last], pos_b, gate_b)
+        partial_out = keep.tile([P, T], F32, name="partial_out")
+        third_out = keep.tile([P, T], F32, name="third_out")
+        pieces = [(0, half), (half, 3 * T // 4), (3 * T // 4, T)]
 
         def finish(a, b):
-            nc.vector.tensor_tensor(res[:, 3, a:b], partial[:, a:b], last[:, a:b], ADD)
-            nc.sync.dma_start(out_rows[:, 3, a:b], res[:, 3, a:b])
+            nc.vector.tensor_tensor(res[:, last, a:b], partial_out[:, a:b], third_out[:, a:b], ADD)
+            nc.sync.dma_start(out_planes[:, last, a:b], res[:, last, a:b])
 
-        tail = [0, T // 2, 3 * T // 4, T]
-        for i in range(3):
-            gated(z[3], pos_b, gate_b, 2, last, tail[i], tail[i + 1])
-            if i == 0:
-                nc.vector.tensor_tensor(partial[:], terms[0][:], terms[1][:], ADD)
-            else:
-                finish(tail[i - 1], tail[i])
-        finish(tail[2], T)
+        gated(z[last], pos_b, gate_b, 2, third_out, *pieces[0])
+        nc.vector.tensor_tensor(partial_out[:], terms[0][:], terms[1][:], ADD)
+        for done, following in zip(pieces, pieces[1:]):
+            gated(z[last], pos_b, gate_b, 2, third_out, *following)
+            finish(*done)
+        finish(*pieces[-1])

@@ -25,6 +25,7 @@ BLOCKS = T // P
 PER_COL = 16
 BANK = 512
 WORD_GATHER = 384
+EARLY = 2
 FLOPS = 2 * 2 * K * K * S
 
 
@@ -56,20 +57,19 @@ def tile_moe_uni_none_kernel(
 
         offs_t = load_list(offs, "offs_t")
         nc.scalar.dma_start(x_w[:], x_words.rearrange("s p t d -> p (s t d)").bitcast(I32))
+        nc.sync.dma_start(w_w[:], w_words.rearrange("e s p n -> p (e s) n").bitcast(I32))
         for q in range(QUADS):
             nc.sync.dma_start(
                 w_s[32 * q : 32 * q + 4, :, :],
                 w_scales[:, 0, 4 * q : 4 * q + 4, :].rearrange("e b n -> b e n").bitcast(I32),
             )
-        nc.sync.dma_start(w_w[:], w_words.rearrange("e s p n -> p (e s) n").bitcast(I32))
         for q in range(QUADS):
             nc.sync.dma_start(x_s[32 * q : 32 * q + 4, :], x_scales[0, 4 * q : 4 * q + 4, :].bitcast(I32))
-        pos_a = [load_list(pos1, "pos_a0")]
-        gate_a = keep.tile([P, CHOICES, T], F32, name="gate_a")
-        nc.sync.dma_start(gate_a[:], gate1.rearrange("r p n -> p r n"))
-        pos_a += [load_list(pos2, "pos_a1"), load_list(pos3, "pos_a2")]
+        pos_a = [load_list(src, "pos_a%d" % r) for r, src in enumerate((pos1, pos2, pos3))]
         offs2_t = load_list(offs2, "offs2_t")
         pos_b = [load_list(src, "pos_b%d" % r) for r, src in enumerate((pos4, pos5, pos6))]
+        gate_a = keep.tile([P, CHOICES, T], F32, name="gate_a")
+        nc.sync.dma_start(gate_a[:], gate1.rearrange("r p n -> p r n"))
         gate_b = keep.tile([P, CHOICES, T], F32, name="gate_b")
         nc.sync.dma_start(gate_b[:], gate2.rearrange("r p n -> p r n"))
 
@@ -81,12 +81,12 @@ def tile_moe_uni_none_kernel(
         plane_s = [keep.tile([P, E * P], U8, name="plane_s%d" % t, align_bytes=64) for t in range(PLANES)]
         w_words16 = w_w[:].rearrange("p e n -> p (e n)").bitcast(U16).rearrange("p (m t) -> p t m", t=PLANES)
         w_scale_bytes = w_s[:].rearrange("p e n -> p (e n)").bitcast(U8).rearrange("p (m t) -> p t m", t=PLANES)
-        first_w = keep.tile([P, E * P * 2], U8, name="first_w", align_bytes=64)
-        plane_w = [first_w[:]]
+        first_w = [keep.tile([P, E * P * 2], U8, name="first_w%d" % t, align_bytes=64) for t in range(EARLY)]
+        plane_w = [tile[:] for tile in first_w]
+        for t in range(EARLY):
+            nc.gpsimd.tensor_copy(plane_w[t].bitcast(U16), w_words16[:, t, :])
         for t in range(PLANES):
             nc.gpsimd.tensor_copy(plane_s[t][:], w_scale_bytes[:, t, :])
-            if t == 0:
-                nc.gpsimd.tensor_copy(plane_w[0].bitcast(U16), w_words16[:, 0, :])
 
         def multiply(codes, scales, t, a, b, pool):
             bank = pool.tile([P, b - a], F32, name="bank")
@@ -103,20 +103,23 @@ def tile_moe_uni_none_kernel(
                 )
             return bank
 
-        borrowed = {(PLANES - 1, 0): sum_psum, (PLANES - 1, S - BANK): back_psum}
+        def bank_of_plane(codes, scales, t, a, dst, pool):
+            nc.scalar.copy(dst[:, a : a + BANK], multiply(codes, scales, t, a, a + BANK, pool)[:])
 
-        def whole_plane(codes, scales, t, dst):
+        def whole_plane(codes, scales, t, dst, borrowed):
             for a in range(0, S, BANK):
-                bank = multiply(codes, scales, t, a, a + BANK, borrowed.get((t, a), mm_psum))
-                nc.scalar.copy(dst[:, a : a + BANK], bank[:])
+                bank_of_plane(codes, scales, t, a, dst, borrowed.get((t, a), mm_psum))
 
         def gated(window, pos, gate, r, dst, a=0, b=T):
             nc.vector.tensor_tensor(dst[:, a:b], window[:].indirect(entries(pos[r], a, b)), gate[:, r, a:b], MULT)
 
-        def sum_on_tensor(window, pos, gate, ident):
-            bank = sum_psum.tile([P, BLOCKS, P], F32, name="bank")
-            for r in range(CHOICES):
-                term = ring.tile([P, T], F32, name="term", bufs=3 * CHOICES)
+        def add_turned(window, pos, gate, choices, last_tag=None, pool=sum_psum):
+            bank = pool.tile([P, BLOCKS, P], F32, name="bank")
+            for r in range(choices):
+                if last_tag is not None and r == choices - 1:
+                    term = keep.tile([P, T], F32, name="last_term", tag=last_tag, align_bytes=64)
+                else:
+                    term = ring.tile([P, T], F32, name="term", bufs=9)
                 gated(window, pos, gate, r, term)
                 for j in range(BLOCKS):
                     nc.tensor.matmul(
@@ -125,14 +128,23 @@ def tile_moe_uni_none_kernel(
                         rhs=ident_f[:],
                         is_transpose=True,
                         start=(r == 0 and j == 0),
-                        stop=(r == CHOICES - 1 and j == BLOCKS - 1),
+                        stop=(r == choices - 1 and j == BLOCKS - 1),
                     )
+            return bank
+
+        def turn_back(bank, ident, blocks):
             turned = ring.tile([P, BLOCKS, P], ident.dtype, name="turned")
             nc.scalar.copy(turned[:], bank[:])
-            back = back_psum.tile([P, T], ident.dtype, name="bank")
             for j in range(BLOCKS):
-                nc.tensor.transpose(back[:, j * P : (j + 1) * P], turned[:, j, :], ident[:])
+                nc.tensor.transpose(blocks[j], turned[:, j, :], ident[:])
+
+        def turn_back_whole(bank, ident, pool=back_psum):
+            back = pool.tile([P, T], ident.dtype, name="bank")
+            turn_back(bank, ident, [back[:, j * P : (j + 1) * P] for j in range(BLOCKS)])
             return back
+
+        def sum_on_tensor(window, pos, gate, ident):
+            return turn_back_whole(add_turned(window, pos, gate, CHOICES), ident)
 
         def first_two_terms(window, pos, gate):
             terms = [ring.tile([P, T], F32, name="early_term", bufs=4) for r in range(2)]
@@ -150,52 +162,83 @@ def tile_moe_uni_none_kernel(
         for a in range(0, S, C):
             nc.vector.tensor_copy(xg_s[:, a : a + C], x_s[:].bitcast(U8).indirect(entries(offs_t, a, a + C)))
             nc.scalar.copy(y[0][:, a : a + C], multiply(xg_w, xg_s, 0, a, a + C, mm_psum)[:])
-        other_w = keep.tile([P, PLANES - 1, E * P * 2], U8, name="other_w", tag="after_tokens", align_bytes=64)
-        for t in range(1, PLANES):
-            plane_w.append(other_w[:, t - 1, :])
+            if a > 0:
+                nc.scalar.copy(y[1][:, a - C : a], multiply(xg_w, xg_s, 1, a - C, a, mm_psum)[:])
+        nc.scalar.copy(y[1][:, S - C : S], multiply(xg_w, xg_s, 1, S - C, S, mm_psum)[:])
+        other_w = keep.tile([P, PLANES - EARLY, E * P * 2], U8, name="other_w", tag="after_tokens", align_bytes=64)
+        for t in range(EARLY, PLANES):
+            plane_w.append(other_w[:, t - EARLY, :])
             nc.vector.tensor_copy(plane_w[t].bitcast(U16), w_words16[:, t, :])
-            whole_plane(xg_w, xg_s, t, y[t])
-
-        c_single = [keep.tile([P, T], BF16, name="c_single%d" % t) for t in range(2)]
-        for t in range(2):
-            nc.scalar.copy(c_single[t][:], sum_on_tensor(y[t], pos_a, gate_a, ident_b)[:])
+        for t in range(EARLY, PLANES):
+            whole_plane(xg_w, xg_s, t, y[t], {})
 
         half = T // 2
-        partial_c = keep.tile([P, 2, T], F32, name="partial_c")
+        c_single = []
+        cg = []
+
+        def new_cg(tag):
+            cg.append(keep.tile([P, 2 * C, PLANES], BF16, name="cg", tag=tag, align_bytes=64))
+
+        def cg_slots(a, b):
+            return cg[a // (2 * C)][:, a % (2 * C) : a % (2 * C) + b - a, :]
+
+        def gather_single(t, e):
+            a = e * C
+            nc.scalar.activation(cg_slots(a, a + C)[:, :, t], c_single[t][:].indirect(entries(offs2_t, a, a + C)), COPY)
+
+
+        def partial_blocks(u):
+            return [partial_c[j // 2][:, u, (j % 2) * P : (j % 2 + 1) * P] for j in range(BLOCKS)]
+
+        back = turn_back_whole(add_turned(y[0], pos_a, gate_a, CHOICES, None, mm_psum), ident_b, sum_psum)
+        c_single.append(keep.tile([P, T], BF16, name="c_single0"))
+        nc.scalar.copy(c_single[0][:], back[:])
+        partial_c = [mm_psum.tile([P, 2, half], F32, name="bank") for h in range(2)]
+        new_cg("cg0")
+        gather_single(0, 0)
+        gather_single(0, 1)
+        back = turn_back_whole(add_turned(y[1], pos_a, gate_a, CHOICES, "after_plane1"), ident_b)
+        new_cg("after_plane1")
+        gather_single(0, 2)
+        gather_single(0, 3)
+        turn_back(add_turned(y[2], pos_a, gate_a, 2, "after_plane2"), ident_f, partial_blocks(0))
+        new_cg("after_plane2")
+        gather_single(0, 4)
+        gather_single(0, 5)
+        turn_back(add_turned(y[3], pos_a, gate_a, 2, "after_plane3"), ident_f, partial_blocks(1))
+        c_single.append(keep.tile([P, T], BF16, name="c_single1", tag="after_plane3", align_bytes=64))
+        nc.scalar.copy(c_single[1][:], back[:])
+        for e in range(E):
+            gather_single(1, e)
+
         third_c = keep.tile([P, 2, T], F32, name="third_c")
-        for u in range(2):
-            terms = first_two_terms(y[2 + u], pos_a, gate_a)
-            gated(y[2 + u], pos_a, gate_a, 2, third_c[:, u, :], 0, half)
-            nc.vector.tensor_tensor(partial_c[:, u, :], terms[0][:], terms[1][:], ADD)
-            gated(y[2 + u], pos_a, gate_a, 2, third_c[:, u, :], half, T)
-        c_pair = keep.tile([P, T, 2], BF16, name="c_pair", align_bytes=64)
+        gated(y[2], pos_a, gate_a, 2, third_c[:, 0, :])
         for a in range(0, T, half):
+            gated(y[3], pos_a, gate_a, 2, third_c[:, 1, :], a, a + half)
+        c_pair = keep.tile([P, T, 2], BF16, name="c_pair", align_bytes=64)
+        for h in range(2):
+            a = h * half
             nc.vector.tensor_tensor(
                 c_pair[:, a : a + half, :],
-                partial_c[:, :, a : a + half].rearrange("p u n -> p n u"),
+                partial_c[h][:].rearrange("p u n -> p n u"),
                 third_c[:, :, a : a + half].rearrange("p u n -> p n u"),
                 ADD,
             )
 
-        cg = keep.tile([P, S, PLANES], BF16, name="cg", align_bytes=64)
         cq_w = keep.tile([P, S], U32, name="cq_w", align_bytes=64)
         cq_s = keep.tile([P, S], U8, name="cq_s", align_bytes=64)
         z = [keep.tile([P, S], F32, name="z%d" % t) for t in range(PLANES)]
-        cg_pairs = cg[:].rearrange("p n t -> p (n t)").bitcast(U32).rearrange("p (n u) -> p n u", u=2)
         c_pair_words = c_pair[:].rearrange("p n u -> p (n u)").bitcast(U32)
 
-        for t in range(2):
-            for a in range(0, S, C):
-                nc.scalar.activation(cg[:, a : a + C, t], c_single[t][:].indirect(entries(offs2_t, a, a + C)), COPY)
-
         def gather_pairs(a, b):
-            nc.vector.tensor_copy(cg_pairs[:, a:b, 1], c_pair_words.indirect(entries(offs2_t, a, b)))
+            pairs = cg_slots(a, b).rearrange("p n t -> p (n t)").bitcast(U32).rearrange("p (n u) -> p n u", u=2)
+            nc.vector.tensor_copy(pairs[:, :, 1], c_pair_words.indirect(entries(offs2_t, a, b)))
 
         def quantise_and_multiply(a, b):
             nc.vector.quantize_mx(
                 out=cq_w[:, a:b].bitcast(FP8X4),
                 scales=cq_s[:, a:b],
-                in_=cg[:, a:b, :].rearrange("p n t -> p (n t)"),
+                in_=cg_slots(a, b).rearrange("p n t -> p (n t)"),
             )
             return multiply(cq_w, cq_s, 0, a, b, mm_psum)
 
@@ -210,7 +253,7 @@ def tile_moe_uni_none_kernel(
         for (a, b), bank in zip(halves, banks):
             nc.vector.tensor_copy(z[0][:, a:b], bank[:])
         for t in range(1, PLANES):
-            whole_plane(cq_w, cq_s, t, z[t])
+            whole_plane(cq_w, cq_s, t, z[t], {(PLANES - 1, 0): sum_psum, (PLANES - 1, S - BANK): back_psum})
 
         out_planes = out.rearrange("(p t) n -> p t n", t=PLANES)
         res = keep.tile([P, PLANES, T], F32, name="res")

@@ -197,16 +197,16 @@ def tile_moe_uni_none_kernel(
         new_cg("cg0")
         gather_single(0, 0)
         gather_single(0, 1)
-        back = turn_back_whole(add_turned(y[1], pos_a, gate_a, CHOICES, "after_plane1"), ident_b)
-        new_cg("after_plane1")
-        gather_single(0, 2)
-        gather_single(0, 3)
         turn_back(add_turned(y[2], pos_a, gate_a, 2, "after_plane2"), ident_f, partial_blocks(0))
         new_cg("after_plane2")
+        gather_single(0, 2)
+        gather_single(0, 3)
+        turn_back(add_turned(y[3], pos_a, gate_a, 2, "after_plane3"), ident_f, partial_blocks(1))
+        new_cg("after_plane3")
         gather_single(0, 4)
         gather_single(0, 5)
-        turn_back(add_turned(y[3], pos_a, gate_a, 2, "after_plane3"), ident_f, partial_blocks(1))
-        c_single.append(keep.tile([P, T], BF16, name="c_single1", tag="after_plane3", align_bytes=64))
+        back = turn_back_whole(add_turned(y[1], pos_a, gate_a, CHOICES), ident_b)
+        c_single.append(keep.tile([P, T], BF16, name="c_single1"))
         nc.scalar.copy(c_single[1][:], back[:])
         for e in range(E):
             gather_single(1, e)

@@ -25,7 +25,10 @@ BLOCKS = T // P
 PER_COL = 16
 BANK = 512
 WORD_GATHER = 384
-EARLY = 2
+EARLY = (0, 2)
+LATE = (3, 1)
+WOVEN = E - 1
+ROWS = 2048
 FLOPS = 2 * 2 * K * K * S
 
 
@@ -36,9 +39,13 @@ def tile_moe_uni_none_kernel(
     with ExitStack() as ctx:
         keep = ctx.enter_context(tc.tile_pool(name="keep", bufs=1))
         ring = ctx.enter_context(tc.tile_pool(name="ring", bufs=2))
-        mm_psum = ctx.enter_context(tc.psum_pool(name="mm_psum", bufs=6))
-        sum_psum = ctx.enter_context(tc.psum_pool(name="sum_psum", bufs=1))
-        back_psum = ctx.enter_context(tc.psum_pool(name="back_psum", bufs=1))
+        lent = ctx.enter_context(tc.tile_pool(name="lent", bufs=1))
+        pair_psum = ctx.enter_context(tc.psum_pool(name="pair_psum", bufs=1))
+
+        def in_bank(where, shape, dtype=F32):
+            return where[0].tile(shape, dtype, name="bank", tag=where[1])
+
+        own = [(pair_psum, "own0"), (pair_psum, "own1")]
 
         def load_list(src, name):
             lst = keep.tile([P, src.shape[1]], U16, name=name)
@@ -81,15 +88,15 @@ def tile_moe_uni_none_kernel(
         plane_s = [keep.tile([P, E * P], U8, name="plane_s%d" % t, align_bytes=64) for t in range(PLANES)]
         w_words16 = w_w[:].rearrange("p e n -> p (e n)").bitcast(U16).rearrange("p (m t) -> p t m", t=PLANES)
         w_scale_bytes = w_s[:].rearrange("p e n -> p (e n)").bitcast(U8).rearrange("p (m t) -> p t m", t=PLANES)
-        first_w = [keep.tile([P, E * P * 2], U8, name="first_w%d" % t, align_bytes=64) for t in range(EARLY)]
-        plane_w = [tile[:] for tile in first_w]
-        for t in range(EARLY):
+        plane_w = {}
+        for t in EARLY:
+            plane_w[t] = keep.tile([P, E * P * 2], U8, name="early_w%d" % t, align_bytes=64)[:]
             nc.gpsimd.tensor_copy(plane_w[t].bitcast(U16), w_words16[:, t, :])
-        for t in range(PLANES):
+        for t in EARLY + LATE:
             nc.gpsimd.tensor_copy(plane_s[t][:], w_scale_bytes[:, t, :])
 
-        def multiply(codes, scales, t, a, b, pool):
-            bank = pool.tile([P, b - a], F32, name="bank")
+        def multiply(codes, scales, t, a, b, k):
+            bank = in_bank(k, [P, b - a])
             for lo in range(a, b, C):
                 e, hi = lo // C, min(lo + C, b)
                 nc.tensor.matmul_mx(
@@ -103,23 +110,23 @@ def tile_moe_uni_none_kernel(
                 )
             return bank
 
-        def bank_of_plane(codes, scales, t, a, dst, pool):
-            nc.scalar.copy(dst[:, a : a + BANK], multiply(codes, scales, t, a, a + BANK, pool)[:])
+        def product(codes, scales, t, a, b, dst, k):
+            nc.scalar.copy(dst[:, a:b], multiply(codes, scales, t, a, b, k)[:])
 
-        def whole_plane(codes, scales, t, dst, borrowed):
-            for a in range(0, S, BANK):
-                bank_of_plane(codes, scales, t, a, dst, borrowed.get((t, a), mm_psum))
+        def whole_plane(codes, scales, t, dst, banks):
+            for a, k in zip(range(0, S, BANK), banks):
+                product(codes, scales, t, a, a + BANK, dst, k)
 
         def gated(window, pos, gate, r, dst, a=0, b=T):
             nc.vector.tensor_tensor(dst[:, a:b], window[:].indirect(entries(pos[r], a, b)), gate[:, r, a:b], MULT)
 
-        def add_turned(window, pos, gate, choices, last_tag=None, pool=sum_psum):
-            bank = pool.tile([P, BLOCKS, P], F32, name="bank")
+        def add_turned(window, pos, gate, choices, k, last_offset=None):
+            bank = in_bank(k, [P, BLOCKS, P])
             for r in range(choices):
-                if last_tag is not None and r == choices - 1:
-                    term = keep.tile([P, T], F32, name="last_term", tag=last_tag, align_bytes=64)
+                if last_offset is not None and r == choices - 1:
+                    term = lent.tile([P, T], F32, name="lent_term", offset=last_offset, align_bytes=64)
                 else:
-                    term = ring.tile([P, T], F32, name="term", bufs=9)
+                    term = ring.tile([P, T], F32, name="term", bufs=10)
                 gated(window, pos, gate, r, term)
                 for j in range(BLOCKS):
                     nc.tensor.matmul(
@@ -132,19 +139,19 @@ def tile_moe_uni_none_kernel(
                     )
             return bank
 
-        def turn_back(bank, ident, blocks):
-            turned = ring.tile([P, BLOCKS, P], ident.dtype, name="turned")
+        def turn_back(bank, ident, blocks, offset=None):
+            if offset is None:
+                turned = ring.tile([P, BLOCKS, P], ident.dtype, name="turned", bufs=3)
+            else:
+                turned = lent.tile([P, BLOCKS, P], ident.dtype, name="lent_turned%d" % offset, offset=offset, align_bytes=64)
             nc.scalar.copy(turned[:], bank[:])
             for j in range(BLOCKS):
                 nc.tensor.transpose(blocks[j], turned[:, j, :], ident[:])
 
-        def turn_back_whole(bank, ident, pool=back_psum):
-            back = pool.tile([P, T], ident.dtype, name="bank")
+        def turn_back_whole(bank, ident, k):
+            back = in_bank(k, [P, T], ident.dtype)
             turn_back(bank, ident, [back[:, j * P : (j + 1) * P] for j in range(BLOCKS)])
             return back
-
-        def sum_on_tensor(window, pos, gate, ident):
-            return turn_back_whole(add_turned(window, pos, gate, CHOICES), ident)
 
         def first_two_terms(window, pos, gate):
             terms = [ring.tile([P, T], F32, name="early_term", bufs=4) for r in range(2)]
@@ -159,107 +166,141 @@ def tile_moe_uni_none_kernel(
         for a in range(0, S, WORD_GATHER):
             b = a + WORD_GATHER
             nc.vector.tensor_copy(xg_w[:, a:b], x_w[:].bitcast(U32).indirect(entries(offs_t, a, b)))
-        for a in range(0, S, C):
-            nc.vector.tensor_copy(xg_s[:, a : a + C], x_s[:].bitcast(U8).indirect(entries(offs_t, a, a + C)))
-            nc.scalar.copy(y[0][:, a : a + C], multiply(xg_w, xg_s, 0, a, a + C, mm_psum)[:])
-            if a > 0:
-                nc.scalar.copy(y[1][:, a - C : a], multiply(xg_w, xg_s, 1, a - C, a, mm_psum)[:])
-        nc.scalar.copy(y[1][:, S - C : S], multiply(xg_w, xg_s, 1, S - C, S, mm_psum)[:])
-        other_w = keep.tile([P, PLANES - EARLY, E * P * 2], U8, name="other_w", tag="after_tokens", align_bytes=64)
-        for t in range(EARLY, PLANES):
-            plane_w.append(other_w[:, t - EARLY, :])
-            nc.vector.tensor_copy(plane_w[t].bitcast(U16), w_words16[:, t, :])
-        for t in range(EARLY, PLANES):
-            whole_plane(xg_w, xg_s, t, y[t], {})
-
         half = T // 2
-        c_single = []
-        cg = []
+        c_single = [keep.tile([P, T], BF16, name="c_single%d" % t) for t in range(2)]
+        c_pair = keep.tile([P, T, 2], BF16, name="c_pair", align_bytes=64)
+        rows = []
 
-        def new_cg(tag):
-            cg.append(keep.tile([P, 2 * C, PLANES], BF16, name="cg", tag=tag, align_bytes=64))
-
-        def cg_slots(a, b):
-            return cg[a // (2 * C)][:, a % (2 * C) : a % (2 * C) + b - a, :]
+        def new_rows(count):
+            for i in range(count):
+                e = len(rows)
+                rows.append(lent.tile([P, 2 * C], U32, name="rows%d" % e, offset=e * ROWS, align_bytes=64))
 
         def gather_single(t, e):
-            a = e * C
-            nc.scalar.activation(cg_slots(a, a + C)[:, :, t], c_single[t][:].indirect(entries(offs2_t, a, a + C)), COPY)
+            if e < WOVEN:
+                dst = rows[e][:, :C].bitcast(BF16).rearrange("p (n v) -> p n v", v=2)
+            else:
+                dst = rows[e][:].bitcast(BF16).rearrange("p (n v) -> p n v", v=PLANES)
+            nc.scalar.activation(dst[:, :, t], c_single[t][:].indirect(entries(offs2_t, e * C, (e + 1) * C)), COPY)
 
+        with tc.psum_pool(name="ring_psum", bufs=6) as ring_psum:
+            in_turn = (ring_psum, "in_turn")
+            for e in range(E + 1):
+                a = e * C
+                if e < E:
+                    nc.vector.tensor_copy(xg_s[:, a : a + C], x_s[:].bitcast(U8).indirect(entries(offs_t, a, a + C)))
+                    product(xg_w, xg_s, 0, a, a + C, y[0], in_turn)
+                if e > 0:
+                    product(xg_w, xg_s, EARLY[1], a - C, a, y[EARLY[1]], in_turn)
+            other_w = keep.tile([P, len(LATE), E * P * 2], U8, name="other_w", tag="after_tokens", align_bytes=64)
+            for i, t in enumerate(LATE):
+                plane_w[t] = other_w[:, i, :]
+                nc.vector.tensor_copy(plane_w[t].bitcast(U16), w_words16[:, t, :])
+            for t in LATE:
+                whole_plane(xg_w, xg_s, t, y[t], [in_turn] * 3)
 
-        def partial_blocks(u):
-            return [partial_c[j // 2][:, u, (j % 2) * P : (j % 2 + 1) * P] for j in range(BLOCKS)]
+            bank = add_turned(y[0], pos_a, gate_a, CHOICES, in_turn)
+            backs = [in_bank(own[h], [P, half], BF16) for h in range(2)]
+            turn_back(bank, ident_b, [backs[j // 2][:, (j % 2) * P : (j % 2 + 1) * P] for j in range(BLOCKS)])
+            for h in range(2):
+                nc.scalar.copy(c_single[0][:, h * half : (h + 1) * half], backs[h][:])
+            partial_c = [in_bank(in_turn, [P, 2, half]) for h in range(2)]
+            new_rows(4)
+            for e in range(4):
+                gather_single(0, e)
+            sums = [add_turned(y[2], pos_a, gate_a, 2, own[0]), add_turned(y[3], pos_a, gate_a, 2, own[1], E * ROWS)]
+            for u, offset in enumerate((E * ROWS, 4 * ROWS + ROWS // 2)):
+                blocks = [partial_c[j // 2][:, u, (j % 2) * P : (j % 2 + 1) * P] for j in range(BLOCKS)]
+                turn_back(sums[u], ident_f, blocks, offset)
+            new_rows(2)
+            for e in range(4, E):
+                gather_single(0, e)
 
-        back = turn_back_whole(add_turned(y[0], pos_a, gate_a, CHOICES, None, mm_psum), ident_b, sum_psum)
-        c_single.append(keep.tile([P, T], BF16, name="c_single0"))
-        nc.scalar.copy(c_single[0][:], back[:])
-        partial_c = [mm_psum.tile([P, 2, half], F32, name="bank") for h in range(2)]
-        new_cg("cg0")
-        gather_single(0, 0)
-        gather_single(0, 1)
-        turn_back(add_turned(y[2], pos_a, gate_a, 2, "after_plane2"), ident_f, partial_blocks(0))
-        new_cg("after_plane2")
-        gather_single(0, 2)
-        gather_single(0, 3)
-        turn_back(add_turned(y[3], pos_a, gate_a, 2, "after_plane3"), ident_f, partial_blocks(1))
-        new_cg("after_plane3")
-        gather_single(0, 4)
-        gather_single(0, 5)
-        back = turn_back_whole(add_turned(y[1], pos_a, gate_a, CHOICES), ident_b)
-        c_single.append(keep.tile([P, T], BF16, name="c_single1"))
-        nc.scalar.copy(c_single[1][:], back[:])
-        for e in range(E):
-            gather_single(1, e)
+            banks = [in_bank(own[h], [P, 2, P]) for h in range(2)]
+            for r in range(CHOICES):
+                for a, b in [(0, half), (half, T)] if r == CHOICES - 1 else [(0, T)]:
+                    term = ring.tile([P, T], F32, name="term", bufs=10)
+                    gated(y[1], pos_a, gate_a, r, term, a, b)
+                    for j in range(a // P, b // P):
+                        nc.tensor.matmul(
+                            banks[j // 2][:, j % 2, :],
+                            lhsT=term[:, j * P : (j + 1) * P],
+                            rhs=ident_f[:],
+                            is_transpose=True,
+                            start=(r == 0 and j % 2 == 0),
+                            stop=(r == CHOICES - 1 and j % 2 == 1),
+                        )
+            for h in range(2):
+                turned = ring.tile([P, 2, P], BF16, name="turned_half")
+                nc.scalar.copy(turned[:], banks[h][:])
+                back = in_bank(in_turn, [P, half], BF16)
+                for j in range(2):
+                    nc.tensor.transpose(back[:, j * P : (j + 1) * P], turned[:, j, :], ident_b[:])
+                nc.scalar.copy(c_single[1][:, h * half : (h + 1) * half], back[:])
+            for e in range(E):
+                gather_single(1, e)
 
-        third_c = keep.tile([P, 2, T], F32, name="third_c")
-        gated(y[2], pos_a, gate_a, 2, third_c[:, 0, :])
-        for a in range(0, T, half):
-            gated(y[3], pos_a, gate_a, 2, third_c[:, 1, :], a, a + half)
-        c_pair = keep.tile([P, T, 2], BF16, name="c_pair", align_bytes=64)
-        for h in range(2):
-            a = h * half
-            nc.vector.tensor_tensor(
-                c_pair[:, a : a + half, :],
-                partial_c[h][:].rearrange("p u n -> p n u"),
-                third_c[:, :, a : a + half].rearrange("p u n -> p n u"),
-                ADD,
-            )
+            thirds = [keep.tile([P, 2, half], F32, name="third_c%d" % h) for h in range(2)]
+            for h in range(2):
+                for u in range(2):
+                    a = h * half
+                    window = y[2 + u][:].indirect(entries(pos_a[2], a, a + half))
+                    nc.vector.tensor_tensor(thirds[h][:, u, :], window, gate_a[:, 2, a : a + half], MULT)
+            for h in range(2):
+                a = h * half
+                nc.vector.tensor_tensor(
+                    c_pair[:, a : a + half, :],
+                    partial_c[h][:].rearrange("p u n -> p n u"),
+                    thirds[h][:].rearrange("p u n -> p n u"),
+                    ADD,
+                )
+
+        named_psum = ctx.enter_context(tc.psum_pool(name="named_psum", bufs=1))
+        named = [(named_psum, "named%d" % k) for k in range(6)] + own
 
         cq_w = keep.tile([P, S], U32, name="cq_w", align_bytes=64)
         cq_s = keep.tile([P, S], U8, name="cq_s", align_bytes=64)
         z = [keep.tile([P, S], F32, name="z%d" % t) for t in range(PLANES)]
         c_pair_words = c_pair[:].rearrange("p n u -> p (n u)").bitcast(U32)
 
-        def gather_pairs(a, b):
-            pairs = cg_slots(a, b).rearrange("p n t -> p (n t)").bitcast(U32).rearrange("p (n u) -> p n u", u=2)
-            nc.vector.tensor_copy(pairs[:, :, 1], c_pair_words.indirect(entries(offs2_t, a, b)))
+        woven = keep.tile([P, WOVEN * 2 * C], U32, name="woven", align_bytes=64)
 
-        def quantise_and_multiply(a, b):
-            nc.vector.quantize_mx(
-                out=cq_w[:, a:b].bitcast(FP8X4),
-                scales=cq_s[:, a:b],
-                in_=cg_slots(a, b).rearrange("p n t -> p (n t)"),
-            )
-            return multiply(cq_w, cq_s, 0, a, b, mm_psum)
+        for e in range(E):
+            pairs = c_pair_words.indirect(entries(offs2_t, e * C, (e + 1) * C))
+            if e < WOVEN:
+                nc.vector.tensor_copy(rows[e][:, C:], pairs)
+                dst = woven[:, e * 2 * C : (e + 1) * 2 * C].rearrange("p (n u) -> p n u", u=2)
+                src = rows[e][:].rearrange("p (u n) -> p n u", u=2)
+                if e < WOVEN - 1:
+                    nc.gpsimd.tensor_copy(dst, src)
+                else:
+                    nc.scalar.copy(dst, src)
+            else:
+                nc.vector.tensor_copy(rows[e][:].rearrange("p (n u) -> p n u", u=2)[:, :, 1], pairs)
 
-        whole = [(a, a + C) for a in range(0, S - C, C)]
+        def quantise(a, b):
+            e = a // C
+            words = woven[:, 2 * a : 2 * b] if e < WOVEN else rows[e][:, 2 * (a - e * C) : 2 * (b - e * C)]
+            nc.vector.quantize_mx(out=cq_w[:, a:b].bitcast(FP8X4), scales=cq_s[:, a:b], in_=words.bitcast(BF16))
+
+        for e, k in enumerate((3, 4, 5, 0, 1)):
+            quantise(e * C, (e + 1) * C)
+            product(cq_w, cq_s, 0, e * C, (e + 1) * C, z[0], named[k])
         halves = [(S - C, S - C // 2), (S - C // 2, S)]
-        gather_pairs(*whole[0])
-        for (a, b), following in zip(whole, whole[1:] + halves[:1]):
-            gather_pairs(*following)
-            nc.scalar.copy(z[0][:, a:b], quantise_and_multiply(a, b)[:])
-        gather_pairs(*halves[1])
-        banks = [quantise_and_multiply(a, b) for a, b in halves]
+        banks = []
+        for (a, b), k in zip(halves, (2, 6)):
+            quantise(a, b)
+            banks.append(multiply(cq_w, cq_s, 0, a, b, named[k]))
         for (a, b), bank in zip(halves, banks):
             nc.vector.tensor_copy(z[0][:, a:b], bank[:])
         for t in range(1, PLANES):
-            whole_plane(cq_w, cq_s, t, z[t], {(PLANES - 1, 0): sum_psum, (PLANES - 1, S - BANK): back_psum})
+            whole_plane(cq_w, cq_s, t, z[t], [named[k] for k in (1, 2, 6)])
 
         out_planes = out.rearrange("(p t) n -> p t n", t=PLANES)
         res = keep.tile([P, PLANES, T], F32, name="res")
         last = PLANES - 1
-        for t in range(last):
-            nc.scalar.copy(res[:, t, :], sum_on_tensor(z[t], pos_b, gate_b, ident_f)[:])
+        for t, k in enumerate((1, 2, 6)):
+            nc.scalar.copy(res[:, t, :], turn_back_whole(add_turned(z[t], pos_b, gate_b, CHOICES, named[k]), ident_f, named[3 + t])[:])
             nc.scalar.dma_start(out_planes[:, t, :], res[:, t, :])
 
         terms = first_two_terms(z[last], pos_b, gate_b)

@@ -24,10 +24,10 @@ QUADS = 4
 BLOCKS = T // P
 PER_COL = 16
 BANK = 512
-WORD_GATHER = 384
+WIDE = 1024
 EARLY = (0, 2)
 LATE = (3, 1)
-WOVEN = E - 1
+FREE = 4 * C
 ROWS = 2048
 FLOPS = 2 * 2 * K * K * S
 
@@ -55,15 +55,18 @@ def tile_moe_uni_none_kernel(
         def entries(lst, a, b):
             return lst[:, a // PER_COL : b // PER_COL]
 
-        x_w = keep.tile([P, T], I32, name="x_w", align_bytes=64)
-        x_s = keep.tile([P, T // 4], I32, name="x_s", tag="after_tokens", align_bytes=64)
+        x_w = keep.tile([P, WIDE], I32, name="x_w", align_bytes=64)
+        x_s = keep.tile([P, WIDE // 4], I32, name="x_s", tag="after_tokens", align_bytes=64)
         w_w = keep.tile([P, E, K // 2], I32, name="w_w", align_bytes=64)
         w_s = keep.tile([P, E, K // 4], I32, name="w_s", align_bytes=64)
         nc.vector.memset(x_s[:], 0)
+        nc.vector.memset(x_w[:, T:], 0)
+        c_pair = keep.tile([P, WIDE], I32, name="c_pair", align_bytes=64)
+        nc.vector.memset(c_pair[:, T:], 0)
         nc.gpsimd.memset(w_s[:], 0)
 
         offs_t = load_list(offs, "offs_t")
-        nc.scalar.dma_start(x_w[:], x_words.rearrange("s p t d -> p (s t d)").bitcast(I32))
+        nc.scalar.dma_start(x_w[:, :T], x_words.rearrange("s p t d -> p (s t d)").bitcast(I32))
         nc.sync.dma_start(w_w[:], w_words.rearrange("e s p n -> p (e s) n").bitcast(I32))
         for q in range(QUADS):
             nc.sync.dma_start(
@@ -71,7 +74,7 @@ def tile_moe_uni_none_kernel(
                 w_scales[:, 0, 4 * q : 4 * q + 4, :].rearrange("e b n -> b e n").bitcast(I32),
             )
         for q in range(QUADS):
-            nc.sync.dma_start(x_s[32 * q : 32 * q + 4, :], x_scales[0, 4 * q : 4 * q + 4, :].bitcast(I32))
+            nc.sync.dma_start(x_s[32 * q : 32 * q + 4, : T // 4], x_scales[0, 4 * q : 4 * q + 4, :].bitcast(I32))
         pos_a = [load_list(src, "pos_a%d" % r) for r, src in enumerate((pos1, pos2, pos3))]
         offs2_t = load_list(offs2, "offs2_t")
         pos_b = [load_list(src, "pos_b%d" % r) for r, src in enumerate((pos4, pos5, pos6))]
@@ -163,35 +166,29 @@ def tile_moe_uni_none_kernel(
         xg_s = keep.tile([P, S], U8, name="xg_s", align_bytes=64)
         y = [keep.tile([P, S], F32, name="y%d" % t) for t in range(PLANES)]
 
-        for a in range(0, S, WORD_GATHER):
-            b = a + WORD_GATHER
-            nc.vector.tensor_copy(xg_w[:, a:b], x_w[:].bitcast(U32).indirect(entries(offs_t, a, b)))
+        for a in range(0, S, S // 2):
+            nc.vector.tensor_copy(xg_w[:, a : a + S // 2], x_w[:].bitcast(U32).indirect(entries(offs_t, a, a + S // 2)))
         half = T // 2
         c_single = [keep.tile([P, T], BF16, name="c_single%d" % t) for t in range(2)]
-        c_pair = keep.tile([P, T, 2], BF16, name="c_pair", align_bytes=64)
-        rows = []
+        c_pair_values = c_pair[:, :T].bitcast(BF16).rearrange("p (n u) -> p n u", u=2)
+        cg = [keep.tile([P, FREE * 2], U32, name="cg_first", align_bytes=64)]
 
-        def new_rows(count):
-            for i in range(count):
-                e = len(rows)
-                rows.append(lent.tile([P, 2 * C], U32, name="rows%d" % e, offset=e * ROWS, align_bytes=64))
+        def slot_words(a, b):
+            return cg[0][:, 2 * a : 2 * b] if b <= FREE else cg[1][:, 2 * (a - FREE) : 2 * (b - FREE)]
 
         def gather_single(t, e):
-            if e < WOVEN:
-                dst = rows[e][:, :C].bitcast(BF16).rearrange("p (n v) -> p n v", v=2)
-            else:
-                dst = rows[e][:].bitcast(BF16).rearrange("p (n v) -> p n v", v=PLANES)
+            dst = slot_words(e * C, (e + 1) * C).bitcast(BF16).rearrange("p (n v) -> p n v", v=PLANES)
             nc.scalar.activation(dst[:, :, t], c_single[t][:].indirect(entries(offs2_t, e * C, (e + 1) * C)), COPY)
 
         with tc.psum_pool(name="ring_psum", bufs=6) as ring_psum:
             in_turn = (ring_psum, "in_turn")
-            for e in range(E + 1):
-                a = e * C
-                if e < E:
-                    nc.vector.tensor_copy(xg_s[:, a : a + C], x_s[:].bitcast(U8).indirect(entries(offs_t, a, a + C)))
-                    product(xg_w, xg_s, 0, a, a + C, y[0], in_turn)
-                if e > 0:
-                    product(xg_w, xg_s, EARLY[1], a - C, a, y[EARLY[1]], in_turn)
+            for a, b in [(0, BANK), (BANK, 2 * BANK), (2 * BANK, S - C), (S - C, S)]:
+                nc.vector.tensor_copy(xg_s[:, a:b], x_s[:].bitcast(U8).indirect(entries(offs_t, a, b)))
+                product(xg_w, xg_s, 0, a, b, y[0], in_turn)
+                if a == 0:
+                    product(xg_w, xg_s, EARLY[1], a, b, y[EARLY[1]], in_turn)
+            for a in range(BANK, S, BANK):
+                product(xg_w, xg_s, EARLY[1], a, a + BANK, y[EARLY[1]], in_turn)
             other_w = keep.tile([P, len(LATE), E * P * 2], U8, name="other_w", tag="after_tokens", align_bytes=64)
             for i, t in enumerate(LATE):
                 plane_w[t] = other_w[:, i, :]
@@ -205,14 +202,13 @@ def tile_moe_uni_none_kernel(
             for h in range(2):
                 nc.scalar.copy(c_single[0][:, h * half : (h + 1) * half], backs[h][:])
             partial_c = [in_bank(in_turn, [P, 2, half]) for h in range(2)]
-            new_rows(4)
             for e in range(4):
                 gather_single(0, e)
-            sums = [add_turned(y[2], pos_a, gate_a, 2, own[0]), add_turned(y[3], pos_a, gate_a, 2, own[1], E * ROWS)]
-            for u, offset in enumerate((E * ROWS, 4 * ROWS + ROWS // 2)):
+            sums = [add_turned(y[2], pos_a, gate_a, 2, own[0]), add_turned(y[3], pos_a, gate_a, 2, own[1], 0)]
+            for u, offset in enumerate((0, ROWS)):
                 blocks = [partial_c[j // 2][:, u, (j % 2) * P : (j % 2 + 1) * P] for j in range(BLOCKS)]
                 turn_back(sums[u], ident_f, blocks, offset)
-            new_rows(2)
+            cg.append(lent.tile([P, (S - FREE) * 2], U32, name="cg_second", offset=ROWS, align_bytes=64))
             for e in range(4, E):
                 gather_single(0, e)
 
@@ -249,7 +245,7 @@ def tile_moe_uni_none_kernel(
             for h in range(2):
                 a = h * half
                 nc.vector.tensor_tensor(
-                    c_pair[:, a : a + half, :],
+                    c_pair_values[:, a : a + half, :],
                     partial_c[h][:].rearrange("p u n -> p n u"),
                     thirds[h][:].rearrange("p u n -> p n u"),
                     ADD,
@@ -261,27 +257,14 @@ def tile_moe_uni_none_kernel(
         cq_w = keep.tile([P, S], U32, name="cq_w", align_bytes=64)
         cq_s = keep.tile([P, S], U8, name="cq_s", align_bytes=64)
         z = [keep.tile([P, S], F32, name="z%d" % t) for t in range(PLANES)]
-        c_pair_words = c_pair[:].rearrange("p n u -> p (n u)").bitcast(U32)
+        c_pair_words = c_pair[:].bitcast(U32)
 
-        woven = keep.tile([P, WOVEN * 2 * C], U32, name="woven", align_bytes=64)
-
-        for e in range(E):
-            pairs = c_pair_words.indirect(entries(offs2_t, e * C, (e + 1) * C))
-            if e < WOVEN:
-                nc.vector.tensor_copy(rows[e][:, C:], pairs)
-                dst = woven[:, e * 2 * C : (e + 1) * 2 * C].rearrange("p (n u) -> p n u", u=2)
-                src = rows[e][:].rearrange("p (u n) -> p n u", u=2)
-                if e < WOVEN - 1:
-                    nc.gpsimd.tensor_copy(dst, src)
-                else:
-                    nc.scalar.copy(dst, src)
-            else:
-                nc.vector.tensor_copy(rows[e][:].rearrange("p (n u) -> p n u", u=2)[:, :, 1], pairs)
+        for a in range(0, S, BANK):
+            pairs = slot_words(a, a + BANK).rearrange("p (n u) -> p n u", u=2)
+            nc.vector.tensor_copy(pairs[:, :, 1], c_pair_words.indirect(entries(offs2_t, a, a + BANK)))
 
         def quantise(a, b):
-            e = a // C
-            words = woven[:, 2 * a : 2 * b] if e < WOVEN else rows[e][:, 2 * (a - e * C) : 2 * (b - e * C)]
-            nc.vector.quantize_mx(out=cq_w[:, a:b].bitcast(FP8X4), scales=cq_s[:, a:b], in_=words.bitcast(BF16))
+            nc.vector.quantize_mx(out=cq_w[:, a:b].bitcast(FP8X4), scales=cq_s[:, a:b], in_=slot_words(a, b).bitcast(BF16))
 
         for e, k in enumerate((3, 4, 5, 0, 1)):
             quantise(e * C, (e + 1) * C)

@@ -27,7 +27,8 @@ BANK = 512
 WIDE = 1024
 EARLY = (0, 2)
 LATE = (3, 1)
-FREE = 4 * C
+FREE = 3 * C
+CUTS = (0, FREE, S)
 ROWS = 2048
 FLOPS = 2 * 2 * K * K * S
 
@@ -123,11 +124,12 @@ def tile_moe_uni_none_kernel(
         def gated(window, pos, gate, r, dst, a=0, b=T):
             nc.vector.tensor_tensor(dst[:, a:b], window[:].indirect(entries(pos[r], a, b)), gate[:, r, a:b], MULT)
 
-        def add_turned(window, pos, gate, choices, k, last_offset=None):
+        def add_turned(window, pos, gate, choices, k, offsets=()):
             bank = in_bank(k, [P, BLOCKS, P])
             for r in range(choices):
-                if last_offset is not None and r == choices - 1:
-                    term = lent.tile([P, T], F32, name="lent_term", offset=last_offset, align_bytes=64)
+                if r >= choices - len(offsets):
+                    offset = offsets[r - choices + len(offsets)]
+                    term = lent.tile([P, T], F32, name="lent_term%d" % offset, offset=offset, align_bytes=64)
                 else:
                     term = ring.tile([P, T], F32, name="term", bufs=10)
                 gated(window, pos, gate, r, term)
@@ -193,50 +195,59 @@ def tile_moe_uni_none_kernel(
             for i, t in enumerate(LATE):
                 plane_w[t] = other_w[:, i, :]
                 nc.vector.tensor_copy(plane_w[t].bitcast(U16), w_words16[:, t, :])
-            for t in LATE:
-                whole_plane(xg_w, xg_s, t, y[t], [in_turn] * 3)
+            whole_plane(xg_w, xg_s, LATE[0], y[LATE[0]], [in_turn] * 3)
+            whole_plane(xg_w, xg_s, LATE[1], y[LATE[1]], [in_turn] * 2)
 
-            bank = add_turned(y[0], pos_a, gate_a, CHOICES, in_turn)
-            backs = [in_bank(own[h], [P, half], BF16) for h in range(2)]
-            turn_back(bank, ident_b, [backs[j // 2][:, (j % 2) * P : (j % 2 + 1) * P] for j in range(BLOCKS)])
-            for h in range(2):
-                nc.scalar.copy(c_single[0][:, h * half : (h + 1) * half], backs[h][:])
+            def add_in_halves(t, sums):
+                banks = [in_bank(k, [P, 2, P]) for k in sums]
+                for r in range(CHOICES):
+                    for a, b in [(0, half), (half, T)] if r == CHOICES - 1 else [(0, T)]:
+                        term = ring.tile([P, T], F32, name="term", bufs=10)
+                        gated(y[t], pos_a, gate_a, r, term, a, b)
+                        for j in range(a // P, b // P):
+                            nc.tensor.matmul(
+                                banks[j // 2][:, j % 2, :],
+                                lhsT=term[:, j * P : (j + 1) * P],
+                                rhs=ident_f[:],
+                                is_transpose=True,
+                                start=(r == 0 and j % 2 == 0),
+                                stop=(r == CHOICES - 1 and j % 2 == 1),
+                            )
+                return banks
+
+            def turn_halves_back(banks, places):
+                backs = []
+                for h in range(2):
+                    turned = ring.tile([P, 2, P], BF16, name="turned_half")
+                    nc.scalar.copy(turned[:], banks[h][:])
+                    backs.append(in_bank(places[h], [P, half], BF16))
+                    for j in range(2):
+                        nc.tensor.transpose(backs[h][:, j * P : (j + 1) * P], turned[:, j, :], ident_b[:])
+                return backs
+
+            def keep_halves(t, backs):
+                for h in range(2):
+                    nc.scalar.copy(c_single[t][:, h * half : (h + 1) * half], backs[h][:])
+
+            backs = turn_halves_back(add_in_halves(0, [in_turn] * 2), own)
+            product(xg_w, xg_s, LATE[1], S - BANK, S, y[LATE[1]], in_turn)
+            keep_halves(0, backs)
             partial_c = [in_bank(in_turn, [P, 2, half]) for h in range(2)]
-            for e in range(4):
+            for e in range(FREE // C):
                 gather_single(0, e)
-            sums = [add_turned(y[2], pos_a, gate_a, 2, own[0]), add_turned(y[3], pos_a, gate_a, 2, own[1], 0)]
-            for u, offset in enumerate((0, ROWS)):
+            sums = [add_turned(y[2], pos_a, gate_a, 2, own[0], (5 * ROWS, 6 * ROWS)), add_turned(y[3], pos_a, gate_a, 2, own[1])]
+            for u, offset in enumerate((0, 7 * ROWS)):
                 blocks = [partial_c[j // 2][:, u, (j % 2) * P : (j % 2 + 1) * P] for j in range(BLOCKS)]
                 turn_back(sums[u], ident_f, blocks, offset)
-            cg.append(lent.tile([P, (S - FREE) * 2], U32, name="cg_second", offset=ROWS, align_bytes=64))
-            for e in range(4, E):
+            cg.append(lent.tile([P, (S - FREE) * 2], U32, name="cg_second", offset=0, align_bytes=64))
+            for e in range(FREE // C, E):
                 gather_single(0, e)
 
-            banks = [in_bank(own[h], [P, 2, P]) for h in range(2)]
-            for r in range(CHOICES):
-                for a, b in [(0, half), (half, T)] if r == CHOICES - 1 else [(0, T)]:
-                    term = ring.tile([P, T], F32, name="term", bufs=10)
-                    gated(y[1], pos_a, gate_a, r, term, a, b)
-                    for j in range(a // P, b // P):
-                        nc.tensor.matmul(
-                            banks[j // 2][:, j % 2, :],
-                            lhsT=term[:, j * P : (j + 1) * P],
-                            rhs=ident_f[:],
-                            is_transpose=True,
-                            start=(r == 0 and j % 2 == 0),
-                            stop=(r == CHOICES - 1 and j % 2 == 1),
-                        )
-            for h in range(2):
-                turned = ring.tile([P, 2, P], BF16, name="turned_half")
-                nc.scalar.copy(turned[:], banks[h][:])
-                back = in_bank(in_turn, [P, half], BF16)
-                for j in range(2):
-                    nc.tensor.transpose(back[:, j * P : (j + 1) * P], turned[:, j, :], ident_b[:])
-                nc.scalar.copy(c_single[1][:, h * half : (h + 1) * half], back[:])
+            keep_halves(1, turn_halves_back(add_in_halves(1, own), [in_turn] * 2))
             for e in range(E):
                 gather_single(1, e)
 
-            thirds = [keep.tile([P, 2, half], F32, name="third_c%d" % h) for h in range(2)]
+            thirds = [lent.tile([P, 2, half], F32, name="third_c%d" % h, offset=(5 + h) * ROWS, align_bytes=64) for h in range(2)]
             for h in range(2):
                 for u in range(2):
                     a = h * half
@@ -259,9 +270,9 @@ def tile_moe_uni_none_kernel(
         z = [keep.tile([P, S], F32, name="z%d" % t) for t in range(PLANES)]
         c_pair_words = c_pair[:].bitcast(U32)
 
-        for a in range(0, S, BANK):
-            pairs = slot_words(a, a + BANK).rearrange("p (n u) -> p n u", u=2)
-            nc.vector.tensor_copy(pairs[:, :, 1], c_pair_words.indirect(entries(offs2_t, a, a + BANK)))
+        for a, b in zip(CUTS, CUTS[1:]):
+            pairs = slot_words(a, b).rearrange("p (n u) -> p n u", u=2)
+            nc.vector.tensor_copy(pairs[:, :, 1], c_pair_words.indirect(entries(offs2_t, a, b)))
 
         def quantise(a, b):
             nc.vector.quantize_mx(out=cq_w[:, a:b].bitcast(FP8X4), scales=cq_s[:, a:b], in_=slot_words(a, b).bitcast(BF16))

@@ -178,8 +178,13 @@ def tile_moe_uni_none_kernel(
         def slot_words(a, b):
             return cg[0][:, 2 * a : 2 * b] if b <= FREE else cg[1][:, 2 * (a - FREE) : 2 * (b - FREE)]
 
+        rows = keep.tile([P, 2 * FREE], U32, name="rows", align_bytes=64)
+
         def gather_single(t, e):
-            dst = slot_words(e * C, (e + 1) * C).bitcast(BF16).rearrange("p (n v) -> p n v", v=PLANES)
+            if e * C < FREE:
+                dst = rows[:, e * C : (e + 1) * C].bitcast(BF16).rearrange("p (n v) -> p n v", v=2)
+            else:
+                dst = slot_words(e * C, (e + 1) * C).bitcast(BF16).rearrange("p (n v) -> p n v", v=PLANES)
             nc.scalar.activation(dst[:, :, t], c_single[t][:].indirect(entries(offs2_t, e * C, (e + 1) * C)), COPY)
 
         with tc.psum_pool(name="ring_psum", bufs=6) as ring_psum:
@@ -270,9 +275,15 @@ def tile_moe_uni_none_kernel(
         z = [keep.tile([P, S], F32, name="z%d" % t) for t in range(PLANES)]
         c_pair_words = c_pair[:].bitcast(U32)
 
-        for a, b in zip(CUTS, CUTS[1:]):
-            pairs = slot_words(a, b).rearrange("p (n u) -> p n u", u=2)
-            nc.vector.tensor_copy(pairs[:, :, 1], c_pair_words.indirect(entries(offs2_t, a, b)))
+        nc.vector.tensor_copy(rows[:, FREE:], c_pair_words.indirect(entries(offs2_t, 0, FREE)))
+        pairs = slot_words(FREE, S).rearrange("p (n u) -> p n u", u=2)
+        nc.vector.tensor_copy(pairs[:, :, 1], c_pair_words.indirect(entries(offs2_t, FREE, S)))
+        for a in range(0, FREE, C):
+            weave = nc.gpsimd.tensor_copy if a + C < FREE else nc.scalar.copy
+            weave(
+                slot_words(a, a + C).rearrange("p (n u) -> p n u", u=2),
+                rows[:].rearrange("p (u n) -> p n u", u=2)[:, a : a + C, :],
+            )
 
         def quantise(a, b):
             nc.vector.quantize_mx(out=cq_w[:, a:b].bitcast(FP8X4), scales=cq_s[:, a:b], in_=slot_words(a, b).bitcast(BF16))

@@ -27,8 +27,7 @@ BANK = 512
 WIDE = 1024
 EARLY = (0, 2)
 LATE = (3, 1)
-FREE = 3 * C
-CUTS = (0, FREE, S)
+FREE = 4 * C
 ROWS = 2048
 FLOPS = 2 * 2 * K * K * S
 
@@ -173,18 +172,15 @@ def tile_moe_uni_none_kernel(
         half = T // 2
         c_single = [keep.tile([P, T], BF16, name="c_single%d" % t) for t in range(2)]
         c_pair_values = c_pair[:, :T].bitcast(BF16).rearrange("p (n u) -> p n u", u=2)
-        cg = [keep.tile([P, FREE * 2], U32, name="cg_first", align_bytes=64)]
+        cg = keep.tile([P, S * 2], U32, name="cg", align_bytes=64)
 
         def slot_words(a, b):
-            return cg[0][:, 2 * a : 2 * b] if b <= FREE else cg[1][:, 2 * (a - FREE) : 2 * (b - FREE)]
+            return cg[:, 2 * a : 2 * b]
 
-        rows = keep.tile([P, 2 * FREE], U32, name="rows", align_bytes=64)
+        rows = [keep.tile([P, 2 * BANK], U32, name="rows%d" % i, align_bytes=64) for i in range(FREE // BANK)]
 
         def gather_single(t, e):
-            if e * C < FREE:
-                dst = rows[:, e * C : (e + 1) * C].bitcast(BF16).rearrange("p (n v) -> p n v", v=2)
-            else:
-                dst = slot_words(e * C, (e + 1) * C).bitcast(BF16).rearrange("p (n v) -> p n v", v=PLANES)
+            dst = rows[e // 2][:, (e % 2) * C : (e % 2 + 1) * C].bitcast(BF16).rearrange("p (n v) -> p n v", v=2)
             nc.scalar.activation(dst[:, :, t], c_single[t][:].indirect(entries(offs2_t, e * C, (e + 1) * C)), COPY)
 
         with tc.psum_pool(name="ring_psum", bufs=6) as ring_psum:
@@ -206,7 +202,7 @@ def tile_moe_uni_none_kernel(
             def add_in_halves(t, sums):
                 banks = [in_bank(k, [P, 2, P]) for k in sums]
                 for r in range(CHOICES):
-                    for a, b in [(0, half), (half, T)] if r == CHOICES - 1 else [(0, T)]:
+                    for a, b in [(0, half), (half, T)] if r == CHOICES - 1 and t == 1 else [(0, T)]:
                         term = ring.tile([P, T], F32, name="term", bufs=10)
                         gated(y[t], pos_a, gate_a, r, term, a, b)
                         for j in range(a // P, b // P):
@@ -244,7 +240,7 @@ def tile_moe_uni_none_kernel(
             for u, offset in enumerate((0, 7 * ROWS)):
                 blocks = [partial_c[j // 2][:, u, (j % 2) * P : (j % 2 + 1) * P] for j in range(BLOCKS)]
                 turn_back(sums[u], ident_f, blocks, offset)
-            cg.append(lent.tile([P, (S - FREE) * 2], U32, name="cg_second", offset=0, align_bytes=64))
+            rows.append(lent.tile([P, 2 * BANK], U32, name="rows_last", offset=0, align_bytes=64))
             for e in range(FREE // C, E):
                 gather_single(0, e)
 
@@ -252,18 +248,16 @@ def tile_moe_uni_none_kernel(
             for e in range(E):
                 gather_single(1, e)
 
-            thirds = [lent.tile([P, 2, half], F32, name="third_c%d" % h, offset=(5 + h) * ROWS, align_bytes=64) for h in range(2)]
+            thirds = lent.tile([P, 2 * T], F32, name="thirds", offset=5 * ROWS, align_bytes=64)
+            gated(y[2], pos_a, gate_a, 2, thirds[:, :T])
             for h in range(2):
-                for u in range(2):
-                    a = h * half
-                    window = y[2 + u][:].indirect(entries(pos_a[2], a, a + half))
-                    nc.vector.tensor_tensor(thirds[h][:, u, :], window, gate_a[:, 2, a : a + half], MULT)
+                gated(y[3], pos_a, gate_a, 2, thirds[:, T:], h * half, (h + 1) * half)
             for h in range(2):
                 a = h * half
                 nc.vector.tensor_tensor(
                     c_pair_values[:, a : a + half, :],
                     partial_c[h][:].rearrange("p u n -> p n u"),
-                    thirds[h][:].rearrange("p u n -> p n u"),
+                    thirds[:].rearrange("p (u n) -> p n u", u=2)[:, a : a + half, :],
                     ADD,
                 )
 
@@ -275,14 +269,14 @@ def tile_moe_uni_none_kernel(
         z = [keep.tile([P, S], F32, name="z%d" % t) for t in range(PLANES)]
         c_pair_words = c_pair[:].bitcast(U32)
 
-        nc.vector.tensor_copy(rows[:, FREE:], c_pair_words.indirect(entries(offs2_t, 0, FREE)))
-        pairs = slot_words(FREE, S).rearrange("p (n u) -> p n u", u=2)
-        nc.vector.tensor_copy(pairs[:, :, 1], c_pair_words.indirect(entries(offs2_t, FREE, S)))
-        for a in range(0, FREE, C):
-            weave = nc.gpsimd.tensor_copy if a + C < FREE else nc.scalar.copy
+        for a, b in [(0, BANK), (BANK, 2 * BANK), (2 * BANK, S - C), (S - C, S)]:
+            lo = BANK + a % BANK
+            nc.vector.tensor_copy(rows[a // BANK][:, lo : lo + b - a], c_pair_words.indirect(entries(offs2_t, a, b)))
+        for e in range(E):
+            weave = nc.gpsimd.tensor_copy if e < E // 2 else nc.scalar.copy
             weave(
-                slot_words(a, a + C).rearrange("p (n u) -> p n u", u=2),
-                rows[:].rearrange("p (u n) -> p n u", u=2)[:, a : a + C, :],
+                slot_words(e * C, (e + 1) * C).rearrange("p (n u) -> p n u", u=2),
+                rows[e // 2][:].rearrange("p (u n) -> p n u", u=2)[:, (e % 2) * C : (e % 2 + 1) * C, :],
             )
 
         def quantise(a, b):

@@ -269,12 +269,11 @@ def tile_moe_uni_none_kernel(
         z = [keep.tile([P, S], F32, name="z%d" % t) for t in range(PLANES)]
         c_pair_words = c_pair[:].bitcast(U32)
 
-        for a, b in [(0, BANK), (BANK, 2 * BANK), (2 * BANK, S - C), (S - C, S)]:
+        for a, b in [(0, C), (C, BANK), (BANK, 2 * BANK), (2 * BANK, S - C), (S - C, S)]:
             lo = BANK + a % BANK
             nc.vector.tensor_copy(rows[a // BANK][:, lo : lo + b - a], c_pair_words.indirect(entries(offs2_t, a, b)))
-        for e in range(E):
-            weave = nc.gpsimd.tensor_copy if e < E // 2 else nc.scalar.copy
-            weave(
+        def weave(copy, e):
+            copy(
                 slot_words(e * C, (e + 1) * C).rearrange("p (n u) -> p n u", u=2),
                 rows[e // 2][:].rearrange("p (u n) -> p n u", u=2)[:, (e % 2) * C : (e % 2 + 1) * C, :],
             )
@@ -282,12 +281,18 @@ def tile_moe_uni_none_kernel(
         def quantise(a, b):
             nc.vector.quantize_mx(out=cq_w[:, a:b].bitcast(FP8X4), scales=cq_s[:, a:b], in_=slot_words(a, b).bitcast(BF16))
 
-        for e, k in enumerate((3, 4, 5, 0, 1)):
+        for e in (0, 1):
+            weave(nc.gpsimd.tensor_copy, e)
+        for e in (2, 3, 4):
+            weave(nc.scalar.copy, e)
+        for e, k in zip((0, 1, 5, 2), (3, 4, 5, 0)):
             quantise(e * C, (e + 1) * C)
+            if e == 0:
+                weave(nc.vector.tensor_copy, 5)
             product(cq_w, cq_s, 0, e * C, (e + 1) * C, z[0], named[k])
-        halves = [(S - C, S - C // 2), (S - C // 2, S)]
+        halves = [(3 * C, 4 * C), (4 * C, 4 * C + C // 2), (4 * C + C // 2, 5 * C)]
         banks = []
-        for (a, b), k in zip(halves, (2, 6)):
+        for (a, b), k in zip(halves, (1, 2, 6)):
             quantise(a, b)
             banks.append(multiply(cq_w, cq_s, 0, a, b, named[k]))
         for (a, b), bank in zip(halves, banks):

@@ -25,10 +25,9 @@ BLOCKS = T // P
 PER_COL = 16
 BANK = 512
 WIDE = 1024
-EARLY = (0, 2)
-LATE = (3, 1)
-FREE = 4 * C
-ROWS = 2048
+HALF = T // 2
+TERM_BUFS = 10
+FREE = 4
 FLOPS = 2 * 2 * K * K * S
 
 
@@ -88,18 +87,21 @@ def tile_moe_uni_none_kernel(
         make_identity(nc, ident_f[:])
         make_identity(nc, ident_b[:])
 
-        plane_s = [keep.tile([P, E * P], U8, name="plane_s%d" % t, align_bytes=64) for t in range(PLANES)]
+        first_s = keep.tile([P, E * P], U8, name="first_s", align_bytes=64)
+        other_s = keep.tile([P, PLANES - 1, E * P], U8, name="other_s", align_bytes=64)
+        plane_s = [first_s[:]] + [other_s[:, t, :] for t in range(PLANES - 1)]
         w_words16 = w_w[:].rearrange("p e n -> p (e n)").bitcast(U16).rearrange("p (m t) -> p t m", t=PLANES)
         w_scale_bytes = w_s[:].rearrange("p e n -> p (e n)").bitcast(U8).rearrange("p (m t) -> p t m", t=PLANES)
         plane_w = {}
-        for t in EARLY:
-            plane_w[t] = keep.tile([P, E * P * 2], U8, name="early_w%d" % t, align_bytes=64)[:]
-            nc.gpsimd.tensor_copy(plane_w[t].bitcast(U16), w_words16[:, t, :])
-        for t in EARLY + LATE:
-            nc.gpsimd.tensor_copy(plane_s[t][:], w_scale_bytes[:, t, :])
+        even_w = keep.tile([P, 2, E * P * 2], U8, name="even_w", align_bytes=64)
+        plane_w[0] = even_w[:, 0, :]
+        plane_w[2] = even_w[:, 1, :]
+        nc.gpsimd.tensor_copy(even_w[:].bitcast(U16), w_words16[:, 0:PLANES:2, :])
+        nc.gpsimd.tensor_copy(first_s[:], w_scale_bytes[:, 0, :])
+        nc.gpsimd.tensor_copy(other_s[:], w_scale_bytes[:, 1:, :])
 
-        def multiply(codes, scales, t, a, b, k):
-            bank = in_bank(k, [P, b - a])
+        def multiply(codes, scales, t, a, b, where):
+            bank = in_bank(where, [P, b - a])
             for lo in range(a, b, C):
                 e, hi = lo // C, min(lo + C, b)
                 nc.tensor.matmul_mx(
@@ -113,24 +115,23 @@ def tile_moe_uni_none_kernel(
                 )
             return bank
 
-        def product(codes, scales, t, a, b, dst, k):
-            nc.scalar.copy(dst[:, a:b], multiply(codes, scales, t, a, b, k)[:])
+        def product(codes, scales, t, a, b, dst, where):
+            nc.scalar.copy(dst[:, a:b], multiply(codes, scales, t, a, b, where)[:])
 
-        def whole_plane(codes, scales, t, dst, banks):
-            for a, k in zip(range(0, S, BANK), banks):
-                product(codes, scales, t, a, a + BANK, dst, k)
+        def banks_of_plane(codes, scales, t, dst, places):
+            for a, where in zip(range(0, S, BANK), places):
+                product(codes, scales, t, a, a + BANK, dst, where)
 
         def gated(window, pos, gate, r, dst, a=0, b=T):
             nc.vector.tensor_tensor(dst[:, a:b], window[:].indirect(entries(pos[r], a, b)), gate[:, r, a:b], MULT)
 
-        def add_turned(window, pos, gate, choices, k, offsets=()):
-            bank = in_bank(k, [P, BLOCKS, P])
+        def new_term(r):
+            return ring.tile([P, T], F32, name="term", bufs=TERM_BUFS)
+
+        def add_turned(window, pos, gate, choices, where, term_tile=new_term):
+            bank = in_bank(where, [P, BLOCKS, P])
             for r in range(choices):
-                if r >= choices - len(offsets):
-                    offset = offsets[r - choices + len(offsets)]
-                    term = lent.tile([P, T], F32, name="lent_term%d" % offset, offset=offset, align_bytes=64)
-                else:
-                    term = ring.tile([P, T], F32, name="term", bufs=10)
+                term = term_tile(r)
                 gated(window, pos, gate, r, term)
                 for j in range(BLOCKS):
                     nc.tensor.matmul(
@@ -143,25 +144,10 @@ def tile_moe_uni_none_kernel(
                     )
             return bank
 
-        def turn_back(bank, ident, blocks, offset=None):
-            if offset is None:
-                turned = ring.tile([P, BLOCKS, P], ident.dtype, name="turned", bufs=3)
-            else:
-                turned = lent.tile([P, BLOCKS, P], ident.dtype, name="lent_turned%d" % offset, offset=offset, align_bytes=64)
+        def turn_back(bank, turned, blocks):
             nc.scalar.copy(turned[:], bank[:])
             for j in range(BLOCKS):
-                nc.tensor.transpose(blocks[j], turned[:, j, :], ident[:])
-
-        def turn_back_whole(bank, ident, k):
-            back = in_bank(k, [P, T], ident.dtype)
-            turn_back(bank, ident, [back[:, j * P : (j + 1) * P] for j in range(BLOCKS)])
-            return back
-
-        def first_two_terms(window, pos, gate):
-            terms = [ring.tile([P, T], F32, name="early_term", bufs=4) for r in range(2)]
-            for r in range(2):
-                gated(window, pos, gate, r, terms[r])
-            return terms
+                nc.tensor.transpose(blocks[j], turned[:, j, :], ident_f[:])
 
         xg_w = keep.tile([P, S], U32, name="xg_w", align_bytes=64)
         xg_s = keep.tile([P, S], U8, name="xg_s", align_bytes=64)
@@ -169,18 +155,12 @@ def tile_moe_uni_none_kernel(
 
         for a in range(0, S, S // 2):
             nc.vector.tensor_copy(xg_w[:, a : a + S // 2], x_w[:].bitcast(U32).indirect(entries(offs_t, a, a + S // 2)))
-        half = T // 2
         c_single = [keep.tile([P, T], BF16, name="c_single%d" % t) for t in range(2)]
         c_pair_values = c_pair[:, :T].bitcast(BF16).rearrange("p (n u) -> p n u", u=2)
-        cg = keep.tile([P, S * 2], U32, name="cg", align_bytes=64)
-
-        def slot_words(a, b):
-            return cg[:, 2 * a : 2 * b]
-
-        rows = [keep.tile([P, 2 * BANK], U32, name="rows%d" % i, align_bytes=64) for i in range(FREE // BANK)]
+        rows = [keep.tile([P, 2 * BANK], U32, name="rows%d" % i, align_bytes=64) for i in range(FREE // 2)]
 
         def gather_single(t, e):
-            dst = rows[e // 2][:, (e % 2) * C : (e % 2 + 1) * C].bitcast(BF16).rearrange("p (n v) -> p n v", v=2)
+            dst = rows[e // 2][:, (e % 2) * C : (e % 2 + 1) * C].bitcast(BF16).rearrange("p (n u) -> p n u", u=2)
             nc.scalar.activation(dst[:, :, t], c_single[t][:].indirect(entries(offs2_t, e * C, (e + 1) * C)), COPY)
 
         with tc.psum_pool(name="ring_psum", bufs=6) as ring_psum:
@@ -188,22 +168,19 @@ def tile_moe_uni_none_kernel(
             for a, b in [(0, BANK), (BANK, 2 * BANK), (2 * BANK, S - C), (S - C, S)]:
                 nc.vector.tensor_copy(xg_s[:, a:b], x_s[:].bitcast(U8).indirect(entries(offs_t, a, b)))
                 product(xg_w, xg_s, 0, a, b, y[0], in_turn)
-                if a == 0:
-                    product(xg_w, xg_s, EARLY[1], a, b, y[EARLY[1]], in_turn)
-            for a in range(BANK, S, BANK):
-                product(xg_w, xg_s, EARLY[1], a, a + BANK, y[EARLY[1]], in_turn)
-            other_w = keep.tile([P, len(LATE), E * P * 2], U8, name="other_w", tag="after_tokens", align_bytes=64)
-            for i, t in enumerate(LATE):
-                plane_w[t] = other_w[:, i, :]
-                nc.vector.tensor_copy(plane_w[t].bitcast(U16), w_words16[:, t, :])
-            whole_plane(xg_w, xg_s, LATE[0], y[LATE[0]], [in_turn] * 3)
-            whole_plane(xg_w, xg_s, LATE[1], y[LATE[1]], [in_turn] * 2)
+            banks_of_plane(xg_w, xg_s, 2, y[2], [in_turn] * 3)
+            odd_w = keep.tile([P, 2, E * P * 2], U8, name="odd_w", tag="after_tokens", align_bytes=64)
+            plane_w[1] = odd_w[:, 0, :]
+            plane_w[3] = odd_w[:, 1, :]
+            nc.vector.tensor_copy(odd_w[:].bitcast(U16), w_words16[:, 1:PLANES:2, :])
+            banks_of_plane(xg_w, xg_s, 3, y[3], [in_turn] * 3)
+            banks_of_plane(xg_w, xg_s, 1, y[1], [in_turn] * 2)
 
-            def add_in_halves(t, sums):
-                banks = [in_bank(k, [P, 2, P]) for k in sums]
+            def add_in_halves(t, places, last_pieces):
+                banks = [in_bank(where, [P, 2, P]) for where in places]
                 for r in range(CHOICES):
-                    for a, b in [(0, half), (half, T)] if r == CHOICES - 1 and t == 1 else [(0, T)]:
-                        term = ring.tile([P, T], F32, name="term", bufs=10)
+                    for a, b in last_pieces if r == CHOICES - 1 else [(0, T)]:
+                        term = new_term(r)
                         gated(y[t], pos_a, gate_a, r, term, a, b)
                         for j in range(a // P, b // P):
                             nc.tensor.matmul(
@@ -219,106 +196,117 @@ def tile_moe_uni_none_kernel(
             def turn_halves_back(banks, places):
                 backs = []
                 for h in range(2):
-                    turned = ring.tile([P, 2, P], BF16, name="turned_half")
-                    nc.scalar.copy(turned[:], banks[h][:])
-                    backs.append(in_bank(places[h], [P, half], BF16))
+                    turned_half = ring.tile([P, 2, P], BF16, name="turned_half")
+                    nc.scalar.copy(turned_half[:], banks[h][:])
+                    backs.append(in_bank(places[h], [P, HALF], BF16))
                     for j in range(2):
-                        nc.tensor.transpose(backs[h][:, j * P : (j + 1) * P], turned[:, j, :], ident_b[:])
+                        nc.tensor.transpose(backs[h][:, j * P : (j + 1) * P], turned_half[:, j, :], ident_b[:])
                 return backs
 
             def keep_halves(t, backs):
                 for h in range(2):
-                    nc.scalar.copy(c_single[t][:, h * half : (h + 1) * half], backs[h][:])
+                    nc.scalar.copy(c_single[t][:, h * HALF : (h + 1) * HALF], backs[h][:])
 
-            backs = turn_halves_back(add_in_halves(0, [in_turn] * 2), own)
-            product(xg_w, xg_s, LATE[1], S - BANK, S, y[LATE[1]], in_turn)
+            backs = turn_halves_back(add_in_halves(0, [in_turn] * 2, [(0, T)]), own)
+            product(xg_w, xg_s, 1, S - BANK, S, y[1], in_turn)
             keep_halves(0, backs)
-            partial_c = [in_bank(in_turn, [P, 2, half]) for h in range(2)]
-            for e in range(FREE // C):
+            partial_c = [in_bank(in_turn, [P, 2, HALF]) for h in range(2)]
+            for e in range(FREE):
                 gather_single(0, e)
-            sums = [add_turned(y[2], pos_a, gate_a, 2, own[0], (5 * ROWS, 6 * ROWS)), add_turned(y[3], pos_a, gate_a, 2, own[1])]
-            for u, offset in enumerate((0, 7 * ROWS)):
-                blocks = [partial_c[j // 2][:, u, (j % 2) * P : (j % 2 + 1) * P] for j in range(BLOCKS)]
-                turn_back(sums[u], ident_f, blocks, offset)
-            rows.append(lent.tile([P, 2 * BANK], U32, name="rows_last", offset=0, align_bytes=64))
-            for e in range(FREE // C, E):
+            two_terms = lent.tile([P, 2 * T], F32, name="two_terms")
+            sums = [
+                add_turned(y[2], pos_a, gate_a, 2, own[0], lambda r: two_terms[:, r * T : (r + 1) * T]),
+                add_turned(y[3], pos_a, gate_a, 2, own[1]),
+            ]
+            for u, pool in enumerate((lent, keep)):
+                turned_partial = pool.tile([P, BLOCKS, P], F32, name="turned_partial", align_bytes=64)
+                turn_back(sums[u], turned_partial, [partial_c[j // 2][:, u, (j % 2) * P : (j % 2 + 1) * P] for j in range(BLOCKS)])
+            rows.append(lent.tile([P, 2 * BANK], U32, name="rows_last", tag="turned_partial", align_bytes=64))
+            for e in range(FREE, E):
                 gather_single(0, e)
 
-            keep_halves(1, turn_halves_back(add_in_halves(1, own), [in_turn] * 2))
+            keep_halves(1, turn_halves_back(add_in_halves(1, own, [(0, HALF), (HALF, T)]), [in_turn] * 2))
             for e in range(E):
                 gather_single(1, e)
 
-            thirds = lent.tile([P, 2 * T], F32, name="thirds", offset=5 * ROWS, align_bytes=64)
+            thirds = lent.tile([P, 2 * T], F32, name="thirds", tag="two_terms")
             gated(y[2], pos_a, gate_a, 2, thirds[:, :T])
-            for h in range(2):
-                gated(y[3], pos_a, gate_a, 2, thirds[:, T:], h * half, (h + 1) * half)
-            for h in range(2):
-                a = h * half
+            for a in (0, HALF):
+                gated(y[3], pos_a, gate_a, 2, thirds[:, T:], a, a + HALF)
+            for h, a in enumerate((0, HALF)):
                 nc.vector.tensor_tensor(
-                    c_pair_values[:, a : a + half, :],
+                    c_pair_values[:, a : a + HALF, :],
                     partial_c[h][:].rearrange("p u n -> p n u"),
-                    thirds[:].rearrange("p (u n) -> p n u", u=2)[:, a : a + half, :],
+                    thirds[:].rearrange("p (u n) -> p n u", u=2)[:, a : a + HALF, :],
                     ADD,
                 )
 
         named_psum = ctx.enter_context(tc.psum_pool(name="named_psum", bufs=1))
-        named = [(named_psum, "named%d" % k) for k in range(6)] + own
+        named = [(named_psum, "named%d" % i) for i in range(6)] + own
 
+        woven = keep.tile([P, S * 2], U32, name="woven", align_bytes=64)
         cq_w = keep.tile([P, S], U32, name="cq_w", align_bytes=64)
         cq_s = keep.tile([P, S], U8, name="cq_s", align_bytes=64)
         z = [keep.tile([P, S], F32, name="z%d" % t) for t in range(PLANES)]
-        c_pair_words = c_pair[:].bitcast(U32)
 
         for a, b in [(0, C), (C, BANK), (BANK, 2 * BANK), (2 * BANK, S - C), (S - C, S)]:
             lo = BANK + a % BANK
-            nc.vector.tensor_copy(rows[a // BANK][:, lo : lo + b - a], c_pair_words.indirect(entries(offs2_t, a, b)))
+            nc.vector.tensor_copy(rows[a // BANK][:, lo : lo + b - a], c_pair[:].bitcast(U32).indirect(entries(offs2_t, a, b)))
+
         def weave(copy, e):
             copy(
-                slot_words(e * C, (e + 1) * C).rearrange("p (n u) -> p n u", u=2),
+                woven[:, 2 * e * C : 2 * (e + 1) * C].rearrange("p (n u) -> p n u", u=2),
                 rows[e // 2][:].rearrange("p (u n) -> p n u", u=2)[:, (e % 2) * C : (e % 2 + 1) * C, :],
             )
 
         def quantise(a, b):
-            nc.vector.quantize_mx(out=cq_w[:, a:b].bitcast(FP8X4), scales=cq_s[:, a:b], in_=slot_words(a, b).bitcast(BF16))
+            nc.vector.quantize_mx(out=cq_w[:, a:b].bitcast(FP8X4), scales=cq_s[:, a:b], in_=woven[:, 2 * a : 2 * b].bitcast(BF16))
 
-        for e in (0, 1):
+        on_gpsimd, on_scalar, on_vector = (0, 1), (2, 3, 4), 5
+        for e in on_gpsimd:
             weave(nc.gpsimd.tensor_copy, e)
-        for e in (2, 3, 4):
+        for e in on_scalar:
             weave(nc.scalar.copy, e)
-        for e, k in zip((0, 1, 5, 2), (3, 4, 5, 0)):
+        for e, where in zip((0, 1, on_vector, 2), (named[3], named[4], named[5], named[0])):
             quantise(e * C, (e + 1) * C)
             if e == 0:
-                weave(nc.vector.tensor_copy, 5)
-            product(cq_w, cq_s, 0, e * C, (e + 1) * C, z[0], named[k])
-        halves = [(3 * C, 4 * C), (4 * C, 4 * C + C // 2), (4 * C + C // 2, 5 * C)]
-        banks = []
-        for (a, b), k in zip(halves, (1, 2, 6)):
+                weave(nc.vector.tensor_copy, on_vector)
+            product(cq_w, cq_s, 0, e * C, (e + 1) * C, z[0], where)
+        late = [named[1], named[2], named[6]]
+        ends = [(3 * C, 4 * C), (4 * C, 4 * C + C // 2), (4 * C + C // 2, 5 * C)]
+        last_banks = []
+        for (a, b), where in zip(ends, late):
             quantise(a, b)
-            banks.append(multiply(cq_w, cq_s, 0, a, b, named[k]))
-        for (a, b), bank in zip(halves, banks):
+            last_banks.append(multiply(cq_w, cq_s, 0, a, b, where))
+        for (a, b), bank in zip(ends, last_banks):
             nc.vector.tensor_copy(z[0][:, a:b], bank[:])
         for t in range(1, PLANES):
-            whole_plane(cq_w, cq_s, t, z[t], [named[k] for k in (1, 2, 6)])
+            banks_of_plane(cq_w, cq_s, t, z[t], late)
 
         out_planes = out.rearrange("(p t) n -> p t n", t=PLANES)
         res = keep.tile([P, PLANES, T], F32, name="res")
         last = PLANES - 1
-        for t, k in enumerate((1, 2, 6)):
-            nc.scalar.copy(res[:, t, :], turn_back_whole(add_turned(z[t], pos_b, gate_b, CHOICES, named[k]), ident_f, named[3 + t])[:])
+        for t in range(last):
+            bank = add_turned(z[t], pos_b, gate_b, CHOICES, late[t])
+            back = in_bank(named[3 + t], [P, T])
+            turned = ring.tile([P, BLOCKS, P], F32, name="turned", bufs=last)
+            turn_back(bank, turned, [back[:, j * P : (j + 1) * P] for j in range(BLOCKS)])
+            nc.scalar.copy(res[:, t, :], back[:])
             nc.scalar.dma_start(out_planes[:, t, :], res[:, t, :])
 
-        terms = first_two_terms(z[last], pos_b, gate_b)
+        terms = [keep.tile([P, T], F32, name="last_term%d" % r) for r in range(CHOICES)]
         partial_out = keep.tile([P, T], F32, name="partial_out")
-        third_out = keep.tile([P, T], F32, name="third_out")
-        pieces = [(0, half), (half, 3 * T // 4), (3 * T // 4, T)]
+        pieces = [(0, HALF), (HALF, 3 * T // 4), (3 * T // 4, T)]
 
         def finish(a, b):
-            nc.vector.tensor_tensor(res[:, last, a:b], partial_out[:, a:b], third_out[:, a:b], ADD)
+            nc.vector.tensor_tensor(res[:, last, a:b], partial_out[:, a:b], terms[2][:, a:b], ADD)
             nc.sync.dma_start(out_planes[:, last, a:b], res[:, last, a:b])
 
-        gated(z[last], pos_b, gate_b, 2, third_out, *pieces[0])
+        for r in range(2):
+            gated(z[last], pos_b, gate_b, r, terms[r])
+        gated(z[last], pos_b, gate_b, 2, terms[2], *pieces[0])
         nc.vector.tensor_tensor(partial_out[:], terms[0][:], terms[1][:], ADD)
         for done, following in zip(pieces, pieces[1:]):
-            gated(z[last], pos_b, gate_b, 2, third_out, *following)
+            gated(z[last], pos_b, gate_b, 2, terms[2], *following)
             finish(*done)
         finish(*pieces[-1])

@@ -165,7 +165,7 @@ def tile_moe_uni_none_kernel(
 
         with tc.psum_pool(name="ring_psum", bufs=6) as ring_psum:
             in_turn = (ring_psum, "in_turn")
-            for a, b in [(0, BANK), (BANK, 2 * BANK), (2 * BANK, S - C), (S - C, S)]:
+            for a, b in [(0, C), (C, 3 * C), (3 * C, 4 * C), (4 * C, S - C), (S - C, S - P), (S - P, S)]:
                 nc.vector.tensor_copy(xg_s[:, a:b], x_s[:].bitcast(U8).indirect(entries(offs_t, a, b)))
                 product(xg_w, xg_s, 0, a, b, y[0], in_turn)
             banks_of_plane(xg_w, xg_s, 2, y[2], [in_turn] * 3)
@@ -262,18 +262,16 @@ def tile_moe_uni_none_kernel(
         def quantise(a, b):
             nc.vector.quantize_mx(out=cq_w[:, a:b].bitcast(FP8X4), scales=cq_s[:, a:b], in_=woven[:, 2 * a : 2 * b].bitcast(BF16))
 
-        on_gpsimd, on_scalar, on_vector = (0, 1), (2, 3, 4), 5
+        on_gpsimd, on_scalar = (0, 1), (2, 3, 4, 5)
         for e in on_gpsimd:
             weave(nc.gpsimd.tensor_copy, e)
         for e in on_scalar:
             weave(nc.scalar.copy, e)
-        for e, where in zip((0, 1, on_vector, 2), (named[3], named[4], named[5], named[0])):
+        for e, where in enumerate((named[3], named[4], named[5], named[0])):
             quantise(e * C, (e + 1) * C)
-            if e == 0:
-                weave(nc.vector.tensor_copy, on_vector)
             product(cq_w, cq_s, 0, e * C, (e + 1) * C, z[0], where)
         late = [named[1], named[2], named[6]]
-        ends = [(3 * C, 4 * C), (4 * C, 4 * C + C // 2), (4 * C + C // 2, 5 * C)]
+        ends = [(4 * C, 5 * C), (5 * C, S - P), (S - P, S)]
         last_banks = []
         for (a, b), where in zip(ends, late):
             quantise(a, b)

@@ -82,6 +82,11 @@ def tile_moe_uni_none_kernel(
         gate_b = keep.tile([P, CHOICES, T], F32, name="gate_b")
         nc.sync.dma_start(gate_b[:], gate2.rearrange("r p n -> p r n"))
 
+        gate_cols = [keep.tile([P, BLOCKS], F32, name="gate_cols%d" % r) for r in range(2)]
+        with nc.allow_non_contiguous_dma(reason="one gate value a partition"):
+            for r in range(2):
+                nc.sync.dma_start(gate_cols[r][:], gate2[r, 0, :].rearrange("(j p) -> p j", p=P))
+
         ident_f = keep.tile([P, P], F32, name="ident_f")
         ident_b = keep.tile([P, P], BF16, name="ident_b")
         make_identity(nc, ident_f[:])
@@ -245,7 +250,7 @@ def tile_moe_uni_none_kernel(
         named = [(named_psum, "named%d" % i) for i in range(6)] + own
 
         woven = keep.tile([P, S * 2], U32, name="woven", align_bytes=64)
-        cq_w = keep.tile([P, S], U32, name="cq_w", align_bytes=64)
+        cq_w = keep.tile([P, S], U32, name="cq_w", tag="cq_w", align_bytes=64)
         cq_s = keep.tile([P, S], U8, name="cq_s", align_bytes=64)
         z = [keep.tile([P, S], F32, name="z%d" % t) for t in range(PLANES)]
 
@@ -284,27 +289,67 @@ def tile_moe_uni_none_kernel(
         out_planes = out.rearrange("(p t) n -> p t n", t=PLANES)
         res = keep.tile([P, PLANES, T], F32, name="res")
         last = PLANES - 1
-        for t in range(last):
-            bank = add_turned(z[t], pos_b, gate_b, CHOICES, late[t])
-            back = in_bank(named[3 + t], [P, T])
-            turned = ring.tile([P, BLOCKS, P], F32, name="turned", bufs=last)
-            turn_back(bank, turned, [back[:, j * P : (j + 1) * P] for j in range(BLOCKS)])
-            nc.scalar.copy(res[:, t, :], back[:])
-            nc.scalar.dma_start(out_planes[:, t, :], res[:, t, :])
 
-        terms = [keep.tile([P, T], F32, name="last_term%d" % r) for r in range(CHOICES)]
-        partial_out = keep.tile([P, T], F32, name="partial_out")
+        def blocks_of(bank):
+            return [bank[:, j * P : (j + 1) * P] for j in range(BLOCKS)]
+
+        def raw_term(r, where):
+            raw = keep.tile([P, T], F32, name="raw%d" % r, tag="raw%d" % r, align_bytes=64)
+            nc.scalar.activation(raw[:], z[last][:].indirect(pos_b[r][:]), COPY)
+            bank = in_bank(where, [P, BLOCKS, P])
+            for j in range(BLOCKS):
+                nc.tensor.transpose(bank[:, j, :], raw[:, j * P : (j + 1) * P], ident_f[:])
+            return bank
+
+        def scale_back(r, bank, partial):
+            scaled = keep.tile([P, BLOCKS, P], F32, name="scaled%d" % r)
+            for j in range(BLOCKS):
+                nc.scalar.activation(scaled[:, j, :], bank[:, j, :], COPY, scale=gate_cols[r][:, j : j + 1])
+            for j in range(BLOCKS):
+                nc.tensor.matmul(
+                    partial[:, j * P : (j + 1) * P],
+                    lhsT=scaled[:, j, :],
+                    rhs=ident_f[:],
+                    is_transpose=True,
+                    start=(r == 0 and j == 0),
+                    stop=(r == 1 and j == BLOCKS - 1),
+                )
+
+        def turned_tile(t):
+            return keep.tile([P, BLOCKS, P], F32, name="turned%d" % t, tag="turned%d" % t)
+
+        def term_on(tags):
+            return lambda r: keep.tile([P, T], F32, name="term_" + tags[r], tag=tags[r], align_bytes=64)
+
+        backs = [in_bank(named[3 + t], [P, T]) for t in range(last)]
+        sum0 = add_turned(z[0], pos_b, gate_b, CHOICES, late[0])
+        sum1 = add_turned(z[1], pos_b, gate_b, 2, late[1], term_on(["first", "cq_w"]))
+        raw_banks = [raw_term(0, named[0]), raw_term(1, named[7])]
+        turn_back(sum0, turned_tile(0), blocks_of(backs[0]))
+        turn_back(sum1, turned_tile(1), blocks_of(backs[1]))
+        nc.scalar.copy(res[:, 0, :], backs[0][:])
+        nc.sync.dma_start(out_planes[:, 0, :], res[:, 0, :])
+        sum2 = add_turned(z[2], pos_b, gate_b, CHOICES, late[2], term_on(["first", "raw0", "raw1"]))
+        partial_last = in_bank(late[0], [P, T])
+        scale_back(0, raw_banks[0], partial_last)
+        scale_back(1, raw_banks[1], partial_last)
+        turn_back(sum2, turned_tile(2), blocks_of(backs[2]))
+        for a in (0, HALF):
+            nc.scalar.copy(res[:, 2, a : a + HALF], backs[2][:, a : a + HALF])
+            nc.scalar.dma_start(out_planes[:, 2, a : a + HALF], res[:, 2, a : a + HALF])
+
+        both_thirds = keep.tile([P, 2 * T], F32, name="both_thirds", tag="turned0")
+        thirds_out = [both_thirds[:, :T], both_thirds[:, T:]]
+
+        def finish(t, partial, third, a, b):
+            nc.vector.tensor_tensor(res[:, t, a:b], partial[:, a:b], third[:, a:b], ADD)
+            nc.sync.dma_start(out_planes[:, t, a:b], res[:, t, a:b])
+
         pieces = [(0, HALF), (HALF, 3 * T // 4), (3 * T // 4, T)]
-
-        def finish(a, b):
-            nc.vector.tensor_tensor(res[:, last, a:b], partial_out[:, a:b], terms[2][:, a:b], ADD)
-            nc.sync.dma_start(out_planes[:, last, a:b], res[:, last, a:b])
-
-        for r in range(2):
-            gated(z[last], pos_b, gate_b, r, terms[r])
-        gated(z[last], pos_b, gate_b, 2, terms[2], *pieces[0])
-        nc.vector.tensor_tensor(partial_out[:], terms[0][:], terms[1][:], ADD)
+        gated(z[1], pos_b, gate_b, 2, thirds_out[0])
+        gated(z[last], pos_b, gate_b, 2, thirds_out[1], *pieces[0])
+        finish(1, backs[1], thirds_out[0], 0, T)
         for done, following in zip(pieces, pieces[1:]):
-            gated(z[last], pos_b, gate_b, 2, terms[2], *following)
-            finish(*done)
-        finish(*pieces[-1])
+            gated(z[last], pos_b, gate_b, 2, thirds_out[1], *following)
+            finish(last, partial_last, thirds_out[1], *done)
+        finish(last, partial_last, thirds_out[1], *pieces[-1])

@@ -27,7 +27,6 @@ BANK = 512
 WIDE = 1024
 HALF = T // 2
 TERM_BUFS = 10
-FREE = 4
 FLOPS = 2 * 2 * K * K * S
 
 
@@ -55,13 +54,14 @@ def tile_moe_uni_none_kernel(
             return lst[:, a // PER_COL : b // PER_COL]
 
         x_w = keep.tile([P, WIDE], I32, name="x_w", align_bytes=64)
-        x_s = keep.tile([P, WIDE // 4], I32, name="x_s", tag="after_tokens", align_bytes=64)
+        x_s = keep.tile([P, WIDE // 4], I32, name="x_s", align_bytes=64)
         w_w = keep.tile([P, E, K // 2], I32, name="w_w", align_bytes=64)
         w_s = keep.tile([P, E, K // 4], I32, name="w_s", align_bytes=64)
         nc.vector.memset(x_s[:], 0)
         nc.vector.memset(x_w[:, T:], 0)
-        c_pair = keep.tile([P, WIDE], I32, name="c_pair", align_bytes=64)
-        nc.vector.memset(c_pair[:, T:], 0)
+        c_pair = [keep.tile([P, WIDE], I32, name="c_pair%d" % u, align_bytes=64) for u in range(2)]
+        for u in range(2):
+            nc.vector.memset(c_pair[u][:, T:], 0)
         nc.gpsimd.memset(w_s[:], 0)
 
         offs_t = load_list(offs, "offs_t")
@@ -82,28 +82,32 @@ def tile_moe_uni_none_kernel(
         gate_b = keep.tile([P, CHOICES, T], F32, name="gate_b")
         nc.sync.dma_start(gate_b[:], gate2.rearrange("r p n -> p r n"))
 
-        gate_cols = [keep.tile([P, BLOCKS], F32, name="gate_cols%d" % r) for r in range(2)]
+        gate_cols = [[keep.tile([P, BLOCKS], F32, name="gate_cols%d%d" % (i, r)) for r in range(2)] for i in range(2)]
         with nc.allow_non_contiguous_dma(reason="one gate value a partition"):
-            for r in range(2):
-                nc.sync.dma_start(gate_cols[r][:], gate2[r, 0, :].rearrange("(j p) -> p j", p=P))
+            for i, gate in enumerate((gate1, gate2)):
+                for r in range(2):
+                    nc.sync.dma_start(gate_cols[i][r][:], gate[r, 0, :].rearrange("(j p) -> p j", p=P))
 
         ident_f = keep.tile([P, P], F32, name="ident_f")
-        ident_b = keep.tile([P, P], BF16, name="ident_b")
         make_identity(nc, ident_f[:])
-        make_identity(nc, ident_b[:])
 
-        first_s = keep.tile([P, E * P], U8, name="first_s", align_bytes=64)
-        other_s = keep.tile([P, PLANES - 1, E * P], U8, name="other_s", align_bytes=64)
-        plane_s = [first_s[:]] + [other_s[:, t, :] for t in range(PLANES - 1)]
+        early_s = [keep.tile([P, E * P], U8, name="early_s%d" % u, align_bytes=64) for u in range(2)]
+        odd_s = keep.tile([P, 2, E * P], U8, name="odd_s", align_bytes=64)
+        plane_s = [early_s[0][:], odd_s[:, 0, :], early_s[1][:], odd_s[:, 1, :]]
         w_words16 = w_w[:].rearrange("p e n -> p (e n)").bitcast(U16).rearrange("p (m t) -> p t m", t=PLANES)
         w_scale_bytes = w_s[:].rearrange("p e n -> p (e n)").bitcast(U8).rearrange("p (m t) -> p t m", t=PLANES)
         plane_w = {}
         even_w = keep.tile([P, 2, E * P * 2], U8, name="even_w", align_bytes=64)
         plane_w[0] = even_w[:, 0, :]
         plane_w[2] = even_w[:, 1, :]
-        nc.gpsimd.tensor_copy(even_w[:].bitcast(U16), w_words16[:, 0:PLANES:2, :])
-        nc.gpsimd.tensor_copy(first_s[:], w_scale_bytes[:, 0, :])
-        nc.gpsimd.tensor_copy(other_s[:], w_scale_bytes[:, 1:, :])
+        nc.scalar.copy(even_w[:].bitcast(U16), w_words16[:, 0:PLANES:2, :])
+        odd_w = keep.tile([P, 2, E * P * 2], U8, name="odd_w", align_bytes=64)
+        plane_w[1] = odd_w[:, 0, :]
+        plane_w[3] = odd_w[:, 1, :]
+        nc.scalar.copy(odd_w[:].bitcast(U16), w_words16[:, 1:PLANES:2, :])
+        for u in range(2):
+            nc.gpsimd.tensor_copy(early_s[u][:], w_scale_bytes[:, 2 * u, :])
+        nc.gpsimd.tensor_copy(odd_s[:], w_scale_bytes[:, 1:PLANES:2, :])
 
         def multiply(codes, scales, t, a, b, where):
             bank = in_bank(where, [P, b - a])
@@ -155,89 +159,100 @@ def tile_moe_uni_none_kernel(
                 nc.tensor.transpose(blocks[j], turned[:, j, :], ident_f[:])
 
         xg_w = keep.tile([P, S], U32, name="xg_w", align_bytes=64)
-        xg_s = keep.tile([P, S], U8, name="xg_s", align_bytes=64)
+        xg_s = keep.tile([P, S], U8, name="xg_s", tag="xg_s", align_bytes=64)
         y = [keep.tile([P, S], F32, name="y%d" % t) for t in range(PLANES)]
 
         for a in range(0, S, S // 2):
             nc.vector.tensor_copy(xg_w[:, a : a + S // 2], x_w[:].bitcast(U32).indirect(entries(offs_t, a, a + S // 2)))
-        c_single = [keep.tile([P, T], BF16, name="c_single%d" % t) for t in range(2)]
-        c_pair_values = c_pair[:, :T].bitcast(BF16).rearrange("p (n u) -> p n u", u=2)
-        rows = [keep.tile([P, 2 * BANK], U32, name="rows%d" % i, align_bytes=64) for i in range(FREE // 2)]
+        rows = [keep.tile([P, 2 * BANK], U32, name="rows%d" % i, align_bytes=64) for i in range(E // 2)]
 
-        def gather_single(t, e):
-            dst = rows[e // 2][:, (e % 2) * C : (e % 2 + 1) * C].bitcast(BF16).rearrange("p (n u) -> p n u", u=2)
-            nc.scalar.activation(dst[:, :, t], c_single[t][:].indirect(entries(offs2_t, e * C, (e + 1) * C)), COPY)
+        def gather_pairs(u, a, b):
+            lo = u * BANK + a % BANK
+            nc.vector.tensor_copy(rows[a // BANK][:, lo : lo + b - a], c_pair[u][:].bitcast(U32).indirect(entries(offs2_t, a, b)))
+
+        def turn(dst, src, start, stop):
+            nc.tensor.matmul(dst, lhsT=src, rhs=ident_f[:], is_transpose=True, start=start, stop=stop)
 
         with tc.psum_pool(name="ring_psum", bufs=6) as ring_psum:
             in_turn = (ring_psum, "in_turn")
+            closing_banks = []
             for a, b in [(0, C), (C, 3 * C), (3 * C, 4 * C), (4 * C, S - C), (S - C, S - P), (S - P, S)]:
                 nc.vector.tensor_copy(xg_s[:, a:b], x_s[:].bitcast(U8).indirect(entries(offs_t, a, b)))
-                product(xg_w, xg_s, 0, a, b, y[0], in_turn)
-            banks_of_plane(xg_w, xg_s, 2, y[2], [in_turn] * 3)
-            odd_w = keep.tile([P, 2, E * P * 2], U8, name="odd_w", tag="after_tokens", align_bytes=64)
-            plane_w[1] = odd_w[:, 0, :]
-            plane_w[3] = odd_w[:, 1, :]
-            nc.vector.tensor_copy(odd_w[:].bitcast(U16), w_words16[:, 1:PLANES:2, :])
-            banks_of_plane(xg_w, xg_s, 3, y[3], [in_turn] * 3)
-            banks_of_plane(xg_w, xg_s, 1, y[1], [in_turn] * 2)
+                if b <= 4 * C:
+                    for t in (0, 2) if b <= 3 * C else (0,):
+                        product(xg_w, xg_s, t, a, b, y[t], in_turn)
+                else:
+                    closing_banks.append((a, b, multiply(xg_w, xg_s, 0, a, b, in_turn)))
+                if b == 4 * C:
+                    product(xg_w, xg_s, 1, 0, BANK, y[1], in_turn)
+            for a, b, bank in closing_banks:
+                nc.vector.tensor_copy(y[0][:, a:b], bank[:])
+            for a, b in [(3 * C, 4 * C), (4 * C, S)]:
+                product(xg_w, xg_s, 2, a, b, y[2], in_turn)
+            raws = {}
 
-            def add_in_halves(t, places, last_pieces):
-                banks = [in_bank(where, [P, 2, P]) for where in places]
+            def gather_raw(r, u, tag):
+                raws[r, u] = keep.tile([P, T], F32, name="raw_c%d%d" % (r, u), tag=tag, align_bytes=64)
+                nc.scalar.activation(raws[r, u][:], y[2 + u][:].indirect(pos_a[r][:]), COPY)
+
+            gather_raw(0, 0, "raw_c00")
+            for a, where in zip((BANK, 2 * BANK), own):
+                product(xg_w, xg_s, 1, a, a + BANK, y[1], where)
+            banks_of_plane(xg_w, xg_s, 3, y[3], [in_turn] * 3)
+
+            sums = [in_bank(where, [P, 2, 2, P]) for where in own]
+            first_term = lent.tile([P, T], F32, name="first_term", tag="first_term")
+            for t in range(2):
                 for r in range(CHOICES):
-                    for a, b in last_pieces if r == CHOICES - 1 else [(0, T)]:
-                        term = new_term(r)
+                    closing = t == 1 and r == CHOICES - 1
+                    for a, b in [(0, HALF), (HALF, T)] if closing else [(0, T)]:
+                        term = first_term if (t, r) == (1, 0) else new_term(r)
                         gated(y[t], pos_a, gate_a, r, term, a, b)
                         for j in range(a // P, b // P):
-                            nc.tensor.matmul(
-                                banks[j // 2][:, j % 2, :],
-                                lhsT=term[:, j * P : (j + 1) * P],
-                                rhs=ident_f[:],
-                                is_transpose=True,
-                                start=(r == 0 and j % 2 == 0),
-                                stop=(r == CHOICES - 1 and j % 2 == 1),
-                            )
-                return banks
+                            turn(sums[j // 2][:, j % 2, t, :], term[:, j * P : (j + 1) * P], (t, r, j % 2) == (0, 0, 0), closing and j % 2 == 1)
 
-            def turn_halves_back(banks, places):
-                backs = []
-                for h in range(2):
-                    turned_half = ring.tile([P, 2, P], BF16, name="turned_half")
-                    nc.scalar.copy(turned_half[:], banks[h][:])
-                    backs.append(in_bank(places[h], [P, HALF], BF16))
-                    for j in range(2):
-                        nc.tensor.transpose(backs[h][:, j * P : (j + 1) * P], turned_half[:, j, :], ident_b[:])
-                return backs
+            def turn_raw(r, u, banks):
+                for j in range(BLOCKS):
+                    nc.tensor.transpose(banks[j // 2][:, j % 2, u, :], raws[r, u][:, j * P : (j + 1) * P], ident_f[:])
 
-            def keep_halves(t, backs):
-                for h in range(2):
-                    nc.scalar.copy(c_single[t][:, h * HALF : (h + 1) * HALF], backs[h][:])
-
-            backs = turn_halves_back(add_in_halves(0, [in_turn] * 2, [(0, T)]), own)
-            product(xg_w, xg_s, 1, S - BANK, S, y[1], in_turn)
-            keep_halves(0, backs)
+            gather_raw(0, 1, "raw_c01")
+            gather_raw(1, 0, "xg_s")
+            raw_turned = [[in_bank(in_turn, [P, 2, 2, P]) for h in range(2)]]
+            for u in range(2):
+                turn_raw(0, u, raw_turned[0])
+            backs = []
+            for h in range(2):
+                turned_pairs = keep.tile([P, 2, P, 2], BF16, name="turned_pairs", tag=("turned_pairs", "raw_c11")[h], align_bytes=64)
+                nc.scalar.copy(turned_pairs[:], sums[h][:].rearrange("p j u m -> p j m u"))
+                backs.append(in_bank(in_turn, [P, HALF]))
+                words = turned_pairs[:].rearrange("p j m u -> p (j m u)").bitcast(F32)
+                for j in range(2):
+                    nc.tensor.transpose(backs[h][:, j * P : (j + 1) * P], words[:, j * P : (j + 1) * P], ident_f[:])
+            for h in range(2):
+                nc.scalar.copy(c_pair[0][:, h * HALF : (h + 1) * HALF].bitcast(F32), backs[h][:])
+            gather_raw(1, 1, "raw_c11")
+            raw_turned.append([in_bank(where, [P, 2, 2, P]) for where in own])
+            for u in range(2):
+                turn_raw(1, u, raw_turned[1])
             partial_c = [in_bank(in_turn, [P, 2, HALF]) for h in range(2)]
-            for e in range(FREE):
-                gather_single(0, e)
-            two_terms = lent.tile([P, 2 * T], F32, name="two_terms")
-            sums = [
-                add_turned(y[2], pos_a, gate_a, 2, own[0], lambda r: two_terms[:, r * T : (r + 1) * T]),
-                add_turned(y[3], pos_a, gate_a, 2, own[1]),
-            ]
-            for u, pool in enumerate((lent, keep)):
-                turned_partial = pool.tile([P, BLOCKS, P], F32, name="turned_partial", align_bytes=64)
-                turn_back(sums[u], turned_partial, [partial_c[j // 2][:, u, (j % 2) * P : (j % 2 + 1) * P] for j in range(BLOCKS)])
-            rows.append(lent.tile([P, 2 * BANK], U32, name="rows_last", tag="turned_partial", align_bytes=64))
-            for e in range(FREE, E):
-                gather_single(0, e)
+            for r in range(2):
+                scaled_c = keep.tile([P, BLOCKS, 2, P], F32, name="scaled_c%d" % r)
+                for j in range(BLOCKS):
+                    nc.scalar.activation(scaled_c[:, j, :, :], raw_turned[r][j // 2][:, j % 2, :, :], COPY, scale=gate_cols[0][r][:, j : j + 1])
+                    for u in range(2):
+                        turn(
+                            partial_c[j // 2][:, u, (j % 2) * P : (j % 2 + 1) * P],
+                            scaled_c[:, j, u, :],
+                            (r, j % 2, u) == (0, 0, 0),
+                            (r, j % 2, u) == (1, 1, 1),
+                        )
 
-            keep_halves(1, turn_halves_back(add_in_halves(1, own, [(0, HALF), (HALF, T)]), [in_turn] * 2))
-            for e in range(E):
-                gather_single(1, e)
-
-            thirds = lent.tile([P, 2 * T], F32, name="thirds", tag="two_terms")
-            gated(y[2], pos_a, gate_a, 2, thirds[:, :T])
-            for a in (0, HALF):
-                gated(y[3], pos_a, gate_a, 2, thirds[:, T:], a, a + HALF)
+            thirds = lent.tile([P, 2 * T], F32, name="thirds", tag="first_term")
+            for u in range(2):
+                gated(y[2 + u], pos_a, gate_a, 2, thirds[:, u * T : (u + 1) * T])
+            for a in range(0, S, BANK):
+                gather_pairs(0, a, a + BANK)
+            c_pair_values = c_pair[1][:, :T].bitcast(BF16).rearrange("p (n u) -> p n u", u=2)
             for h, a in enumerate((0, HALF)):
                 nc.vector.tensor_tensor(
                     c_pair_values[:, a : a + HALF, :],
@@ -255,8 +270,7 @@ def tile_moe_uni_none_kernel(
         z = [keep.tile([P, S], F32, name="z%d" % t) for t in range(PLANES)]
 
         for a, b in [(0, C), (C, BANK), (BANK, 2 * BANK), (2 * BANK, S - C), (S - C, S)]:
-            lo = BANK + a % BANK
-            nc.vector.tensor_copy(rows[a // BANK][:, lo : lo + b - a], c_pair[:].bitcast(U32).indirect(entries(offs2_t, a, b)))
+            gather_pairs(1, a, b)
 
         def weave(copy, e):
             copy(
@@ -304,7 +318,7 @@ def tile_moe_uni_none_kernel(
         def scale_back(r, bank, partial):
             scaled = keep.tile([P, BLOCKS, P], F32, name="scaled%d" % r)
             for j in range(BLOCKS):
-                nc.scalar.activation(scaled[:, j, :], bank[:, j, :], COPY, scale=gate_cols[r][:, j : j + 1])
+                nc.scalar.activation(scaled[:, j, :], bank[:, j, :], COPY, scale=gate_cols[1][r][:, j : j + 1])
             for j in range(BLOCKS):
                 nc.tensor.matmul(
                     partial[:, j * P : (j + 1) * P],

@@ -101,13 +101,13 @@ def tile_moe_uni_none_kernel(
         plane_w[0] = even_w[:, 0, :]
         plane_w[2] = even_w[:, 1, :]
         nc.scalar.copy(even_w[:].bitcast(U16), w_words16[:, 0:PLANES:2, :])
-        odd_w = keep.tile([P, 2, E * P * 2], U8, name="odd_w", align_bytes=64)
-        plane_w[1] = odd_w[:, 0, :]
-        plane_w[3] = odd_w[:, 1, :]
-        nc.scalar.copy(odd_w[:].bitcast(U16), w_words16[:, 1:PLANES:2, :])
+        for t in (1, 3):
+            plane_w[t] = keep.tile([P, E * P * 2], U8, name="plane_w%d" % t, align_bytes=64)
+        nc.scalar.copy(plane_w[1][:].bitcast(U16), w_words16[:, 1, :])
         for u in range(2):
             nc.gpsimd.tensor_copy(early_s[u][:], w_scale_bytes[:, 2 * u, :])
         nc.gpsimd.tensor_copy(odd_s[:], w_scale_bytes[:, 1:PLANES:2, :])
+        nc.gpsimd.tensor_copy(plane_w[3][:].bitcast(U16), w_words16[:, 3, :])
 
         def multiply(codes, scales, t, a, b, where):
             bank = in_bank(where, [P, b - a])
@@ -182,7 +182,7 @@ def tile_moe_uni_none_kernel(
                     for t in (0, 2) if b <= 3 * C else (0,):
                         product(xg_w, xg_s, t, a, b, y[t], in_turn)
                 else:
-                    closing_banks.append((a, b, multiply(xg_w, xg_s, 0, a, b, in_turn)))
+                    closing_banks.append((a, b, multiply(xg_w, xg_s, 0, a, b, (own + [in_turn])[len(closing_banks)])))
                 if b == 4 * C:
                     product(xg_w, xg_s, 1, 0, BANK, y[1], in_turn)
             for a, b, bank in closing_banks:
@@ -196,7 +196,7 @@ def tile_moe_uni_none_kernel(
                 nc.scalar.activation(raws[r, u][:], y[2 + u][:].indirect(pos_a[r][:]), COPY)
 
             gather_raw(0, 0, "raw_c00")
-            for a, where in zip((BANK, 2 * BANK), own):
+            for a, where in zip((BANK, 2 * BANK), [in_turn] * 2):
                 product(xg_w, xg_s, 1, a, a + BANK, y[1], where)
             banks_of_plane(xg_w, xg_s, 3, y[3], [in_turn] * 3)
 
@@ -230,12 +230,9 @@ def tile_moe_uni_none_kernel(
                     nc.tensor.transpose(backs[h][:, j * P : (j + 1) * P], words[:, j * P : (j + 1) * P], ident_f[:])
             for h in range(2):
                 nc.scalar.copy(c_pair[0][:, h * HALF : (h + 1) * HALF].bitcast(F32), backs[h][:])
-            gather_raw(1, 1, "raw_c11")
-            raw_turned.append([in_bank(where, [P, 2, 2, P]) for where in own])
-            for u in range(2):
-                turn_raw(1, u, raw_turned[1])
             partial_c = [in_bank(in_turn, [P, 2, HALF]) for h in range(2)]
-            for r in range(2):
+
+            def scale_and_add(r):
                 scaled_c = keep.tile([P, BLOCKS, 2, P], F32, name="scaled_c%d" % r)
                 for j in range(BLOCKS):
                     nc.scalar.activation(scaled_c[:, j, :, :], raw_turned[r][j // 2][:, j % 2, :, :], COPY, scale=gate_cols[0][r][:, j : j + 1])
@@ -246,6 +243,15 @@ def tile_moe_uni_none_kernel(
                             (r, j % 2, u) == (0, 0, 0),
                             (r, j % 2, u) == (1, 1, 1),
                         )
+
+            raw_turned.append([in_bank(where, [P, 2, 2, P]) for where in own])
+            turn_raw(1, 0, raw_turned[1])
+            scale_and_add(0)
+            raws[1, 1] = keep.tile([P, T], F32, name="raw_c11", tag="raw_c11", align_bytes=64)
+            for a in (0, HALF):
+                nc.scalar.activation(raws[1, 1][:, a : a + HALF], y[3][:].indirect(entries(pos_a[1], a, a + HALF)), COPY)
+            turn_raw(1, 1, raw_turned[1])
+            scale_and_add(1)
 
             thirds = lent.tile([P, 2 * T], F32, name="thirds", tag="first_term")
             for u in range(2):

@@ -228,8 +228,6 @@ def tile_moe_uni_none_kernel(
                 words = turned_pairs[:].rearrange("p j m u -> p (j m u)").bitcast(F32)
                 for j in range(2):
                     nc.tensor.transpose(backs[h][:, j * P : (j + 1) * P], words[:, j * P : (j + 1) * P], ident_f[:])
-            for h in range(2):
-                nc.scalar.copy(c_pair[0][:, h * HALF : (h + 1) * HALF].bitcast(F32), backs[h][:])
             partial_c = [in_bank(in_turn, [P, 2, HALF]) for h in range(2)]
 
             def scale_and_add(r):
@@ -256,8 +254,16 @@ def tile_moe_uni_none_kernel(
             thirds = lent.tile([P, 2 * T], F32, name="thirds", tag="first_term")
             for u in range(2):
                 gated(y[2 + u], pos_a, gate_a, 2, thirds[:, u * T : (u + 1) * T])
-            for a in range(0, S, BANK):
+            for h in range(2):
+                nc.vector.tensor_copy(c_pair[0][:, h * HALF : (h + 1) * HALF].bitcast(F32), backs[h][:])
+            for a in range(0, S - BANK, BANK):
                 gather_pairs(0, a, a + BANK)
+            c_single = keep.tile([P, 2, T], BF16, name="c_single", tag="raw_c11", align_bytes=64)
+            nc.gpsimd.tensor_copy(c_single[:], c_pair[0][:, :T].bitcast(BF16).rearrange("p (n u) -> p u n", u=2))
+            for e in (E - 2, E - 1):
+                dst = rows[e // 2][:, (e % 2) * C : (e % 2 + 1) * C].bitcast(BF16).rearrange("p (n u) -> p n u", u=2)
+                for u in range(2):
+                    nc.scalar.activation(dst[:, :, u], c_single[:, u, :].indirect(entries(offs2_t, e * C, (e + 1) * C)), COPY)
             c_pair_values = c_pair[1][:, :T].bitcast(BF16).rearrange("p (n u) -> p n u", u=2)
             for h, a in enumerate((0, HALF)):
                 nc.vector.tensor_tensor(

@@ -18,15 +18,13 @@ COPY = mybir.ActivationFunctionType.Copy
 K, T, E, C = 512, 512, 6, 256
 S = E * C
 P = 128
-PLANES = 4
+BLOCKS = K // P
+TURNS = T // P
 CHOICES = 3
 QUADS = 4
-BLOCKS = T // P
 PER_COL = 16
-BANK = 512
-WIDE = 1024
 HALF = T // 2
-TERM_BUFS = 10
+BANKS = 8
 FLOPS = 2 * 2 * K * K * S
 
 
@@ -37,13 +35,10 @@ def tile_moe_uni_none_kernel(
     with ExitStack() as ctx:
         keep = ctx.enter_context(tc.tile_pool(name="keep", bufs=1))
         ring = ctx.enter_context(tc.tile_pool(name="ring", bufs=2))
-        lent = ctx.enter_context(tc.tile_pool(name="lent", bufs=1))
-        pair_psum = ctx.enter_context(tc.psum_pool(name="pair_psum", bufs=1))
+        psum = ctx.enter_context(tc.psum_pool(name="psum", bufs=1))
 
-        def in_bank(where, shape, dtype=F32):
-            return where[0].tile(shape, dtype, name="bank", tag=where[1])
-
-        own = [(pair_psum, "own0"), (pair_psum, "own1")]
+        def in_bank(n, shape):
+            return psum.tile(shape, F32, name="bank", tag="bank%d" % n)
 
         def load_list(src, name):
             lst = keep.tile([P, src.shape[1]], U16, name=name)
@@ -53,329 +48,275 @@ def tile_moe_uni_none_kernel(
         def entries(lst, a, b):
             return lst[:, a // PER_COL : b // PER_COL]
 
-        x_w = keep.tile([P, WIDE], I32, name="x_w", align_bytes=64)
-        x_s = keep.tile([P, WIDE // 4], I32, name="x_s", align_bytes=64)
-        w_w = keep.tile([P, E, K // 2], I32, name="w_w", align_bytes=64)
+        x_w = keep.tile([P, T], I32, name="x_w", align_bytes=64)
+        x_s = keep.tile([P, T // 4], I32, name="x_s", align_bytes=64)
+        w_w = [keep.tile([P, 2 + 2 * i, K // 2], I32, name="w_w%d" % i, align_bytes=64) for i in range(2)]
         w_s = keep.tile([P, E, K // 4], I32, name="w_s", align_bytes=64)
-        nc.vector.memset(x_s[:], 0)
-        nc.vector.memset(x_w[:, T:], 0)
-        c_pair = [keep.tile([P, WIDE], I32, name="c_pair%d" % u, align_bytes=64) for u in range(2)]
-        for u in range(2):
-            nc.vector.memset(c_pair[u][:, T:], 0)
-        nc.gpsimd.memset(w_s[:], 0)
+        nc.gpsimd.memset(x_s[:], 0)
 
+        w_rows = w_words.rearrange("e s p n -> p (e s) n").bitcast(I32)
         offs_t = load_list(offs, "offs_t")
-        nc.scalar.dma_start(x_w[:, :T], x_words.rearrange("s p t d -> p (s t d)").bitcast(I32))
-        nc.sync.dma_start(w_w[:], w_words.rearrange("e s p n -> p (e s) n").bitcast(I32))
-        for q in range(QUADS):
+
+        def load_w_scales(q):
             nc.sync.dma_start(
                 w_s[32 * q : 32 * q + 4, :, :],
                 w_scales[:, 0, 4 * q : 4 * q + 4, :].rearrange("e b n -> b e n").bitcast(I32),
             )
+
+        load_w_scales(0)
         for q in range(QUADS):
-            nc.sync.dma_start(x_s[32 * q : 32 * q + 4, : T // 4], x_scales[0, 4 * q : 4 * q + 4, :].bitcast(I32))
+            nc.sync.dma_start(x_s[32 * q : 32 * q + 4, :], x_scales[0, 4 * q : 4 * q + 4, :].bitcast(I32))
+        nc.sync.dma_start(x_w[:], x_words.rearrange("s p t d -> p (s t d)").bitcast(I32))
+        nc.sync.dma_start(w_w[0][:], w_rows[:, :2, :])
+        for q in range(1, QUADS):
+            load_w_scales(q)
+        nc.sync.dma_start(w_w[1][:], w_rows[:, 2:, :])
         pos_a = [load_list(src, "pos_a%d" % r) for r, src in enumerate((pos1, pos2, pos3))]
-        offs2_t = load_list(offs2, "offs2_t")
-        pos_b = [load_list(src, "pos_b%d" % r) for r, src in enumerate((pos4, pos5, pos6))]
         gate_a = keep.tile([P, CHOICES, T], F32, name="gate_a")
         nc.sync.dma_start(gate_a[:], gate1.rearrange("r p n -> p r n"))
+
+        def load_gate_columns(gate, choices, name):
+            cols = keep.tile([P, choices * TURNS], F32, name=name)
+            pieces = gate.rearrange("r p (j m) -> (r p j) m", m=P)
+            with nc.allow_non_contiguous_dma(reason="one gate value a partition"):
+                nc.sync.dma_start(cols[:], pieces[0 : (choices * TURNS - 1) * (P + 1) + 1 : P + 1, :].rearrange("i m -> m i"))
+            return cols
+
+        cols_a = load_gate_columns(gate1, CHOICES, "cols_a")
+        offs2_t = load_list(offs2, "offs2_t")
+        pos_b = [load_list(src, "pos_b%d" % r) for r, src in enumerate((pos4, pos5, pos6))]
         gate_b = keep.tile([P, CHOICES, T], F32, name="gate_b")
         nc.sync.dma_start(gate_b[:], gate2.rearrange("r p n -> p r n"))
+        cols_b = load_gate_columns(gate2, 2, "cols_b")
 
-        gate_cols = [[keep.tile([P, BLOCKS], F32, name="gate_cols%d%d" % (i, r)) for r in range(2)] for i in range(2)]
-        with nc.allow_non_contiguous_dma(reason="one gate value a partition"):
-            for i, gate in enumerate((gate1, gate2)):
-                for r in range(2):
-                    nc.sync.dma_start(gate_cols[i][r][:], gate[r, 0, :].rearrange("(j p) -> p j", p=P))
+        ident = keep.tile([P, P], F32, name="ident")
+        make_identity(nc, ident[:])
 
-        ident_f = keep.tile([P, P], F32, name="ident_f")
-        make_identity(nc, ident_f[:])
+        w_codes = [w_w[min(e // 2, 1)][:, e if e < 2 else e - 2, :].bitcast(U8) for e in range(E)]
 
-        early_s = [keep.tile([P, E * P], U8, name="early_s%d" % u, align_bytes=64) for u in range(2)]
-        odd_s = keep.tile([P, 2, E * P], U8, name="odd_s", align_bytes=64)
-        plane_s = [early_s[0][:], odd_s[:, 0, :], early_s[1][:], odd_s[:, 1, :]]
-        w_words16 = w_w[:].rearrange("p e n -> p (e n)").bitcast(U16).rearrange("p (m t) -> p t m", t=PLANES)
-        w_scale_bytes = w_s[:].rearrange("p e n -> p (e n)").bitcast(U8).rearrange("p (m t) -> p t m", t=PLANES)
-        plane_w = {}
-        even_w = keep.tile([P, 2, E * P * 2], U8, name="even_w", align_bytes=64)
-        plane_w[0] = even_w[:, 0, :]
-        plane_w[2] = even_w[:, 1, :]
-        nc.scalar.copy(even_w[:].bitcast(U16), w_words16[:, 0:PLANES:2, :])
-        for t in (1, 3):
-            plane_w[t] = keep.tile([P, E * P * 2], U8, name="plane_w%d" % t, align_bytes=64)
-        nc.scalar.copy(plane_w[1][:].bitcast(U16), w_words16[:, 1, :])
-        for u in range(2):
-            nc.gpsimd.tensor_copy(early_s[u][:], w_scale_bytes[:, 2 * u, :])
-        nc.gpsimd.tensor_copy(odd_s[:], w_scale_bytes[:, 1:PLANES:2, :])
-        nc.gpsimd.tensor_copy(plane_w[3][:].bitcast(U16), w_words16[:, 3, :])
+        def product(dst, codes, scales, e, b):
+            nc.tensor.matmul_mx(
+                out=dst,
+                lhsT=w_codes[e][:, 2 * P * b : 2 * P * (b + 1)].bitcast(FP4X4),
+                lhsT_scale=w_s[:, e, :].bitcast(U8)[:, P * b : P * (b + 1)],
+                rhs=codes.bitcast(FP8X4),
+                rhs_scale=scales,
+                start=True,
+                stop=True,
+            )
 
-        def multiply(codes, scales, t, a, b, where):
-            bank = in_bank(where, [P, b - a])
-            for lo in range(a, b, C):
-                e, hi = lo // C, min(lo + C, b)
-                nc.tensor.matmul_mx(
-                    out=bank[:, lo - a : hi - a],
-                    lhsT=plane_w[t][:, e * 2 * P : (e + 1) * 2 * P].bitcast(FP4X4),
-                    lhsT_scale=plane_s[t][:, e * P : (e + 1) * P],
-                    rhs=codes[:, lo:hi].bitcast(FP8X4),
-                    rhs_scale=scales[:, lo:hi],
-                    start=True,
-                    stop=True,
-                )
+        def multiply(codes, scales, e, first, bank_no):
+            bank = in_bank(bank_no, [P, 2, C])
+            for i in range(2):
+                product(bank[:, i, :], codes, scales, e, first + i)
             return bank
 
-        def product(codes, scales, t, a, b, dst, where):
-            nc.scalar.copy(dst[:, a:b], multiply(codes, scales, t, a, b, where)[:])
+        def products(codes, scales, e):
+            return [multiply(codes, scales, e, first, (2 * e + first // 2) % BANKS) for first in (0, 2)]
 
-        def banks_of_plane(codes, scales, t, dst, places):
-            for a, where in zip(range(0, S, BANK), places):
-                product(codes, scales, t, a, a + BANK, dst, where)
+        def empty(copy, banks, e, dst, first):
+            for i in range(2):
+                copy(dst[first + i][:, e * C : (e + 1) * C], banks[first // 2][:, i, :])
+
+        def turn(dst, src, start=True, stop=True):
+            nc.tensor.matmul(dst, lhsT=src, rhs=ident[:], is_transpose=True, start=start, stop=stop)
 
         def gated(window, pos, gate, r, dst, a=0, b=T):
             nc.vector.tensor_tensor(dst[:, a:b], window[:].indirect(entries(pos[r], a, b)), gate[:, r, a:b], MULT)
 
-        def new_term(r):
-            return ring.tile([P, T], F32, name="term", bufs=TERM_BUFS)
+        def raw(window, pos, r, dst, a=0, b=T):
+            nc.scalar.activation(dst[:, a:b], window[:].indirect(entries(pos[r], a, b)), COPY)
 
-        def add_turned(window, pos, gate, choices, where, term_tile=new_term):
-            bank = in_bank(where, [P, BLOCKS, P])
-            for r in range(choices):
-                term = term_tile(r)
-                gated(window, pos, gate, r, term)
-                for j in range(BLOCKS):
-                    nc.tensor.matmul(
-                        bank[:, j, :],
-                        lhsT=term[:, j * P : (j + 1) * P],
-                        rhs=ident_f[:],
-                        is_transpose=True,
-                        start=(r == 0 and j == 0),
-                        stop=(r == choices - 1 and j == BLOCKS - 1),
-                    )
-            return bank
+        def new_term():
+            return ring.tile([P, T], F32, name="term", bufs=4)
 
-        def turn_back(bank, turned, blocks):
-            nc.scalar.copy(turned[:], bank[:])
-            for j in range(BLOCKS):
-                nc.tensor.transpose(blocks[j], turned[:, j, :], ident_f[:])
+        def new_raw():
+            return ring.tile([P, T], F32, name="raw", bufs=4)
 
-        xg_w = keep.tile([P, S], U32, name="xg_w", align_bytes=64)
-        xg_s = keep.tile([P, S], U8, name="xg_s", tag="xg_s", align_bytes=64)
-        y = [keep.tile([P, S], F32, name="y%d" % t) for t in range(PLANES)]
+        y = [keep.tile([P, S], F32, name="y%d" % b) for b in range(BLOCKS)]
+        banks_y = []
+        for e in range(E):
+            xg_w = ring.tile([P, C], U32, name="xg_w", bufs=4, align_bytes=64)
+            xg_s = ring.tile([P, C], U8, name="xg_s", bufs=2, align_bytes=64)
+            slots = entries(offs_t, e * C, (e + 1) * C)
+            nc.vector.tensor_copy(xg_s[:], x_s[:].bitcast(U8).indirect(slots))
+            nc.vector.tensor_copy(xg_w[:], x_w[:].bitcast(U32).indirect(slots))
+            banks_y.append(products(xg_w[:], xg_s[:], e))
+            if e < E // 2:
+                empty(nc.scalar.copy, banks_y[e], e, y, 0)
+            if e == E - 1:
+                empty(nc.scalar.copy, banks_y[E // 2], E // 2, y, 0)
+            if e != E - 2:
+                empty(nc.scalar.copy, banks_y[e], e, y, 2)
+        for e, first in ((E - 2, 2), (E - 2, 0), (E - 1, 0)):
+            empty(nc.vector.tensor_copy, banks_y[e], e, y, first)
 
-        for a in range(0, S, S // 2):
-            nc.vector.tensor_copy(xg_w[:, a : a + S // 2], x_w[:].bitcast(U32).indirect(entries(offs_t, a, a + S // 2)))
-        rows = [keep.tile([P, 2 * BANK], U32, name="rows%d" % i, align_bytes=64) for i in range(E // 2)]
+        def turn_terms(term, banks, i, a, b, first=None, last=None):
+            for j in range(a // P, b // P):
+                start = True if first is None else (first and j % 2 == 0)
+                stop = True if last is None else (last and j % 2 == 1)
+                dst = banks[j // 2][:, j % 2, :, 64 * i : 64 * (i + 1)].rearrange("p u (m v) -> p m u v", v=2)
+                turn(dst, term[:, j * P : (j + 1) * P], start, stop)
 
-        def gather_pairs(u, a, b):
-            lo = u * BANK + a % BANK
-            nc.vector.tensor_copy(rows[a // BANK][:, lo : lo + b - a], c_pair[u][:].bitcast(U32).indirect(entries(offs2_t, a, b)))
+        def bank_pair(n):
+            return [in_bank(n + h, [P, 2, 2, P]) for h in range(2)]
 
-        def turn(dst, src, start, stop):
-            nc.tensor.matmul(dst, lhsT=src, rhs=ident_f[:], is_transpose=True, start=start, stop=stop)
+        sums = bank_pair(4)
+        raws = [bank_pair(6), bank_pair(0), bank_pair(2)]
+        c_tok = [keep.tile([P, 2, 2 * P], BF16, name="c_tok%d" % j, align_bytes=64) for j in range(TURNS)]
+        part = [[keep.tile([P, 2, P], F32, name="part%d%d" % (r, j)) for j in range(TURNS)] for r in range(2)]
 
-        with tc.psum_pool(name="ring_psum", bufs=6) as ring_psum:
-            in_turn = (ring_psum, "in_turn")
-            closing_banks = []
-            for a, b in [(0, C), (C, 3 * C), (3 * C, 4 * C), (4 * C, S - C), (S - C, S - P), (S - P, S)]:
-                nc.vector.tensor_copy(xg_s[:, a:b], x_s[:].bitcast(U8).indirect(entries(offs_t, a, b)))
-                if b <= 4 * C:
-                    for t in (0, 2) if b <= 3 * C else (0,):
-                        product(xg_w, xg_s, t, a, b, y[t], in_turn)
-                else:
-                    closing_banks.append((a, b, multiply(xg_w, xg_s, 0, a, b, (own + [in_turn])[len(closing_banks)])))
-                if b == 4 * C:
-                    product(xg_w, xg_s, 1, 0, BANK, y[1], in_turn)
-            for a, b, bank in closing_banks:
-                nc.vector.tensor_copy(y[0][:, a:b], bank[:])
-            for a, b in [(3 * C, 4 * C), (4 * C, S)]:
-                product(xg_w, xg_s, 2, a, b, y[2], in_turn)
-            raws = {}
+        def region(banks, j):
+            return banks[j // 2][:, j % 2, :, :]
 
-            def gather_raw(r, u, tag):
-                raws[r, u] = keep.tile([P, T], F32, name="raw_c%d%d" % (r, u), tag=tag, align_bytes=64)
-                nc.scalar.activation(raws[r, u][:], y[2 + u][:].indirect(pos_a[r][:]), COPY)
+        def gated_turned(i, r):
+            term = new_term()
+            gated(y[i], pos_a, gate_a, r, term)
+            turn_terms(term, sums, i, 0, T, (i, r) == (0, 0), (i, r) == (1, CHOICES - 1))
 
-            gather_raw(0, 0, "raw_c00")
-            for a, where in zip((BANK, 2 * BANK), [in_turn] * 2):
-                product(xg_w, xg_s, 1, a, a + BANK, y[1], where)
-            banks_of_plane(xg_w, xg_s, 3, y[3], [in_turn] * 3)
+        def raw_turned(i, r, a=0, b=T):
+            term = new_raw()
+            raw(y[2 + i], pos_a, r, term, a, b)
+            turn_terms(term, raws[r], i, a, b)
 
-            sums = [in_bank(where, [P, 2, 2, P]) for where in own]
-            first_term = lent.tile([P, T], F32, name="first_term", tag="first_term")
-            for t in range(2):
-                for r in range(CHOICES):
-                    closing = t == 1 and r == CHOICES - 1
-                    for a, b in [(0, HALF), (HALF, T)] if closing else [(0, T)]:
-                        term = first_term if (t, r) == (1, 0) else new_term(r)
-                        gated(y[t], pos_a, gate_a, r, term, a, b)
-                        for j in range(a // P, b // P):
-                            turn(sums[j // 2][:, j % 2, t, :], term[:, j * P : (j + 1) * P], (t, r, j % 2) == (0, 0, 0), closing and j % 2 == 1)
-
-            def turn_raw(r, u, banks):
-                for j in range(BLOCKS):
-                    nc.tensor.transpose(banks[j // 2][:, j % 2, u, :], raws[r, u][:, j * P : (j + 1) * P], ident_f[:])
-
-            gather_raw(0, 1, "raw_c01")
-            gather_raw(1, 0, "xg_s")
-            raw_turned = [[in_bank(in_turn, [P, 2, 2, P]) for h in range(2)]]
-            for u in range(2):
-                turn_raw(0, u, raw_turned[0])
-            backs = []
-            for h in range(2):
-                turned_pairs = keep.tile([P, 2, P, 2], BF16, name="turned_pairs", tag=("turned_pairs", "raw_c11")[h], align_bytes=64)
-                nc.scalar.copy(turned_pairs[:], sums[h][:].rearrange("p j u m -> p j m u"))
-                backs.append(in_bank(in_turn, [P, HALF]))
-                words = turned_pairs[:].rearrange("p j m u -> p (j m u)").bitcast(F32)
-                for j in range(2):
-                    nc.tensor.transpose(backs[h][:, j * P : (j + 1) * P], words[:, j * P : (j + 1) * P], ident_f[:])
-            partial_c = [in_bank(in_turn, [P, 2, HALF]) for h in range(2)]
-
-            def scale_and_add(r):
-                scaled_c = keep.tile([P, BLOCKS, 2, P], F32, name="scaled_c%d" % r)
-                for j in range(BLOCKS):
-                    nc.scalar.activation(scaled_c[:, j, :, :], raw_turned[r][j // 2][:, j % 2, :, :], COPY, scale=gate_cols[0][r][:, j : j + 1])
-                    for u in range(2):
-                        turn(
-                            partial_c[j // 2][:, u, (j % 2) * P : (j % 2 + 1) * P],
-                            scaled_c[:, j, u, :],
-                            (r, j % 2, u) == (0, 0, 0),
-                            (r, j % 2, u) == (1, 1, 1),
-                        )
-
-            raw_turned.append([in_bank(where, [P, 2, 2, P]) for where in own])
-            turn_raw(1, 0, raw_turned[1])
-            scale_and_add(0)
-            raws[1, 1] = keep.tile([P, T], F32, name="raw_c11", tag="raw_c11", align_bytes=64)
-            for a in (0, HALF):
-                nc.scalar.activation(raws[1, 1][:, a : a + HALF], y[3][:].indirect(entries(pos_a[1], a, a + HALF)), COPY)
-            turn_raw(1, 1, raw_turned[1])
-            scale_and_add(1)
-
-            thirds = lent.tile([P, 2 * T], F32, name="thirds", tag="first_term")
-            for u in range(2):
-                gated(y[2 + u], pos_a, gate_a, 2, thirds[:, u * T : (u + 1) * T])
-            for h in range(2):
-                nc.vector.tensor_copy(c_pair[0][:, h * HALF : (h + 1) * HALF].bitcast(F32), backs[h][:])
-            for a in range(0, S - BANK, BANK):
-                gather_pairs(0, a, a + BANK)
-            c_single = keep.tile([P, 2, T], BF16, name="c_single", tag="raw_c11", align_bytes=64)
-            nc.gpsimd.tensor_copy(c_single[:], c_pair[0][:, :T].bitcast(BF16).rearrange("p (n u) -> p u n", u=2))
-            for e in (E - 2, E - 1):
-                dst = rows[e // 2][:, (e % 2) * C : (e % 2 + 1) * C].bitcast(BF16).rearrange("p (n u) -> p n u", u=2)
-                for u in range(2):
-                    nc.scalar.activation(dst[:, :, u], c_single[:, u, :].indirect(entries(offs2_t, e * C, (e + 1) * C)), COPY)
-            c_pair_values = c_pair[1][:, :T].bitcast(BF16).rearrange("p (n u) -> p n u", u=2)
-            for h, a in enumerate((0, HALF)):
-                nc.vector.tensor_tensor(
-                    c_pair_values[:, a : a + HALF, :],
-                    partial_c[h][:].rearrange("p u n -> p n u"),
-                    thirds[:].rearrange("p (u n) -> p n u", u=2)[:, a : a + HALF, :],
-                    ADD,
+        for n in range(4):
+            gated_turned(n // CHOICES, n % CHOICES)
+            raw_turned(n % 2, n // 2)
+        for j in range(TURNS):
+            nc.scalar.activation(part[0][j][:], region(raws[0], j), COPY, scale=cols_a[:, j : j + 1])
+        gated_turned(1, 1)
+        for i in range(2):
+            raw_turned(i, 2, 0, HALF)
+        gated_turned(1, 2)
+        for i in range(2):
+            raw_turned(i, 2, HALF, T)
+        for j in range(TURNS):
+            nc.vector.scalar_tensor_tensor(part[1][j][:], region(raws[1], j), cols_a[:, TURNS + j : TURNS + j + 1], part[0][j][:], MULT, ADD)
+        c_pair = keep.tile([P, 2, T], I32, name="c_pair", align_bytes=64)
+        first_back = in_bank(6, [P, 2, HALF])
+        backs = [[first_back[:, u, :] for u in range(2)], []]
+        for h in range(2):
+            if h == 1:
+                backs[1].extend(in_bank(n, [P, HALF]) for n in (7, 4))
+            for j in (2 * h, 2 * h + 1):
+                nc.scalar.copy(c_tok[j][:, :, :P], region(sums, j))
+                nc.vector.scalar_tensor_tensor(
+                    c_tok[j][:, :, P:], region(raws[2], j), cols_a[:, 2 * TURNS + j : 2 * TURNS + j + 1], part[1][j][:], MULT, ADD
                 )
+                words = c_tok[j][:].bitcast(F32)
+                for u in range(2):
+                    turn(backs[h][u][:, (j % 2) * P : (j % 2 + 1) * P], words[:, u, :])
+        nc.vector.tensor_copy(c_pair[:, :, :HALF].bitcast(F32), first_back[:])
+        nc.vector.tensor_copy(c_pair[:, 0, HALF:].bitcast(F32), backs[1][0][:])
+        nc.scalar.copy(c_pair[:, 1, HALF:].bitcast(F32), backs[1][1][:])
 
-        named_psum = ctx.enter_context(tc.psum_pool(name="named_psum", bufs=1))
-        named = [(named_psum, "named%d" % i) for i in range(6)] + own
+        z = [keep.tile([P, S], F32, name="z%d" % b) for b in range(BLOCKS)]
+        woven = {}
 
-        woven = keep.tile([P, S * 2], U32, name="woven", align_bytes=64)
-        cq_w = keep.tile([P, S], U32, name="cq_w", tag="cq_w", align_bytes=64)
-        cq_s = keep.tile([P, S], U8, name="cq_s", align_bytes=64)
-        z = [keep.tile([P, S], F32, name="z%d" % t) for t in range(PLANES)]
-
-        for a, b in [(0, C), (C, BANK), (BANK, 2 * BANK), (2 * BANK, S - C), (S - C, S)]:
-            gather_pairs(1, a, b)
-
-        def weave(copy, e):
-            copy(
-                woven[:, 2 * e * C : 2 * (e + 1) * C].rearrange("p (n u) -> p n u", u=2),
-                rows[e // 2][:].rearrange("p (u n) -> p n u", u=2)[:, (e % 2) * C : (e % 2 + 1) * C, :],
-            )
+        def gather_and_weave(a, b, tag, copy):
+            rows = keep.tile([P, 2, b - a], U32, name="rows", tag=tag, align_bytes=64)
+            for u in range(2):
+                nc.vector.tensor_copy(rows[:, u, :], c_pair[:, u, :].bitcast(U32).indirect(entries(offs2_t, a, b)))
+            woven[a] = keep.tile([P, b - a, 2], U32, name="woven%d" % a, align_bytes=64)
+            copy(woven[a][:], rows[:].rearrange("p u n -> p n u"))
 
         def quantise(a, b):
-            nc.vector.quantize_mx(out=cq_w[:, a:b].bitcast(FP8X4), scales=cq_s[:, a:b], in_=woven[:, 2 * a : 2 * b].bitcast(BF16))
+            cq_w = keep.tile([P, b - a], U32, name="cq_w%d" % a, align_bytes=64)
+            cq_s = keep.tile([P, b - a], U8, name="cq_s%d" % a, align_bytes=64)
+            nc.vector.quantize_mx(out=cq_w[:].bitcast(FP8X4), scales=cq_s[:], in_=woven[a][:].rearrange("p n u -> p (n u)").bitcast(BF16))
+            return cq_w[:], cq_s[:]
 
-        on_gpsimd, on_scalar = (0, 1), (2, 3, 4, 5)
-        for e in on_gpsimd:
-            weave(nc.gpsimd.tensor_copy, e)
-        for e in on_scalar:
-            weave(nc.scalar.copy, e)
-        for e, where in enumerate((named[3], named[4], named[5], named[0])):
-            quantise(e * C, (e + 1) * C)
-            product(cq_w, cq_s, 0, e * C, (e + 1) * C, z[0], where)
-        late = [named[1], named[2], named[6]]
-        ends = [(4 * C, 5 * C), (5 * C, S - P), (S - P, S)]
-        last_banks = []
-        for (a, b), where in zip(ends, late):
-            quantise(a, b)
-            last_banks.append(multiply(cq_w, cq_s, 0, a, b, where))
-        for (a, b), bank in zip(ends, last_banks):
-            nc.vector.tensor_copy(z[0][:, a:b], bank[:])
-        for t in range(1, PLANES):
-            banks_of_plane(cq_w, cq_s, t, z[t], late)
+        last = E - 1
+        for e in range(2):
+            gather_and_weave(e * C, (e + 1) * C, "rows%d" % e, nc.scalar.copy)
+        left = []
+        for e in range(last):
+            banks = products(*quantise(e * C, (e + 1) * C), e)
+            if e + 2 < last:
+                gather_and_weave((e + 2) * C, (e + 3) * C, "rows%d" % (e % 2), nc.gpsimd.tensor_copy)
+            else:
+                a = last * C + (e + 2 - last) * P
+                gather_and_weave(a, a + P, "rows%d" % (e % 2), nc.scalar.copy)
+            if e != E // 2:
+                empty(nc.scalar.copy, banks, e, z, 0)
+            else:
+                left.append((banks, e))
+            empty(nc.scalar.copy, banks, e, z, 2)
+        alone = [in_bank(n, [P, C]) for n in (2, 4)]
+        together = in_bank(3, [P, 2, C])
+        places = [alone[0][:], alone[1][:], together[:, 0, :], together[:, 1, :]]
+        for h in range(2):
+            codes, scales = quantise(last * C + h * P, last * C + (h + 1) * P)
+            for b in (0, 2, 3, 1):
+                product(places[b][:, h * P : (h + 1) * P], codes, scales, last, b)
+            if h == 0:
+                empty(nc.vector.tensor_copy, *left[h], z, 0)
+        nc.vector.tensor_copy(z[0][:, last * C :], places[0])
+        for b in (2, 3, 1):
+            nc.scalar.copy(z[b][:, last * C :], places[b])
 
-        out_planes = out.rearrange("(p t) n -> p t n", t=PLANES)
-        res = keep.tile([P, PLANES, T], F32, name="res")
-        last = PLANES - 1
+        res = [keep.tile([P, T], F32, name="res%d" % b) for b in range(BLOCKS)]
 
-        def blocks_of(bank):
-            return [bank[:, j * P : (j + 1) * P] for j in range(BLOCKS)]
+        def add_turned(b, r, bank, pieces=((0, T),)):
+            for a, end in pieces:
+                term = new_term()
+                gated(z[b], pos_b, gate_b, r, term, a, end)
+                for j in range(a // P, end // P):
+                    turn(bank[:, j, :], term[:, j * P : (j + 1) * P], r == 0 and j == 0, r == CHOICES - 1 and j == TURNS - 1)
 
-        def raw_term(r, where):
-            raw = keep.tile([P, T], F32, name="raw%d" % r, tag="raw%d" % r, align_bytes=64)
-            nc.scalar.activation(raw[:], z[last][:].indirect(pos_b[r][:]), COPY)
-            bank = in_bank(where, [P, BLOCKS, P])
-            for j in range(BLOCKS):
-                nc.tensor.transpose(bank[:, j, :], raw[:, j * P : (j + 1) * P], ident_f[:])
-            return bank
+        def turn_back(b, bank, bank_no):
+            turned = keep.tile([P, TURNS, P], F32, name="turned%d" % b)
+            nc.scalar.copy(turned[:], bank[:])
+            back = in_bank(bank_no, [P, T])
+            for j in range(TURNS):
+                turn(back[:, j * P : (j + 1) * P], turned[:, j, :])
+            return back
 
-        def scale_back(r, bank, partial):
-            scaled = keep.tile([P, BLOCKS, P], F32, name="scaled%d" % r)
-            for j in range(BLOCKS):
-                nc.scalar.activation(scaled[:, j, :], bank[:, j, :], COPY, scale=gate_cols[1][r][:, j : j + 1])
-            for j in range(BLOCKS):
-                nc.tensor.matmul(
-                    partial[:, j * P : (j + 1) * P],
-                    lhsT=scaled[:, j, :],
-                    rhs=ident_f[:],
-                    is_transpose=True,
-                    start=(r == 0 and j == 0),
-                    stop=(r == 1 and j == BLOCKS - 1),
-                )
+        def store(b, back):
+            nc.scalar.copy(res[b][:], back[:])
+            nc.sync.dma_start(out[b * P : (b + 1) * P, :], res[b][:])
 
-        def turned_tile(t):
-            return keep.tile([P, BLOCKS, P], F32, name="turned%d" % t, tag="turned%d" % t)
+        def raw_out(i, r):
+            term = new_raw()
+            raw(z[2 + i], pos_b, r, term)
+            for j in range(TURNS):
+                turn(raw_banks[r][j // 2][:, j % 2, i, :], term[:, j * P : (j + 1) * P])
 
-        def term_on(tags):
-            return lambda r: keep.tile([P, T], F32, name="term_" + tags[r], tag=tags[r], align_bytes=64)
+        def scale_back(r):
+            for j in range(TURNS):
+                scaled = keep.tile([P, 2, P], F32, name="scaled%d%d" % (r, j))
+                nc.scalar.activation(scaled[:], region(raw_banks[r], j), COPY, scale=cols_b[:, TURNS * r + j : TURNS * r + j + 1])
+                for i in range(2):
+                    turn(partial[i][:, j * P : (j + 1) * P], scaled[:, i, :], r == 0 and j == 0, r == 1 and j == TURNS - 1)
 
-        backs = [in_bank(named[3 + t], [P, T]) for t in range(last)]
-        sum0 = add_turned(z[0], pos_b, gate_b, CHOICES, late[0])
-        sum1 = add_turned(z[1], pos_b, gate_b, 2, late[1], term_on(["first", "cq_w"]))
-        raw_banks = [raw_term(0, named[0]), raw_term(1, named[7])]
-        turn_back(sum0, turned_tile(0), blocks_of(backs[0]))
-        turn_back(sum1, turned_tile(1), blocks_of(backs[1]))
-        nc.scalar.copy(res[:, 0, :], backs[0][:])
-        nc.sync.dma_start(out_planes[:, 0, :], res[:, 0, :])
-        sum2 = add_turned(z[2], pos_b, gate_b, CHOICES, late[2], term_on(["first", "raw0", "raw1"]))
-        partial_last = in_bank(late[0], [P, T])
-        scale_back(0, raw_banks[0], partial_last)
-        scale_back(1, raw_banks[1], partial_last)
-        turn_back(sum2, turned_tile(2), blocks_of(backs[2]))
-        for a in (0, HALF):
-            nc.scalar.copy(res[:, 2, a : a + HALF], backs[2][:, a : a + HALF])
-            nc.scalar.dma_start(out_planes[:, 2, a : a + HALF], res[:, 2, a : a + HALF])
+        sum0 = in_bank(5, [P, TURNS, P])
+        raw_banks = [bank_pair(6), bank_pair(0)]
+        partial = [in_bank(2 + i, [P, T]) for i in range(2)]
+        add_turned(0, 0, sum0, ((0, HALF), (HALF, T)))
+        raw_out(0, 0)
+        add_turned(0, 1, sum0)
+        raw_out(1, 0)
+        add_turned(0, 2, sum0)
+        raw_out(0, 1)
+        raw_out(1, 1)
+        scale_back(0)
+        sum1 = in_bank(6, [P, TURNS, P])
+        add_turned(1, 0, sum1)
+        add_turned(1, 1, sum1)
+        back0 = turn_back(0, sum0, 4)
+        add_turned(1, 2, sum1)
+        store(0, back0)
+        scale_back(1)
+        store(1, turn_back(1, sum1, 7))
 
-        both_thirds = keep.tile([P, 2 * T], F32, name="both_thirds", tag="turned0")
-        thirds_out = [both_thirds[:, :T], both_thirds[:, T:]]
+        thirds = [keep.tile([P, T], F32, name="third%d" % i) for i in range(2)]
 
-        def finish(t, partial, third, a, b):
-            nc.vector.tensor_tensor(res[:, t, a:b], partial[:, a:b], third[:, a:b], ADD)
-            nc.sync.dma_start(out_planes[:, t, a:b], res[:, t, a:b])
+        def finish(i, a, b):
+            nc.vector.tensor_tensor(res[2 + i][:, a:b], partial[i][:, a:b], thirds[i][:, a:b], ADD)
+            nc.sync.dma_start(out[(2 + i) * P : (3 + i) * P, a:b], res[2 + i][:, a:b])
 
-        pieces = [(0, HALF), (HALF, 3 * T // 4), (3 * T // 4, T)]
-        gated(z[1], pos_b, gate_b, 2, thirds_out[0])
-        gated(z[last], pos_b, gate_b, 2, thirds_out[1], *pieces[0])
-        finish(1, backs[1], thirds_out[0], 0, T)
-        for done, following in zip(pieces, pieces[1:]):
-            gated(z[last], pos_b, gate_b, 2, thirds_out[1], *following)
-            finish(last, partial_last, thirds_out[1], *done)
-        finish(last, partial_last, thirds_out[1], *pieces[-1])
+        for i in range(2):
+            gated(z[2 + i], pos_b, gate_b, 2, thirds[i])
+        finish(0, 0, T)
+        finish(1, 0, HALF + P)
+        finish(1, HALF + P, T)

@@ -35,6 +35,7 @@ def tile_moe_uni_none_kernel(
     with ExitStack() as ctx:
         keep = ctx.enter_context(tc.tile_pool(name="keep", bufs=1))
         ring = ctx.enter_context(tc.tile_pool(name="ring", bufs=2))
+        lent = ctx.enter_context(tc.tile_pool(name="lent", bufs=1))
         psum = ctx.enter_context(tc.psum_pool(name="psum", bufs=1))
 
         def in_bank(n, shape):
@@ -57,8 +58,8 @@ def tile_moe_uni_none_kernel(
         w_rows = w_words.rearrange("e s p n -> p (e s) n").bitcast(I32)
         offs_t = load_list(offs, "offs_t")
 
-        def load_w_scales(q):
-            nc.sync.dma_start(
+        def load_w_scales(q, queue=nc.sync):
+            queue.dma_start(
                 w_s[32 * q : 32 * q + 4, :, :],
                 w_scales[:, 0, 4 * q : 4 * q + 4, :].rearrange("e b n -> b e n").bitcast(I32),
             )
@@ -111,8 +112,8 @@ def tile_moe_uni_none_kernel(
                 product(bank[:, i, :], codes, scales, e, first + i)
             return bank
 
-        def products(codes, scales, e):
-            return [multiply(codes, scales, e, first, (2 * e + first // 2) % BANKS) for first in (0, 2)]
+        def products(codes, scales, turn_no, e=None):
+            return [multiply(codes, scales, turn_no if e is None else e, first, (2 * turn_no + first // 2) % BANKS) for first in (0, 2)]
 
         def empty(copy, banks, e, dst, first):
             for i in range(2):
@@ -141,6 +142,13 @@ def tile_moe_uni_none_kernel(
             slots = entries(offs_t, e * C, (e + 1) * C)
             nc.vector.tensor_copy(xg_s[:], x_s[:].bitcast(U8).indirect(slots))
             nc.vector.tensor_copy(xg_w[:], x_w[:].bitcast(U32).indirect(slots))
+            if e == 0:
+                for b in range(BLOCKS):
+                    bank = in_bank(4 + b, [P, C])
+                    product(bank[:], xg_w[:], xg_s[:], e, b)
+                    nc.scalar.copy(y[b][:, :C], bank[:])
+                banks_y.append(None)
+                continue
             banks_y.append(products(xg_w[:], xg_s[:], e))
             if e < E // 2:
                 empty(nc.scalar.copy, banks_y[e], e, y, 0)
@@ -213,44 +221,80 @@ def tile_moe_uni_none_kernel(
         z = [keep.tile([P, S], F32, name="z%d" % b) for b in range(BLOCKS)]
         woven = {}
 
-        def gather_and_weave(a, b, tag, copy):
-            rows = keep.tile([P, 2, b - a], U32, name="rows", tag=tag, align_bytes=64)
-            for u in range(2):
-                nc.vector.tensor_copy(rows[:, u, :], c_pair[:, u, :].bitcast(U32).indirect(entries(offs2_t, a, b)))
-            woven[a] = keep.tile([P, b - a, 2], U32, name="woven%d" % a, align_bytes=64)
-            copy(woven[a][:], rows[:].rearrange("p u n -> p n u"))
+        def gather_pairs(e, tag, first_row=0):
+            if tag is None:
+                rows[e] = lent.tile([P, 2, C], U32, name="lent_rows", align_bytes=64, offset=8 * C)
+            else:
+                rows[e] = keep.tile([P, 2, C], U32, name="rows", tag=tag, align_bytes=64)
+            for u in range(first_row, 2):
+                nc.vector.tensor_copy(rows[e][:, u, :], c_pair[:, u, :].bitcast(U32).indirect(entries(offs2_t, e * C, (e + 1) * C)))
+
+        def gather_single(e):
+            dst = rows[e][:, 0, :].bitcast(BF16).rearrange("p (n v) -> p n v", v=2)
+            for v in range(2):
+                nc.scalar.activation(dst[:, :, v], c_single[:, v, :].indirect(entries(offs2_t, e * C, (e + 1) * C)), COPY)
+
+        def weave(copy, e, dst):
+            copy(dst, rows[e][:].rearrange("p u n -> p n u"))
+
+        def new_woven(a, experts, tag):
+            if tag is None:
+                woven[a] = lent.tile([P, experts * C, 2], U32, name="lent_woven%d" % a, align_bytes=64, offset=0 if a == 0 else 16 * C)
+            else:
+                woven[a] = keep.tile([P, experts * C, 2], U32, name="woven", tag=tag, align_bytes=64)
+            return [woven[a][:, i * C : (i + 1) * C, :] for i in range(experts)]
 
         def quantise(a, b):
-            cq_w = keep.tile([P, b - a], U32, name="cq_w%d" % a, align_bytes=64)
+            if a <= 2 * C:
+                cq_w = lent.tile([P, b - a], U32, name="lent_codes%d" % a, align_bytes=64, offset=16 * C if a == 0 else 0)
+            else:
+                cq_w = keep.tile([P, b - a], U32, name="cq_w%d" % a, align_bytes=64)
             cq_s = keep.tile([P, b - a], U8, name="cq_s%d" % a, align_bytes=64)
             nc.vector.quantize_mx(out=cq_w[:].bitcast(FP8X4), scales=cq_s[:], in_=woven[a][:].rearrange("p n u -> p (n u)").bitcast(BF16))
             return cq_w[:], cq_s[:]
 
+        def quantise_and_multiply(e, experts):
+            codes, scales = quantise(e * C, (e + experts) * C)
+            for i in range(experts):
+                banks_z[e + i] = products(codes[:, i * C : (i + 1) * C], scales[:, i * C : (i + 1) * C], e + i)
+
+        def empty_z(copy, e, first):
+            empty(copy, banks_z[e], e, z, first)
+
         last = E - 1
+        rows, banks_z = {}, {}
+        c_single = keep.tile([P, 2, T], BF16, name="c_single", align_bytes=64)
+        nc.scalar.copy(c_single[:], c_pair[:, 0, :].bitcast(BF16).rearrange("p (n v) -> p v n", v=2))
+        places = new_woven(0, 2, None)
         for e in range(2):
-            gather_and_weave(e * C, (e + 1) * C, "rows%d" % e, nc.scalar.copy)
-        left = []
-        for e in range(last):
-            banks = products(*quantise(e * C, (e + 1) * C), e)
-            if e + 2 < last:
-                gather_and_weave((e + 2) * C, (e + 3) * C, "rows%d" % (e % 2), nc.gpsimd.tensor_copy)
-            else:
-                a = last * C + (e + 2 - last) * P
-                gather_and_weave(a, a + P, "rows%d" % (e % 2), nc.scalar.copy)
-            if e != E // 2:
-                empty(nc.scalar.copy, banks, e, z, 0)
-            else:
-                left.append((banks, e))
-            empty(nc.scalar.copy, banks, e, z, 2)
+            gather_pairs(e, "rows%d" % e)
+            weave(nc.gpsimd.tensor_copy, e, places[e])
+        for e in (2, 3):
+            gather_pairs(e, "rows%d" % e, 1)
+            gather_single(e)
+        quantise_and_multiply(0, 2)
+        places = new_woven(2 * C, 2, "woven_single")
+        for e in (2, 3):
+            weave(nc.scalar.copy, e, places[e - 2])
+        gather_pairs(4, "rows1")
+        quantise_and_multiply(2, 2)
+        weave(nc.gpsimd.tensor_copy, 4, new_woven(4 * C, 1, "woven4")[0])
+        gather_pairs(last, None)
+        weave(nc.scalar.copy, last, new_woven(last * C, 1, None)[0])
+        for e in range(3):
+            for first in (0, 2):
+                empty_z(nc.scalar.copy, e, first)
+        quantise_and_multiply(4, 1)
+        empty_z(nc.scalar.copy, 3, 2)
+        empty_z(nc.vector.tensor_copy, 3, 0)
+        codes, scales = quantise(last * C, S)
         alone = [in_bank(n, [P, C]) for n in (2, 4)]
         together = in_bank(3, [P, 2, C])
         places = [alone[0][:], alone[1][:], together[:, 0, :], together[:, 1, :]]
-        for h in range(2):
-            codes, scales = quantise(last * C + h * P, last * C + (h + 1) * P)
-            for b in (0, 2, 3, 1):
-                product(places[b][:, h * P : (h + 1) * P], codes, scales, last, b)
-            if h == 0:
-                empty(nc.vector.tensor_copy, *left[h], z, 0)
+        for b in (0, 2, 3, 1):
+            product(places[b], codes, scales, last, b)
+        empty_z(nc.vector.tensor_copy, 4, 0)
+        empty_z(nc.vector.tensor_copy, 4, 2)
         nc.vector.tensor_copy(z[0][:, last * C :], places[0])
         for b in (2, 3, 1):
             nc.scalar.copy(z[b][:, last * C :], places[b])
@@ -305,9 +349,10 @@ def tile_moe_uni_none_kernel(
         add_turned(1, 1, sum1)
         back0 = turn_back(0, sum0, 4)
         add_turned(1, 2, sum1)
-        store(0, back0)
         scale_back(1)
-        store(1, turn_back(1, sum1, 7))
+        back1 = turn_back(1, sum1, 7)
+        store(0, back0)
+        store(1, back1)
 
         thirds = [keep.tile([P, T], F32, name="third%d" % i) for i in range(2)]
 

@@ -36,6 +36,7 @@ def tile_moe_uni_none_kernel(
         keep = ctx.enter_context(tc.tile_pool(name="keep", bufs=1))
         ring = ctx.enter_context(tc.tile_pool(name="ring", bufs=2))
         lent = ctx.enter_context(tc.tile_pool(name="lent", bufs=1))
+        lent_bytes = ctx.enter_context(tc.tile_pool(name="lent_bytes", bufs=1))
         psum = ctx.enter_context(tc.psum_pool(name="psum", bufs=1))
 
         def in_bank(n, shape):
@@ -135,29 +136,40 @@ def tile_moe_uni_none_kernel(
             return ring.tile([P, T], F32, name="raw", bufs=4)
 
         y = [keep.tile([P, S], F32, name="y%d" % b) for b in range(BLOCKS)]
-        banks_y = []
-        for e in range(E):
+        gathered, single = [], {}
+        for e, at in enumerate((P, 9 * P, 0, 2 * P, 8 * P, 0)):
             xg_w = ring.tile([P, C], U32, name="xg_w", bufs=4, align_bytes=64)
-            xg_s = ring.tile([P, C], U8, name="xg_s", bufs=2, align_bytes=64)
+            xg_s = lent_bytes.tile([P, C], U8, name="xg_s%d" % e, align_bytes=64, offset=at)
             slots = entries(offs_t, e * C, (e + 1) * C)
             nc.vector.tensor_copy(xg_s[:], x_s[:].bitcast(U8).indirect(slots))
             nc.vector.tensor_copy(xg_w[:], x_w[:].bitcast(U32).indirect(slots))
-            if e == 0:
-                for b in range(BLOCKS):
-                    bank = in_bank(4 + b, [P, C])
-                    product(bank[:], xg_w[:], xg_s[:], e, b)
-                    nc.scalar.copy(y[b][:, :C], bank[:])
-                banks_y.append(None)
-                continue
-            banks_y.append(products(xg_w[:], xg_s[:], e))
-            if e < E // 2:
-                empty(nc.scalar.copy, banks_y[e], e, y, 0)
-            if e == E - 1:
-                empty(nc.scalar.copy, banks_y[E // 2], E // 2, y, 0)
-            if e != E - 2:
-                empty(nc.scalar.copy, banks_y[e], e, y, 2)
-        for e, first in ((E - 2, 2), (E - 2, 0), (E - 1, 0)):
-            empty(nc.vector.tensor_copy, banks_y[e], e, y, first)
+            gathered.append((xg_w[:], xg_s[:]))
+
+            def alone(e, b, n):
+                single[e, b] = in_bank(n, [P, C])
+                product(single[e, b][:], *gathered[e], e, b)
+
+            def copy_out(copy, e, b):
+                copy(y[b][:, e * C : (e + 1) * C], single[e, b][:])
+
+            if e in (1, 2):
+                banks = products(*gathered[e], e % 2, e)
+                for first in (0, 2):
+                    empty(nc.scalar.copy, banks, e, y, first)
+            elif e in (0, 3):
+                for n, b in enumerate((2, 0, 3, 1)):
+                    alone(e, b, 4 + n)
+                    copy_out(nc.scalar.copy, e, b)
+            elif e == 4:
+                for b, n in ((2, 2), (0, 3), (3, 0)):
+                    alone(e, b, n)
+                copy_out(nc.scalar.copy, e, 2)
+                copy_out(nc.scalar.copy, e, 3)
+        copy_out(nc.vector.tensor_copy, 4, 0)
+        for e, b, n in ((5, 2, 4), (5, 0, 5), (5, 3, 2), (4, 1, 1), (5, 1, 3)):
+            alone(e, b, n)
+        copy_out(nc.scalar.copy, 5, 2)
+        copy_out(nc.vector.tensor_copy, 5, 0)
 
         def turn_terms(term, banks, i, a, b, first=None, last=None):
             for j in range(a // P, b // P):
@@ -171,7 +183,7 @@ def tile_moe_uni_none_kernel(
 
         sums = bank_pair(4)
         raws = [bank_pair(6), bank_pair(0), bank_pair(2)]
-        c_tok = [keep.tile([P, 2, 2 * P], BF16, name="c_tok%d" % j, align_bytes=64) for j in range(TURNS)]
+        c_tok = [[keep.tile([P, 2, 2 * P], BF16, name="c_tok%d%d" % (u, h), align_bytes=64) for h in range(2)] for u in range(2)]
         part = [[keep.tile([P, 2, P], F32, name="part%d%d" % (r, j)) for j in range(TURNS)] for r in range(2)]
 
         def region(banks, j):
@@ -190,6 +202,10 @@ def tile_moe_uni_none_kernel(
         for n in range(4):
             gated_turned(n // CHOICES, n % CHOICES)
             raw_turned(n % 2, n // 2)
+            if n == 0:
+                copy_out(nc.scalar.copy, 5, 3)
+                copy_out(nc.vector.tensor_copy, 4, 1)
+                copy_out(nc.vector.tensor_copy, 5, 1)
         for j in range(TURNS):
             nc.scalar.activation(part[0][j][:], region(raws[0], j), COPY, scale=cols_a[:, j : j + 1])
         gated_turned(1, 1)
@@ -200,101 +216,87 @@ def tile_moe_uni_none_kernel(
             raw_turned(i, 2, HALF, T)
         for j in range(TURNS):
             nc.vector.scalar_tensor_tensor(part[1][j][:], region(raws[1], j), cols_a[:, TURNS + j : TURNS + j + 1], part[0][j][:], MULT, ADD)
-        c_pair = keep.tile([P, 2, T], I32, name="c_pair", align_bytes=64)
-        first_back = in_bank(6, [P, 2, HALF])
-        backs = [[first_back[:, u, :] for u in range(2)], []]
-        for h in range(2):
-            if h == 1:
-                backs[1].extend(in_bank(n, [P, HALF]) for n in (7, 4))
-            for j in (2 * h, 2 * h + 1):
-                nc.scalar.copy(c_tok[j][:, :, :P], region(sums, j))
-                nc.vector.scalar_tensor_tensor(
-                    c_tok[j][:, :, P:], region(raws[2], j), cols_a[:, 2 * TURNS + j : 2 * TURNS + j + 1], part[1][j][:], MULT, ADD
-                )
-                words = c_tok[j][:].bitcast(F32)
-                for u in range(2):
-                    turn(backs[h][u][:, (j % 2) * P : (j % 2 + 1) * P], words[:, u, :])
-        nc.vector.tensor_copy(c_pair[:, :, :HALF].bitcast(F32), first_back[:])
-        nc.vector.tensor_copy(c_pair[:, 0, HALF:].bitcast(F32), backs[1][0][:])
-        nc.scalar.copy(c_pair[:, 1, HALF:].bitcast(F32), backs[1][1][:])
+        c_pair = [keep.tile([P, T], I32, name="c_pair%d" % u, align_bytes=64) for u in range(2)]
+        backs = []
+        for u in range(2):
+            back = in_bank(6 + u, [P, T])
+            for h in range(2):
+                nc.scalar.copy(c_tok[u][h][:, :, :P], sums[h][:, :, u, :])
+                for j in (2 * h, 2 * h + 1):
+                    nc.vector.scalar_tensor_tensor(
+                        c_tok[u][h][:, j % 2, P:],
+                        region(raws[2], j)[:, u, :],
+                        cols_a[:, 2 * TURNS + j : 2 * TURNS + j + 1],
+                        part[1][j][:, u, :],
+                        MULT,
+                        ADD,
+                    )
+                words = c_tok[u][h][:].bitcast(F32)
+                for j in (2 * h, 2 * h + 1):
+                    turn(back[:, j * P : (j + 1) * P], words[:, j % 2, :])
+            backs.append(back)
+        nc.scalar.copy(c_pair[0][:].bitcast(F32), backs[0][:])
+        nc.vector.tensor_copy(c_pair[1][:].bitcast(F32), backs[1][:])
 
         z = [keep.tile([P, S], F32, name="z%d" % b) for b in range(BLOCKS)]
-        woven = {}
 
-        def gather_pairs(e, tag, first_row=0):
-            if tag is None:
-                rows[e] = lent.tile([P, 2, C], U32, name="lent_rows", align_bytes=64, offset=8 * C)
-            else:
-                rows[e] = keep.tile([P, 2, C], U32, name="rows", tag=tag, align_bytes=64)
-            for u in range(first_row, 2):
-                nc.vector.tensor_copy(rows[e][:, u, :], c_pair[:, u, :].bitcast(U32).indirect(entries(offs2_t, e * C, (e + 1) * C)))
+        def lent_tile(shape, name, at):
+            return lent.tile(shape, U32, name=name, align_bytes=64, offset=at * 4 * C)
 
-        def gather_single(e):
-            dst = rows[e][:, 0, :].bitcast(BF16).rearrange("p (n v) -> p n v", v=2)
-            for v in range(2):
-                nc.scalar.activation(dst[:, :, v], c_single[:, v, :].indirect(entries(offs2_t, e * C, (e + 1) * C)), COPY)
+        def gather_pairs(rows, a, b):
+            for u in range(2):
+                nc.vector.tensor_copy(rows[:, u, :], c_pair[u][:].bitcast(U32).indirect(entries(offs2_t, a, b)))
 
-        def weave(copy, e, dst):
-            copy(dst, rows[e][:].rearrange("p u n -> p n u"))
+        def weave(copy, rows, dst):
+            copy(dst, rows[:].rearrange("p u n -> p n u"))
 
-        def new_woven(a, experts, tag):
-            if tag is None:
-                woven[a] = lent.tile([P, experts * C, 2], U32, name="lent_woven%d" % a, align_bytes=64, offset=0 if a == 0 else 16 * C)
-            else:
-                woven[a] = keep.tile([P, experts * C, 2], U32, name="woven", tag=tag, align_bytes=64)
-            return [woven[a][:, i * C : (i + 1) * C, :] for i in range(experts)]
-
-        def quantise(a, b):
-            if a <= 2 * C:
-                cq_w = lent.tile([P, b - a], U32, name="lent_codes%d" % a, align_bytes=64, offset=16 * C if a == 0 else 0)
-            else:
-                cq_w = keep.tile([P, b - a], U32, name="cq_w%d" % a, align_bytes=64)
-            cq_s = keep.tile([P, b - a], U8, name="cq_s%d" % a, align_bytes=64)
-            nc.vector.quantize_mx(out=cq_w[:].bitcast(FP8X4), scales=cq_s[:], in_=woven[a][:].rearrange("p n u -> p (n u)").bitcast(BF16))
+        def quantise(src, name, codes=None):
+            n = src.shape[1]
+            cq_w = keep.tile([P, n], U32, name="cq_w" + name, align_bytes=64) if codes is None else codes
+            cq_s = keep.tile([P, n], U8, name="cq_s" + name, align_bytes=64)
+            nc.vector.quantize_mx(out=cq_w[:].bitcast(FP8X4), scales=cq_s[:], in_=src[:].rearrange("p n u -> p (n u)").bitcast(BF16))
             return cq_w[:], cq_s[:]
-
-        def quantise_and_multiply(e, experts):
-            codes, scales = quantise(e * C, (e + experts) * C)
-            for i in range(experts):
-                banks_z[e + i] = products(codes[:, i * C : (i + 1) * C], scales[:, i * C : (i + 1) * C], e + i)
 
         def empty_z(copy, e, first):
             empty(copy, banks_z[e], e, z, first)
 
         last = E - 1
-        rows, banks_z = {}, {}
-        c_single = keep.tile([P, 2, T], BF16, name="c_single", align_bytes=64)
-        nc.scalar.copy(c_single[:], c_pair[:, 0, :].bitcast(BF16).rearrange("p (n v) -> p v n", v=2))
-        places = new_woven(0, 2, None)
+        banks_z = {}
+        woven = [keep.tile([P, C, 2], U32, name="woven%d" % e, align_bytes=64) for e in range(last)]
+
+        def gather_and_weave(e, copy):
+            rows = lent_tile([P, 2, C], "rows%d" % e, 2 * (e % 2))
+            gather_pairs(rows, e * C, (e + 1) * C)
+            weave(copy, rows, woven[e][:])
+
         for e in range(2):
-            gather_pairs(e, "rows%d" % e)
-            weave(nc.gpsimd.tensor_copy, e, places[e])
-        for e in (2, 3):
-            gather_pairs(e, "rows%d" % e, 1)
-            gather_single(e)
-        quantise_and_multiply(0, 2)
-        places = new_woven(2 * C, 2, "woven_single")
-        for e in (2, 3):
-            weave(nc.scalar.copy, e, places[e - 2])
-        gather_pairs(4, "rows1")
-        quantise_and_multiply(2, 2)
-        weave(nc.gpsimd.tensor_copy, 4, new_woven(4 * C, 1, "woven4")[0])
-        gather_pairs(last, None)
-        weave(nc.scalar.copy, last, new_woven(last * C, 1, None)[0])
+            gather_and_weave(e, nc.scalar.copy)
         for e in range(3):
+            banks_z[e] = products(*quantise(woven[e], "%d" % e), e)
+            gather_and_weave(e + 2, nc.gpsimd.tensor_copy)
             for first in (0, 2):
                 empty_z(nc.scalar.copy, e, first)
-        quantise_and_multiply(4, 1)
-        empty_z(nc.scalar.copy, 3, 2)
-        empty_z(nc.vector.tensor_copy, 3, 0)
-        codes, scales = quantise(last * C, S)
+        banks_z[3] = products(*quantise(woven[3], "3"), 3)
+        halves = []
+        for h in range(2):
+            rows = lent_tile([P, 2, P], "rows5%d" % h, 2 + h)
+            gather_pairs(rows, last * C + h * P, last * C + (h + 1) * P)
+            halves.append(keep.tile([P, P, 2], U32, name="woven5%d" % h, align_bytes=64))
+            weave(nc.scalar.copy, rows, halves[h][:])
+        codes, scales = quantise(woven[4], "4")
+        banks_z[4] = [multiply(codes, scales, 4, 0, 0)]
         alone = [in_bank(n, [P, C]) for n in (2, 4)]
         together = in_bank(3, [P, 2, C])
         places = [alone[0][:], alone[1][:], together[:, 0, :], together[:, 1, :]]
-        for b in (0, 2, 3, 1):
-            product(places[b], codes, scales, last, b)
-        empty_z(nc.vector.tensor_copy, 4, 0)
-        empty_z(nc.vector.tensor_copy, 4, 2)
+        ends = [quantise(halves[h], "5%d" % h) for h in range(2)]
+        for h in range(2):
+            product(places[0][:, h * P : (h + 1) * P], *ends[h], last, 0)
+        banks_z[4].append(multiply(codes, scales, 4, 2, 1))
+        for b in (2, 3, 1):
+            for h in range(2):
+                product(places[b][:, h * P : (h + 1) * P], *ends[h], last, b)
+        for e, first in ((3, 0), (4, 0), (3, 2), (4, 2)):
+            empty_z(nc.scalar.copy, e, first)
         nc.vector.tensor_copy(z[0][:, last * C :], places[0])
         for b in (2, 3, 1):
             nc.scalar.copy(z[b][:, last * C :], places[b])

@@ -239,64 +239,82 @@ def tile_moe_uni_none_kernel(
         nc.vector.tensor_copy(c_pair[1][:].bitcast(F32), backs[1][:])
 
         z = [keep.tile([P, S], F32, name="z%d" % b) for b in range(BLOCKS)]
+        woven = {}
 
-        def lent_tile(shape, name, at):
-            return lent.tile(shape, U32, name=name, align_bytes=64, offset=at * 4 * C)
+        def gather_pairs(e, tag, first_row=0):
+            if tag is None:
+                rows[e] = lent.tile([P, 2, C], U32, name="lent_rows", align_bytes=64, offset=8 * C)
+            else:
+                rows[e] = keep.tile([P, 2, C], U32, name="rows", tag=tag, align_bytes=64)
+            for u in range(first_row, 2):
+                nc.vector.tensor_copy(rows[e][:, u, :], c_pair[u][:].bitcast(U32).indirect(entries(offs2_t, e * C, (e + 1) * C)))
 
-        def gather_pairs(rows, a, b):
-            for u in range(2):
-                nc.vector.tensor_copy(rows[:, u, :], c_pair[u][:].bitcast(U32).indirect(entries(offs2_t, a, b)))
+        def gather_single(e):
+            dst = rows[e][:, 0, :].bitcast(BF16).rearrange("p (n v) -> p n v", v=2)
+            for v in range(2):
+                nc.scalar.activation(dst[:, :, v], c_single[:, v, :].indirect(entries(offs2_t, e * C, (e + 1) * C)), COPY)
 
-        def weave(copy, rows, dst):
-            copy(dst, rows[:].rearrange("p u n -> p n u"))
+        def weave(copy, e, dst):
+            copy(dst, rows[e][:].rearrange("p u n -> p n u"))
 
-        def quantise(src, name, codes=None):
-            n = src.shape[1]
-            cq_w = keep.tile([P, n], U32, name="cq_w" + name, align_bytes=64) if codes is None else codes
-            cq_s = keep.tile([P, n], U8, name="cq_s" + name, align_bytes=64)
-            nc.vector.quantize_mx(out=cq_w[:].bitcast(FP8X4), scales=cq_s[:], in_=src[:].rearrange("p n u -> p (n u)").bitcast(BF16))
+        def new_woven(a, experts, tag):
+            if tag is None:
+                woven[a] = lent.tile([P, experts * C, 2], U32, name="lent_woven%d" % a, align_bytes=64, offset=0 if a == 0 else 16 * C)
+            else:
+                woven[a] = keep.tile([P, experts * C, 2], U32, name="woven", tag=tag, align_bytes=64)
+            return [woven[a][:, i * C : (i + 1) * C, :] for i in range(experts)]
+
+        def quantise(a, b):
+            if a <= 2 * C:
+                cq_w = lent.tile([P, b - a], U32, name="lent_codes%d" % a, align_bytes=64, offset=16 * C if a == 0 else 0)
+            else:
+                cq_w = keep.tile([P, b - a], U32, name="cq_w%d" % a, align_bytes=64)
+            cq_s = keep.tile([P, b - a], U8, name="cq_s%d" % a, align_bytes=64)
+            nc.vector.quantize_mx(out=cq_w[:].bitcast(FP8X4), scales=cq_s[:], in_=woven[a][:].rearrange("p n u -> p (n u)").bitcast(BF16))
             return cq_w[:], cq_s[:]
+
+        def quantise_and_multiply(e, experts):
+            codes, scales = quantise(e * C, (e + experts) * C)
+            for i in range(experts):
+                banks_z[e + i] = products(codes[:, i * C : (i + 1) * C], scales[:, i * C : (i + 1) * C], e + i)
 
         def empty_z(copy, e, first):
             empty(copy, banks_z[e], e, z, first)
 
         last = E - 1
-        banks_z = {}
-        woven = [keep.tile([P, C, 2], U32, name="woven%d" % e, align_bytes=64) for e in range(last)]
-
-        def gather_and_weave(e, copy):
-            rows = lent_tile([P, 2, C], "rows%d" % e, 2 * (e % 2))
-            gather_pairs(rows, e * C, (e + 1) * C)
-            weave(copy, rows, woven[e][:])
-
+        rows, banks_z = {}, {}
+        c_single = keep.tile([P, 2, T], BF16, name="c_single", align_bytes=64)
+        nc.scalar.copy(c_single[:], c_pair[0][:].bitcast(BF16).rearrange("p (n v) -> p v n", v=2))
+        places = new_woven(0, 2, None)
         for e in range(2):
-            gather_and_weave(e, nc.scalar.copy)
+            gather_pairs(e, "rows%d" % e)
+            weave(nc.gpsimd.tensor_copy, e, places[e])
+        gather_pairs(2, "rows2")
+        gather_pairs(3, "rows3", 1)
+        gather_single(3)
+        quantise_and_multiply(0, 2)
+        places = new_woven(2 * C, 2, "woven_single")
+        for e in (2, 3):
+            weave(nc.scalar.copy, e, places[e - 2])
+        gather_pairs(4, "rows1")
+        quantise_and_multiply(2, 2)
+        weave(nc.gpsimd.tensor_copy, 4, new_woven(4 * C, 1, "woven4")[0])
+        gather_pairs(last, None)
+        weave(nc.scalar.copy, last, new_woven(last * C, 1, None)[0])
         for e in range(3):
-            banks_z[e] = products(*quantise(woven[e], "%d" % e), e)
-            gather_and_weave(e + 2, nc.gpsimd.tensor_copy)
             for first in (0, 2):
                 empty_z(nc.scalar.copy, e, first)
-        banks_z[3] = products(*quantise(woven[3], "3"), 3)
-        halves = []
-        for h in range(2):
-            rows = lent_tile([P, 2, P], "rows5%d" % h, 2 + h)
-            gather_pairs(rows, last * C + h * P, last * C + (h + 1) * P)
-            halves.append(keep.tile([P, P, 2], U32, name="woven5%d" % h, align_bytes=64))
-            weave(nc.scalar.copy, rows, halves[h][:])
-        codes, scales = quantise(woven[4], "4")
-        banks_z[4] = [multiply(codes, scales, 4, 0, 0)]
+        quantise_and_multiply(4, 1)
+        empty_z(nc.scalar.copy, 3, 2)
+        empty_z(nc.vector.tensor_copy, 3, 0)
+        codes, scales = quantise(last * C, S)
         alone = [in_bank(n, [P, C]) for n in (2, 4)]
         together = in_bank(3, [P, 2, C])
         places = [alone[0][:], alone[1][:], together[:, 0, :], together[:, 1, :]]
-        ends = [quantise(halves[h], "5%d" % h) for h in range(2)]
-        for h in range(2):
-            product(places[0][:, h * P : (h + 1) * P], *ends[h], last, 0)
-        banks_z[4].append(multiply(codes, scales, 4, 2, 1))
-        for b in (2, 3, 1):
-            for h in range(2):
-                product(places[b][:, h * P : (h + 1) * P], *ends[h], last, b)
-        for e, first in ((3, 0), (4, 0), (3, 2), (4, 2)):
-            empty_z(nc.scalar.copy, e, first)
+        for b in (0, 2, 3, 1):
+            product(places[b], codes, scales, last, b)
+        empty_z(nc.vector.tensor_copy, 4, 0)
+        empty_z(nc.vector.tensor_copy, 4, 2)
         nc.vector.tensor_copy(z[0][:, last * C :], places[0])
         for b in (2, 3, 1):
             nc.scalar.copy(z[b][:, last * C :], places[b])

from contextlib import ExitStack

import concourse.mybir as mybir
from concourse.masks import make_identity

F32 = mybir.dt.float32
BF16 = mybir.dt.bfloat16
I32 = mybir.dt.int32
U32 = mybir.dt.uint32
U16 = mybir.dt.uint16
U8 = mybir.dt.uint8
FP8X4 = mybir.dt.float8_e4m3fn_x4
FP4X4 = mybir.dt.float4_e2m1fn_x4
MULT = mybir.AluOpType.mult
ADD = mybir.AluOpType.add
COPY = mybir.ActivationFunctionType.Copy

K, T, E, C = 512, 512, 6, 256
S = E * C
P = 128
BLOCKS = K // P
TURNS = T // P
CHOICES = 3
QUADS = 4
PER_COL = 16
HALF = T // 2
BANKS = 8
FLOPS = 2 * 2 * K * K * S


def tile_moe_uni_none_kernel(
    tc, x_words, x_scales, w_words, w_scales, gate1, gate2, offs, pos1, pos2, pos3, offs2, pos4, pos5, pos6, out
):
    nc = tc.nc
    with ExitStack() as ctx:
        keep = ctx.enter_context(tc.tile_pool(name="keep", bufs=1))
        ring = ctx.enter_context(tc.tile_pool(name="ring", bufs=2))
        lent = ctx.enter_context(tc.tile_pool(name="lent", bufs=1))
        lent_bytes = ctx.enter_context(tc.tile_pool(name="lent_bytes", bufs=1))
        psum = ctx.enter_context(tc.psum_pool(name="psum", bufs=1))

        def in_bank(n, shape):
            return psum.tile(shape, F32, name="bank", tag="bank%d" % n)

        def load_list(src, name):
            lst = keep.tile([P, src.shape[1]], U16, name=name)
            nc.sync.dma_start(lst[:], src)
            return lst

        def entries(lst, a, b):
            return lst[:, a // PER_COL : b // PER_COL]

        x_w = keep.tile([P, T], I32, name="x_w", align_bytes=64)
        x_s = keep.tile([P, T // 4], I32, name="x_s", align_bytes=64)
        w_w = [keep.tile([P, 2 + 2 * i, K // 2], I32, name="w_w%d" % i, align_bytes=64) for i in range(2)]
        w_s = keep.tile([P, E, K // 4], I32, name="w_s", align_bytes=64)
        nc.gpsimd.memset(x_s[:], 0)

        w_rows = w_words.rearrange("e s p n -> p (e s) n").bitcast(I32)
        offs_t = load_list(offs, "offs_t")

        def load_w_scales(q, queue=nc.sync):
            queue.dma_start(
                w_s[32 * q : 32 * q + 4, :, :],
                w_scales[:, 0, 4 * q : 4 * q + 4, :].rearrange("e b n -> b e n").bitcast(I32),
            )

        load_w_scales(0)
        for q in range(QUADS):
            nc.sync.dma_start(x_s[32 * q : 32 * q + 4, :], x_scales[0, 4 * q : 4 * q + 4, :].bitcast(I32))
        nc.sync.dma_start(x_w[:], x_words.rearrange("s p t d -> p (s t d)").bitcast(I32))
        nc.sync.dma_start(w_w[0][:], w_rows[:, :2, :])
        for q in range(1, QUADS):
            load_w_scales(q)
        nc.sync.dma_start(w_w[1][:], w_rows[:, 2:, :])
        pos_a = [load_list(src, "pos_a%d" % r) for r, src in enumerate((pos1, pos2, pos3))]
        gate_a = keep.tile([P, CHOICES, T], F32, name="gate_a")
        nc.sync.dma_start(gate_a[:], gate1.rearrange("r p n -> p r n"))

        def load_gate_columns(gate, choices, name):
            cols = keep.tile([P, choices * TURNS], F32, name=name)
            pieces = gate.rearrange("r p (j m) -> (r p j) m", m=P)
            with nc.allow_non_contiguous_dma(reason="one gate value a partition"):
                nc.sync.dma_start(cols[:], pieces[0 : (choices * TURNS - 1) * (P + 1) + 1 : P + 1, :].rearrange("i m -> m i"))
            return cols

        cols_a = load_gate_columns(gate1, CHOICES, "cols_a")
        offs2_t = load_list(offs2, "offs2_t")
        pos_b = [load_list(src, "pos_b%d" % r) for r, src in enumerate((pos4, pos5, pos6))]
        gate_b = keep.tile([P, CHOICES, T], F32, name="gate_b")
        nc.sync.dma_start(gate_b[:], gate2.rearrange("r p n -> p r n"))
        cols_b = load_gate_columns(gate2, 2, "cols_b")

        ident = keep.tile([P, P], F32, name="ident")
        make_identity(nc, ident[:])

        w_codes = [w_w[min(e // 2, 1)][:, e if e < 2 else e - 2, :].bitcast(U8) for e in range(E)]

        def product(dst, codes, scales, e, b):
            nc.tensor.matmul_mx(
                out=dst,
                lhsT=w_codes[e][:, 2 * P * b : 2 * P * (b + 1)].bitcast(FP4X4),
                lhsT_scale=w_s[:, e, :].bitcast(U8)[:, P * b : P * (b + 1)],
                rhs=codes.bitcast(FP8X4),
                rhs_scale=scales,
                start=True,
                stop=True,
            )

        def multiply(codes, scales, e, first, bank_no):
            bank = in_bank(bank_no, [P, 2, C])
            for i in range(2):
                product(bank[:, i, :], codes, scales, e, first + i)
            return bank

        def products(codes, scales, turn_no, e=None):
            return [multiply(codes, scales, turn_no if e is None else e, first, (2 * turn_no + first // 2) % BANKS) for first in (0, 2)]

        def empty(copy, banks, e, dst, first):
            for i in range(2):
                copy(dst[first + i][:, e * C : (e + 1) * C], banks[first // 2][:, i, :])

        def turn(dst, src, start=True, stop=True):
            nc.tensor.matmul(dst, lhsT=src, rhs=ident[:], is_transpose=True, start=start, stop=stop)

        def gated(window, pos, gate, r, dst, a=0, b=T):
            nc.vector.tensor_tensor(dst[:, a:b], window[:].indirect(entries(pos[r], a, b)), gate[:, r, a:b], MULT)

        def raw(window, pos, r, dst, a=0, b=T):
            nc.scalar.activation(dst[:, a:b], window[:].indirect(entries(pos[r], a, b)), COPY)

        def new_term():
            return ring.tile([P, T], F32, name="term", bufs=4)

        def new_raw():
            return ring.tile([P, T], F32, name="raw", bufs=4)

        y = [keep.tile([P, S], F32, name="y%d" % b) for b in range(BLOCKS)]
        gathered, single = [], {}
        for e, at in enumerate((P, 9 * P, 0, 2 * P, 8 * P, 0)):
            xg_w = ring.tile([P, C], U32, name="xg_w", bufs=4, align_bytes=64)
            xg_s = lent_bytes.tile([P, C], U8, name="xg_s%d" % e, align_bytes=64, offset=at)
            slots = entries(offs_t, e * C, (e + 1) * C)
            nc.vector.tensor_copy(xg_s[:], x_s[:].bitcast(U8).indirect(slots))
            nc.vector.tensor_copy(xg_w[:], x_w[:].bitcast(U32).indirect(slots))
            gathered.append((xg_w[:], xg_s[:]))

            def alone(e, b, n):
                single[e, b] = in_bank(n, [P, C])
                product(single[e, b][:], *gathered[e], e, b)

            def copy_out(copy, e, b):
                copy(y[b][:, e * C : (e + 1) * C], single[e, b][:])

            if e in (1, 2):
                banks = products(*gathered[e], e % 2, e)
                for first in (0, 2):
                    empty(nc.scalar.copy, banks, e, y, first)
            elif e in (0, 3):
                for n, b in enumerate((2, 0, 3, 1)):
                    alone(e, b, 4 + n)
                    copy_out(nc.scalar.copy, e, b)
            elif e == 4:
                for b, n in ((2, 2), (0, 3), (3, 0)):
                    alone(e, b, n)
                copy_out(nc.scalar.copy, e, 2)
                copy_out(nc.scalar.copy, e, 3)
        copy_out(nc.vector.tensor_copy, 4, 0)
        for e, b, n in ((5, 2, 4), (5, 0, 5), (5, 3, 2), (4, 1, 1), (5, 1, 3)):
            alone(e, b, n)
        copy_out(nc.scalar.copy, 5, 2)
        copy_out(nc.vector.tensor_copy, 5, 0)

        def turn_terms(term, banks, i, a, b, first=None, last=None):
            for j in range(a // P, b // P):
                start = True if first is None else (first and j % 2 == 0)
                stop = True if last is None else (last and j % 2 == 1)
                dst = banks[j // 2][:, j % 2, :, 64 * i : 64 * (i + 1)].rearrange("p u (m v) -> p m u v", v=2)
                turn(dst, term[:, j * P : (j + 1) * P], start, stop)

        def bank_pair(n):
            return [in_bank(n + h, [P, 2, 2, P]) for h in range(2)]

        sums = bank_pair(4)
        raws = [bank_pair(6), bank_pair(0), bank_pair(2)]
        c_tok = [[keep.tile([P, 2, 2 * P], BF16, name="c_tok%d%d" % (u, h), align_bytes=64) for h in range(2)] for u in range(2)]
        part = [[keep.tile([P, 2, P], F32, name="part%d%d" % (r, j)) for j in range(TURNS)] for r in range(2)]

        def region(banks, j):
            return banks[j // 2][:, j % 2, :, :]

        def gated_turned(i, r):
            term = new_term()
            gated(y[i], pos_a, gate_a, r, term)
            turn_terms(term, sums, i, 0, T, (i, r) == (0, 0), (i, r) == (1, CHOICES - 1))

        def raw_turned(i, r, a=0, b=T):
            term = new_raw()
            raw(y[2 + i], pos_a, r, term, a, b)
            turn_terms(term, raws[r], i, a, b)

        for n in range(4):
            gated_turned(n // CHOICES, n % CHOICES)
            raw_turned(n % 2, n // 2)
            if n == 0:
                copy_out(nc.scalar.copy, 5, 3)
                copy_out(nc.vector.tensor_copy, 4, 1)
                copy_out(nc.vector.tensor_copy, 5, 1)
        for j in range(TURNS):
            nc.scalar.activation(part[0][j][:], region(raws[0], j), COPY, scale=cols_a[:, j : j + 1])
        gated_turned(1, 1)
        for i in range(2):
            raw_turned(i, 2, 0, HALF)
        gated_turned(1, 2)
        for i in range(2):
            raw_turned(i, 2, HALF, T)
        for j in range(TURNS):
            nc.vector.scalar_tensor_tensor(part[1][j][:], region(raws[1], j), cols_a[:, TURNS + j : TURNS + j + 1], part[0][j][:], MULT, ADD)
        c_pair = [keep.tile([P, T], I32, name="c_pair%d" % u, align_bytes=64) for u in range(2)]
        backs = []
        for u in range(2):
            back = in_bank(6 + u, [P, T])
            for h in range(2):
                nc.scalar.copy(c_tok[u][h][:, :, :P], sums[h][:, :, u, :])
                for j in (2 * h, 2 * h + 1):
                    nc.vector.scalar_tensor_tensor(
                        c_tok[u][h][:, j % 2, P:],
                        region(raws[2], j)[:, u, :],
                        cols_a[:, 2 * TURNS + j : 2 * TURNS + j + 1],
                        part[1][j][:, u, :],
                        MULT,
                        ADD,
                    )
                words = c_tok[u][h][:].bitcast(F32)
                for j in (2 * h, 2 * h + 1):
                    turn(back[:, j * P : (j + 1) * P], words[:, j % 2, :])
            backs.append(back)
        nc.scalar.copy(c_pair[0][:].bitcast(F32), backs[0][:])
        nc.vector.tensor_copy(c_pair[1][:].bitcast(F32), backs[1][:])

        z = [keep.tile([P, S], F32, name="z%d" % b) for b in range(BLOCKS)]
        woven = {}

        def gather_pairs(e, tag, first_row=0):
            if tag is None:
                rows[e] = lent.tile([P, 2, C], U32, name="lent_rows", align_bytes=64, offset=8 * C)
            else:
                rows[e] = keep.tile([P, 2, C], U32, name="rows", tag=tag, align_bytes=64)
            for u in range(first_row, 2):
                nc.vector.tensor_copy(rows[e][:, u, :], c_pair[u][:].bitcast(U32).indirect(entries(offs2_t, e * C, (e + 1) * C)))

        def gather_single(e):
            dst = rows[e][:, 0, :].bitcast(BF16).rearrange("p (n v) -> p n v", v=2)
            for v in range(2):
                nc.scalar.activation(dst[:, :, v], c_single[:, v, :].indirect(entries(offs2_t, e * C, (e + 1) * C)), COPY)

        def weave(copy, e, dst):
            copy(dst, rows[e][:].rearrange("p u n -> p n u"))

        def new_woven(a, experts, tag):
            if tag is None:
                woven[a] = lent.tile([P, experts * C, 2], U32, name="lent_woven%d" % a, align_bytes=64, offset=0 if a == 0 else 16 * C)
            else:
                woven[a] = keep.tile([P, experts * C, 2], U32, name="woven", tag=tag, align_bytes=64)
            return [woven[a][:, i * C : (i + 1) * C, :] for i in range(experts)]

        def quantise(a, b):
            if a <= 2 * C:
                cq_w = lent.tile([P, b - a], U32, name="lent_codes%d" % a, align_bytes=64, offset=16 * C if a == 0 else 0)
            else:
                cq_w = keep.tile([P, b - a], U32, name="cq_w%d" % a, align_bytes=64)
            cq_s = keep.tile([P, b - a], U8, name="cq_s%d" % a, align_bytes=64)
            nc.vector.quantize_mx(out=cq_w[:].bitcast(FP8X4), scales=cq_s[:], in_=woven[a][:].rearrange("p n u -> p (n u)").bitcast(BF16))
            return cq_w[:], cq_s[:]

        def quantise_and_multiply(e, experts):
            codes, scales = quantise(e * C, (e + experts) * C)
            for i in range(experts):
                banks_z[e + i] = products(codes[:, i * C : (i + 1) * C], scales[:, i * C : (i + 1) * C], e + i)

        def empty_z(copy, e, first):
            empty(copy, banks_z[e], e, z, first)

        last = E - 1
        rows, banks_z = {}, {}
        c_single = keep.tile([P, 2, T], BF16, name="c_single", align_bytes=64)
        nc.scalar.copy(c_single[:], c_pair[0][:].bitcast(BF16).rearrange("p (n v) -> p v n", v=2))
        places = new_woven(0, 2, None)
        for e in range(2):
            gather_pairs(e, "rows%d" % e)
            weave(nc.gpsimd.tensor_copy, e, places[e])
        gather_pairs(2, "rows2")
        gather_pairs(3, "rows3", 1)
        gather_single(3)
        quantise_and_multiply(0, 2)
        places = new_woven(2 * C, 2, "woven_single")
        for e in (2, 3):
            weave(nc.scalar.copy, e, places[e - 2])
        gather_pairs(4, "rows1")
        quantise_and_multiply(2, 2)
        weave(nc.gpsimd.tensor_copy, 4, new_woven(4 * C, 1, "woven4")[0])
        gather_pairs(last, None)
        weave(nc.scalar.copy, last, new_woven(last * C, 1, None)[0])
        for e in range(3):
            for first in (0, 2):
                empty_z(nc.scalar.copy, e, first)
        quantise_and_multiply(4, 1)
        empty_z(nc.scalar.copy, 3, 2)
        empty_z(nc.vector.tensor_copy, 3, 0)
        codes, scales = quantise(last * C, S)
        alone = [in_bank(n, [P, C]) for n in (2, 4)]
        together = in_bank(3, [P, 2, C])
        places = [alone[0][:], alone[1][:], together[:, 0, :], together[:, 1, :]]
        for b in (0, 2, 3, 1):
            product(places[b], codes, scales, last, b)
        empty_z(nc.vector.tensor_copy, 4, 0)
        empty_z(nc.vector.tensor_copy, 4, 2)
        nc.vector.tensor_copy(z[0][:, last * C :], places[0])
        for b in (2, 3, 1):
            nc.scalar.copy(z[b][:, last * C :], places[b])

        res = [keep.tile([P, T], F32, name="res%d" % b) for b in range(BLOCKS)]

        def add_turned(b, r, bank, pieces=((0, T),)):
            for a, end in pieces:
                term = new_term()
                gated(z[b], pos_b, gate_b, r, term, a, end)
                for j in range(a // P, end // P):
                    turn(bank[:, j, :], term[:, j * P : (j + 1) * P], r == 0 and j == 0, r == CHOICES - 1 and j == TURNS - 1)

        def turn_back(b, bank, bank_no):
            turned = keep.tile([P, TURNS, P], F32, name="turned%d" % b)
            nc.scalar.copy(turned[:], bank[:])
            back = in_bank(bank_no, [P, T])
            for j in range(TURNS):
                turn(back[:, j * P : (j + 1) * P], turned[:, j, :])
            return back

        def store(b, back):
            nc.scalar.copy(res[b][:], back[:])
            nc.sync.dma_start(out[b * P : (b + 1) * P, :], res[b][:])

        def raw_out(i, r):
            term = new_raw()
            raw(z[2 + i], pos_b, r, term)
            for j in range(TURNS):
                turn(raw_banks[r][j // 2][:, j % 2, i, :], term[:, j * P : (j + 1) * P])

        def scale_back(r):
            for j in range(TURNS):
                scaled = keep.tile([P, 2, P], F32, name="scaled%d%d" % (r, j))
                nc.scalar.activation(scaled[:], region(raw_banks[r], j), COPY, scale=cols_b[:, TURNS * r + j : TURNS * r + j + 1])
                for i in range(2):
                    turn(partial[i][:, j * P : (j + 1) * P], scaled[:, i, :], r == 0 and j == 0, r == 1 and j == TURNS - 1)

        sum0 = in_bank(5, [P, TURNS, P])
        raw_banks = [bank_pair(6), bank_pair(0)]
        partial = [in_bank(2 + i, [P, T]) for i in range(2)]
        add_turned(0, 0, sum0, ((0, HALF), (HALF, T)))
        raw_out(0, 0)
        add_turned(0, 1, sum0)
        raw_out(1, 0)
        add_turned(0, 2, sum0)
        raw_out(0, 1)
        raw_out(1, 1)
        scale_back(0)
        sum1 = in_bank(6, [P, TURNS, P])
        add_turned(1, 0, sum1)
        add_turned(1, 1, sum1)
        back0 = turn_back(0, sum0, 4)
        add_turned(1, 2, sum1)
        scale_back(1)
        back1 = turn_back(1, sum1, 7)
        store(0, back0)
        store(1, back1)

        thirds = [keep.tile([P, T], F32, name="third%d" % i) for i in range(2)]

        def finish(i, a, b):
            nc.vector.tensor_tensor(res[2 + i][:, a:b], partial[i][:, a:b], thirds[i][:, a:b], ADD)
            nc.sync.dma_start(out[(2 + i) * P : (3 + i) * P, a:b], res[2 + i][:, a:b])

        for i in range(2):
            gated(z[2 + i], pos_b, gate_b, 2, thirds[i])
        finish(0, 0, T)
        finish(1, 0, HALF + P)
        finish(1, HALF + P, T)
